import numpy as np, ml_dtypes
CORES = [16,18,20,22]
N = 4
BF = ml_dtypes.bfloat16
W, C, B, VI, S = 4096, 4096, 256, 3, 4
def parts(rng):
    rt = rng.integers(0, 16, (N, 8, 16, W)); pf = rng.integers(0, W, (N, 8, 16, C))
    jc = np.argsort(rng.random((N, 8, C)), axis=-1)[..., :16 * B].reshape(N, 8, 16, B)
    return rt, pf, jc, rng.integers(0, 16, (N, 8, 16, B)), rng.integers(0, 16, (N, 8, B))
def pack(rt, pf, jc, fx, sr):
    return {"rt": np.ascontiguousarray(rt.reshape(N, 128, W)).astype(np.float32).astype(BF),
            "pk": np.ascontiguousarray((pf[..., :C // 2] + 4096 * pf[..., C // 2:]).reshape(N, 128, C // 2)).astype(np.int32),
            "jc": np.ascontiguousarray(jc.reshape(N, 128, B)).astype(np.int32),
            "fx": np.ascontiguousarray(fx.reshape(N, 128, B)).astype(np.float32).astype(BF), "sr": np.ascontiguousarray(sr).astype(np.int32)}
def setup_inputs(rng):
    return pack(*parts(rng))
def setup_inputs_ties(rng):
    rt, pf, jc, fx, sr = parts(rng)
    pool = rng.integers(0, 16, (N, 8, 16, 8)); pool[:, 1::2] = rng.integers(0, 2, (N, 4, 16, 8))
    rt = np.take_along_axis(pool, rng.integers(0, 8, (N, 8, 1, W)), 3)
    fx = np.where(rng.random((N, 8, 1, B)) < 0.5, np.take_along_axis(pool, rng.integers(0, 8, (N, 8, 1, B)), 3), fx)
    q = rng.permutation(C)[:C // 8]; pf[..., q] = pf[:, :, :1, q]
    return pack(rt, pf, jc, fx, sr)
def setup_inputs_rounds(rng):
    rt, pf, jc, fx, sr = parts(rng); h = W // 2
    o = np.argsort(rng.random((N, 8, W)), axis=-1); light = np.zeros((N, 8, W), bool); np.put_along_axis(light, o[..., :h], True, 2)
    rt = np.where(light[:, :, None, :], rng.integers(0, 2, (N, 8, 16, W)), rng.integers(8, 16, (N, 8, 16, W)))
    ln = rng.integers(1, S + 2, (8, B)); back = (rng.random((8, B)) * ln).astype(np.int64)
    ln[0] = S; back[0] = 0; ln[1] = S + 1; ln[2] = 1; back[2] = 0
    if np.count_nonzero(ln <= S) % 2 == 0:
        ln[3, 0] = S + 1 if ln[3, 0] <= S else S; back[3, 0] = 0
    s0 = rng.integers(0, 16, (8, B)); a = (np.arange(16)[None, :, None] - s0[:, None, :]) % 16
    nxt = (np.where(a == ln[:, None, :] - 1, back[:, None, :], a + 1) + s0[:, None, :]) % 16
    pc = np.argsort(rng.random((8, C)), axis=-1)[:, :16 * B]
    kap = rng.integers(0, 16, (8, C)); np.put_along_axis(kap, pc, nxt.reshape(8, 16 * B), 1)
    one = kap[None, :, None, :] == np.arange(16)[None, None, :, None]
    pf = np.take_along_axis(o[:, :, None, :], rng.integers(0, h, (N, 8, 16, C)) + np.where(one, 0, h), 3)
    e = np.argsort(rng.random((N, 8, B)), axis=-1)
    jc = np.take_along_axis(np.broadcast_to(pc.reshape(1, 8, 16, B), (N, 8, 16, B)), np.broadcast_to(e[:, :, None, :], (N, 8, 16, B)), 3)
    sr = np.take_along_axis(np.broadcast_to(s0[None], (N, 8, B)), e, 2)
    return pack(rt, pf, jc, rng.integers(0, 2, (N, 8, 16, B)), sr)
def setup_inputs_full(rng):
    h = W // 2; u = h // 2; rows = np.arange(16)
    side = (np.arange(N)[:, None] + np.arange(8)[None, :]) % 2 * h
    o = np.argsort(rng.random((N, 8, h)), axis=-1) + side[:, :, None]; light = np.zeros((N, 8, W), bool); np.put_along_axis(light, o[..., :u], True, 2)
    rt = np.where(light[:, :, None, :], rng.integers(0, 2, (N, 8, 16, W)), rng.integers(8, 16, (N, 8, 16, W)))
    s0 = 2 * rng.permutation(8) + rng.integers(0, 2, 8); a = (rows[None, :] - s0[:, None]) % 16
    nxt = (np.where(a == S - 1, 0, a + 1) + s0[:, None]) % 16
    lower = np.argsort(rng.random((8, C // 2)), axis=-1)[:, :8 * B]; upper = np.argsort(rng.random((8, C // 2)), axis=-1)[:, :8 * B] + C // 2
    pc = np.concatenate([lower, upper], axis=1).reshape(8, 16, B)
    kap = rng.integers(0, 16, (N, 8, C))
    np.put_along_axis(kap, np.broadcast_to(pc.reshape(1, 8, 16 * B), (N, 8, 16 * B)), np.broadcast_to(np.repeat(nxt, B, axis=1)[None], (N, 8, 16 * B)), 2)
    whole = int(rng.integers(0, 8))
    for g in range(8):
        if g != whole: kap[1::2, g, int(pc[g, (s0[g] + S - 1) % 16, 0])] = (s0[g] + S) % 16
    one = kap[:, :, None, :] == rows[None, None, :, None]
    pf = np.take_along_axis(o[:, :, None, :], rng.integers(0, u, (N, 8, 16, C)) + np.where(one, 0, u), 3)
    e = np.argsort(rng.random((N, 8, 16, B)), axis=-1)
    jc = np.take_along_axis(np.broadcast_to(pc[None], (N, 8, 16, B)), e, 3)
    return pack(rt, pf, jc, rng.integers(0, 2, (N, 8, 16, B)), np.broadcast_to(s0[None, :, None], (N, 8, B)))
def setup_inputs_ends(rng):
    rt, pf, jc, fx, sr = parts(rng)
    pf[:, ::2] = rng.choice(np.array([0, 1, W // 2, W - 1]), (N, 4, 16, C)); pf[:, 1::2, :, C // 2 - 1] = W - 1; pf[:, 1::2, :, C - 1] = W - 1
    jc[:, ::2] = np.concatenate([np.arange(8 * B), np.arange(C - 8 * B, C)]).reshape(16, B)
    rt[:, 1::2] = 15 * rng.integers(0, 2, (N, 4, 16, W)); fx = 15 * rng.integers(0, 2, (N, 8, 16, B)); sr = 15 * rng.integers(0, 2, (N, 8, B))
    o = rng.permutation(W); n = B // 2; hi = o[:W // 4]; mid = o[W // 4:W // 2]; lo = o[W // 2:3 * W // 4]
    rt[:, 1][:, :, hi] = 15; rt[:, 1][:, :, mid] = 14; rt[:, 1][:, :, lo] = 0
    for q in range(N):
        x = rng.permutation(B)[:n]; p = np.argsort(rng.random((16, n)), axis=0)[:3]; c = jc[q, 1, p, x]
        for i, k, a, b in ((0, p[1], mid, hi), (1, p[2], hi, lo), (2, p[1], lo, hi)):
            pf[q, 1][:, c[i]] = rng.choice(b, (16, n)); pf[q, 1][k, c[i]] = rng.choice(a, n)
        fx[q, 1][:, x] = 0; sr[q, 1][x] = p[0]
    return pack(rt, pf, jc, fx, sr)
def setup_inputs_spread(rng):
    rt, pf, jc, fx, sr = parts(rng)
    rt = np.minimum((16 * rng.random((N, 8, 16, W)) ** np.exp2(rng.integers(-2, 4, (N, 8, 1, W)))).astype(np.int64), 15)
    pf = np.minimum((W * rng.random((N, 8, 16, C)) ** np.exp2(rng.integers(-2, 4, (N, 8, 1, C)))).astype(np.int64), W - 1)
    fx = np.minimum((16 * rng.random((N, 8, 16, B)) ** np.exp2(rng.integers(-2, 4, (N, 8, 1, B)))).astype(np.int64), 15)
    sr = np.minimum((16 * rng.random((N, 8, B)) ** np.exp2(rng.integers(-1, 3, (N, 8, 1)))).astype(np.int64), 15)
    return pack(rt, pf, jc, fx, sr)
def check_inputs(d):
    bad = []
    for k in ("rt", "fx"):
        a = np.asarray(d[k]).astype(np.float32)
        if not np.all((a >= 0) & (a <= 15) & (a == np.floor(a))): bad.append("whole numbers of " + k)
    a = np.asarray(d["pk"]).astype(np.int64)
    if np.min(a) < 0 or np.max(a & 4095) >= W or np.max(a >> 12) >= W: bad.append("range of pk")
    for k, hi in (("jc", C - 1), ("sr", 15)):
        if np.min(d[k]) < 0 or np.max(d[k]) > hi: bad.append("range of " + k)
    s = np.sort(np.asarray(d["jc"]).reshape(N, 8, 16 * B), axis=-1)
    if np.any(s[..., 1:] == s[..., :-1]): bad.append("courts of a group differ")
    return bad
def reference(rt, pk, jc, fx, sr):
    R = rt.astype(np.float32).astype(np.int32).reshape(N, 8, 16, W); f = fx.astype(np.float32).astype(np.int32).reshape(N, 8, 16, B)
    two = pk.astype(np.int32).reshape(N, 8, 16, C // 2); pf = np.concatenate([two & 4095, two >> 12], axis=3)
    J = jc.astype(np.int32).reshape(N, 8, 16, B); start = sr.astype(np.int32); Z = np.zeros(N, np.int32); rows = np.arange(16, dtype=np.int32)
    for t in range(VI):
        if t > 0:
            f = np.roll(f, 1, axis=0); J = np.roll(J, 1, axis=0); start = np.roll(start, 1, axis=0)
        m = np.zeros((N, 8, 16, B), np.int32); v = np.zeros((N, 8, 16, B), np.int32); num = np.zeros((N, 8, 16, B), np.int32)
        p = start; go = np.ones((N, 8, B), bool); first = np.zeros((N, 8, B), np.int32); new = np.zeros((N, 8, B), np.int32)
        for s in range(1, S + 1):
            c = np.take_along_axis(J, p[:, :, None, :], 2)
            n = np.take_along_axis(pf, np.broadcast_to(c, (N, 8, 16, B)), 3)
            x = np.take_along_axis(R, np.broadcast_to(n.reshape(N, 8, 1, 16 * B), (N, 8, 16, 16 * B)), 3).reshape(N, 8, 16, 16, B)
            dist = np.add.reduce(np.abs(x - f[:, :, :, None, :]), axis=2)
            k = np.argmin(dist, axis=2).astype(np.int32)
            kk = k[:, :, None, :]; nk = np.take_along_axis(n, kk, 2)
            rule = np.take_along_axis(R, np.broadcast_to(nk, (N, 8, 16, B)), 3)
            here = (rows[None, None, :, None] == p[:, :, None, :]) & go[:, :, None, :]
            v = np.where(here, kk, v); num = np.where(here, nk, num); m = np.where(here, np.int32(s), m)
            f = np.where(go[:, :, None, :], np.abs(f - rule), f)
            mk = np.take_along_axis(m, kk, 2)[:, :, 0]; nr = np.take_along_axis(num, kk, 2)
            shut = go & (mk > 0)
            tot = np.add.reduce(np.take_along_axis(R, np.broadcast_to(nr, (N, 8, 16, B)), 3), axis=2)
            odd = ((tot + Z[:, None, None]) & 1) == 1
            new = np.where(shut, np.where(odd, nk[:, :, 0], nr[:, :, 0]), new); first = np.where(shut, mk, first)
            go = go & ~shut; p = np.where(go, k, p)
        closed = first > 0
        loop = closed[:, :, None, :] & (m >= first[:, :, None, :])
        at = np.broadcast_to(J.reshape(N, 8, 1, 16 * B), (N, 8, 16, 16 * B))
        old = np.take_along_axis(pf, at, 3).reshape(N, 8, 16, 16, B)
        hit = loop[:, :, None] & (v[:, :, None] == rows[None, None, :, None, None])
        np.put_along_axis(pf, at, np.where(hit, new[:, :, None, None, :], old).reshape(N, 8, 16, 16 * B), 3)
        Z = Z + np.add.reduce(closed.astype(np.int32), axis=(1, 2))
    return {"yp": (pf[..., :C // 2] + 4096 * pf[..., C // 2:]).reshape(N, 128, C // 2).astype(np.float32), "yf": f.reshape(N, 128, B).astype(np.float32).astype(BF)}

@@ -1,0 +1,468 @@
+from concourse.mybir import dt, AluOpType, AxisListType, ActivationFunctionType
+import comms_topo
+
+AO = AluOpType
+AF = ActivationFunctionType
+CH = [(0, 5), (5, 8)]
+FE = {"v": (0, 3), "a": (3, 5), "b": (5, 8)}
+
+F32, BF, I32, U16 = "float32", "bfloat16", "int32", "uint16"
+SCRATCH = {}
+
+
+def _s(name, cols, dtype, where="sbuf"):
+    SCRATCH[name] = (where, [128] + (cols if isinstance(cols, list) else [cols]), dtype)
+
+
+for _n, _c, _d in [
+        ("R", 4096, BF), ("PF", 5136, F32), ("PK", 2048, I32), ("TI", 2048, I32), ("YO", 2048, F32),
+        ("JI", [16, 16], I32), ("JF", [16, 16], F32), ("JT", [16, 128], F32), ("SRI", 256, I32), ("SRB", 256, BF),
+        ("SRG", 256, BF), ("FX0", 256, BF), ("FIN1", 256, BF), ("FIN2", 256, BF),
+        ("FO0", 256, BF), ("FO1", 256, BF), ("FO2", 256, BF),
+        ("ST0", 288, F32), ("ST1", 288, F32), ("ST2", 288, F32),
+        ("FS", 4096, BF), ("WW", 8192, BF), ("A3", [16, 256], BF),
+        ("NU", 1024, U16), ("NHF", 1024, F32), ("NP", 1024, F32), ("OHM", 1024, F32), ("BB", 1024, F32), ("SEL", 256, F32), ("OHD", 256, F32),
+        ("SC", 1024, I32), ("KF", 16, I32), ("HK", 96, I32), ("OPN", 96, F32), ("LST", 64, F32),
+        ("CI", 128, I32), ("LW", 160, U16), ("OX", 16, F32), ("OXT", 16, F32), ("XLW", 16, F32),
+        ("T0", 16, F32), ("T1", 16, F32), ("T2", 16, F32), ("T3", 16, F32),
+        ("DP", 80, I32), ("AS", 80, I32), ("OD", 80, I32), ("CLB", 80, F32),
+        ("KSS", 80, F32), ("H16", 96, F32), ("EQB", 80, F32), ("GB", 80, F32), ("PG", 80, F32), ("UB", 80, F32),
+        ("QB", 400, F32), ("QS", 400, F32), ("DF", 32, F32), ("DG", 32, F32), ("RS", 32, F32), ("LJA", 16, F32), ("LJD", 16, U16), ("LKD", 16, U16),
+        ("KU", 80, F32), ("LC", 64, U16), ("Q0", 64, F32), ("Q1", 64, F32), ("Q2", 64, F32), ("SL", 64, U16),
+        ("ZR", 1, F32), ("ZA", 1, F32),
+        ("IM", 160, F32), ("IG", 128, F32), ("IPI", 2, I32), ("IQI", 2, I32), ("IGI", 2, I32), ("CF", 4, F32),
+        ("IDN", 128, F32), ("WB", 144, BF), ("BO", 128, F32), ("ONE", 128, F32), ("L8", 128, BF), ("MG", 8, F32), ("E16", 16, F32),
+        ("OHW", 32, F32), ("OHC", 32, F32), ("KEEP", 768, BF), ("RST", 128, F32), ("KEEP5", 400, F32), ("XRI", 128, I32), ("XREP", 128, U16),
+        ("IA", 16, F32), ("XL", 16, F32), ("TRI", 64, F32), ("TR", 64, F32), ("SI", 80, F32), ("PLC", 256, F32),
+        ("QK", 256, F32), ("XZ", 256, F32), ("XA", 256, F32), ("XB", 256, F32), ("XC", 256, F32)]:
+    _s(_n, _c, _d)
+for _n in ["KEY0", "KEY1", "AUX0", "AUX1", "HP0", "HP1", "HP2", "HP3"]:
+    _s(_n, 512, F32, "psum")
+
+SEMAPHORES = ["sv", "ss", "sp", "sg", "aS1", "aS2", "aF1", "aF2", "ls"] + ["d%d" % i for i in range(12)]
+
+
+def rank_program(g, core, T, topo):
+    rank = T.rank_of(core)
+    if rank is None:
+        return
+    nrank = len(T.cores)
+    ENG = {"V": (g.vector, "sv"), "S": (g.scalar, "ss"), "P": (g.tensor, "sp"), "G": (g, "sg"), "Y": (g.sync, None)}
+    cnt = {s: 0 for s in SEMAPHORES}
+    waited, Wr, Rd, ndma = {}, {}, {}, [0]
+
+    def need(e, sem, val):
+        if waited.get((e, sem), 0) < val:
+            ENG[e][0].wait_ge(T.sem[sem], val)
+            waited[(e, sem)] = val
+
+    def sync(e, reads, writes):
+        own, todo = ENG[e][1], {}
+        for k in reads:
+            for s, v in Wr.get(k, {}).items():
+                todo[s] = max(todo.get(s, 0), v)
+        for k in writes:
+            for s, v in Wr.get(k, {}).items():
+                todo[s] = max(todo.get(s, 0), v)
+            for s, v in Rd.get(k, {}).items():
+                if s != own:
+                    todo[s] = max(todo.get(s, 0), v)
+        for s, v in todo.items():
+            need(e, s, v)
+
+    def note(sem, val, reads, writes):
+        for k in reads:
+            Rd.setdefault(k, {})[sem] = val
+        for k in writes:
+            Wr.setdefault(k, {})[sem] = val
+
+    def run(e, reads, writes, name, *a, **kw):
+        reads, writes = reads.split(), writes.split()
+        sync(e, reads, writes)
+        q, sem = ENG[e]
+        ins = {"tc": lambda: q.tensor_copy(*a, **kw), "tt": lambda: q.tensor_tensor(*a, **kw), "ts": lambda: q.tensor_scalar(*a, **kw),
+               "scan": lambda: q.tensor_tensor_scan(*a, **kw), "memset": lambda: q.memset(*a, **kw), "red": lambda: q.tensor_reduce(*a, **kw),
+               "act": lambda: q.activation(*a, **kw), "mm": lambda: q.matmul(*a, **kw), "iota": lambda: q.iota(*a, **kw)}[name]()
+        cnt[sem] += 1
+        ins.then_inc(T.sem[sem], 1)
+        note(sem, cnt[sem], reads, writes)
+
+    def V(reads, writes, name, *a, **kw):
+        run("V", reads, writes, name, *a, **kw)
+
+    def S(reads, writes, out, in_, func, **kw):
+        run("S", reads, writes, "act", out, in_, func, **kw)
+
+    def mms(reads, writes, calls):
+        sync("P", reads.split(), writes.split())
+        for c in calls[:-1]:
+            g.tensor.matmul(*c)
+        run("P", reads, writes, "mm", *calls[-1])
+
+    def dma(e, reads, writes, out, in_):
+        reads, writes = reads.split(), writes.split()
+        sync(e, reads, writes)
+        sem = "d%d" % ndma[0]
+        ndma[0] += 1
+        ENG[e][0].dma_start(out, in_).then_inc(T.sem[sem], 16)
+        cnt[sem] = 16
+        note(sem, 16, reads, writes)
+
+    def send(dst_rank, src, dst, arr, key):
+        d = T.cores[dst_rank]
+        rid, pid, _ = topo.addr(d)
+        sync("G", [key], [])
+        g.remote_dma(out_ap=dst, in_ap=src, remote_sem=T.sem[arr], local_sem=T.sem["ls"], pid=pid, routing_id=rid,
+                     dma_engine_mask=topo.mask(core, d))
+        cnt["ls"] += len(topo.engines(core, d))
+
+    narr = len(topo.engines(core, T.cores[(rank + 1) % nrank]))
+
+    dma("Y", "", "JI", T.JI[:, :, :], T.jc[:])
+    dma("S", "", "SRI", T.SRI[0:8, :], T.sr[:])
+    dma("Y", "", "PK0", T.PK[:, 0:1024], T.pk[:, 0:1024])
+    dma("S", "", "FX0", T.FX0[:], T.fx[:])
+    dma("Y", "", "PK1", T.PK[:, 1024:2048], T.pk[:, 1024:2048])
+    dma("Y", "", "R", T.R[:], T.rt[:])
+
+    def iota(name, pat, base, cm, key=None):
+        run("G", "", key or name, "iota", T[name][:], pat, base, cm,
+            **({} if SCRATCH[name][2] == I32 else {"allow_small_or_imprecise_dtypes": True}))
+    iota("IPI", [[0, 2]], 0, 1)
+    iota("IM", [[1, 160]], 0, 0)
+    iota("IG", [[1, 8], [0, 16]], 0, 0)
+    iota("XZ", [[0, 256]], 0, 0)
+    iota("KEEP", [[0, 768]], 1, 0)
+    iota("QK", [[0, 16], [1, 16]], 0, 0)
+    iota("PLC", [[0, 16], [8192, 16]], -16777215, 0)
+    iota("XRI", [[16, 128]], 0, 0)
+    iota("IA", [[16, 16]], 0, 0)
+    iota("RST", [[0, 128]], 0, 0)
+    iota("FS", [[0, 4096]], 0, 0, "FS0 FS1")
+    iota("OPN", [[0, 96]], 1, 0)
+    iota("HK", [[0, 96]], 0, 0)
+    iota("TRI", [[256, 4], [16, 16]], 4097, 0)
+    iota("SI", [[0, 16], [256, 5]], 0, 0)
+    iota("KEEP5", [[0, 400]], 1, 0)
+    iota("ONE", [[0, 128]], 1, 0)
+    iota("AS", [[0, 80]], 0, 0)
+    iota("EQB", [[0, 80]], 0, 0)
+    iota("OHW", [[0, 32]], 0, 0)
+    iota("OHC", [[0, 32]], 1, 0)
+    V("IPI", "IQI", "ts", T.IQI[:], T.IPI[:], 15, None, AO.bitwise_and)
+    V("IPI", "IGI", "ts", T.IGI[:], T.IPI[:], 4, None, AO.arith_shift_right)
+    V("IPI", "CF0", "tc", T.CF[:, 0:1], T.IPI[:, 0:1])
+    V("IQI", "CF1", "tc", T.CF[:, 1:2], T.IQI[:, 0:1])
+    V("IGI", "CF2", "tc", T.CF[:, 2:3], T.IGI[:, 0:1])
+    V("IGI", "CF3", "ts", T.CF[:, 3:4], T.IGI[:, 0:1], 16.0, 15.0, AO.mult, AO.add)
+    p_c, q_c, g_c, e_c = [T.CF[:, i:i + 1] for i in range(4)]
+    V("IM CF2", "MG", "ts", T.MG[:], T.IM[:, 0:8], g_c, None, AO.is_equal)
+    V("IM CF3", "WB", "ts", T.WB[:, 0:143], T.IM[:, 0:143], e_c, 131072.0, AO.is_equal, AO.mult)
+    V("IM CF1", "E16", "ts", T.E16[:], T.IM[:, 0:16], q_c, None, AO.is_equal)
+    V("IG CF0", "L8", "ts", T.L8[0:8, :], T.IG[0:8, :], T.CF[0:8, 0:1], None, AO.is_equal)
+    V("IM CF0", "IDN", "ts", T.IDN[:], T.IM[:, 0:128], p_c, None, AO.is_equal)
+
+    def late_constants():
+        V("IG CF2", "BO", "ts", T.BO[:], T.IG[:], g_c, None, AO.is_equal)
+        V("IM CF1", "OHW", "ts", T.OHW[:, 16:32], T.IM[:, 0:16], q_c, None, AO.is_equal)
+        V("IM CF1", "OHC", "ts", T.OHC[:, 16:32], T.IM[:, 0:16], q_c, None, AO.not_equal)
+        V("TRI CF1", "TR", "ts", T.TR[:], T.TRI[:], q_c, None, AO.add)
+        V("", "KEEP5", "memset", T.KEEP5[:, 0::5], 0.0)
+
+    def unpack_hi(q):
+        c0, c1, k = 512 * q, 512 * q + 512, str(q)
+        V("PK%d" % (q // 2), "TI" + k, "ts", T.TI[:, c0:c1], T.PK[:, c0:c1], 12, None, AO.arith_shift_right)
+        V("PFT TI" + k, "PFH" + k, "tc", T.PF[:, 2049 + c0:2049 + c1], T.TI[:, c0:c1])
+        S("PFH" + k, "HP" + k, T["HP" + k][:], T.PF[:, 2049 + c0:2049 + c1], AF.Copy, scale=4096.0)
+
+    def unpack_lo(q):
+        c0, c1, k = 512 * q, 512 * q + 512, str(q)
+        V("PFT PK%d HP%s" % (q // 2, k), "PFL" + k, "tt", T.PF[:, 1 + c0:1 + c1], T.PK[:, c0:c1], T["HP" + k][:], AO.subtract)
+    PFA = "PFT " + " ".join("PFH%d PFL%d" % (q, q) for q in range(4))
+
+    V("JI", "JF", "tc", T.JF[:, :, :], T.JI[:, :, :])
+    for h in range(8):
+        S("JF MG", "JT%d" % h, T.JT[:, :, 16 * h:16 * h + 16], T.JF[:, :, :], AF.Identity, scale=T.MG[:, h:h + 1])
+    V("SRI", "SRB", "tc", T.SRB[0:8, :], T.SRI[0:8, :])
+    mms("L8 SRB", "AUX0", [(T.AUX0[:, 0:256], T.L8[0:8, :], T.SRB[0:8, :], True, True)])
+    V("", "PFT", "memset", T.PF[:, 0:16], 4096.0)
+    V("", "PFT", "memset", T.PF[:, 4096:4112], 0.0)
+    V("XRI", "XREP", "tc", T.XREP[:], T.XRI[:])
+    V("AUX0", "SRG", "tc", T.SRG[:], T.AUX0[:, 0:256])
+    mms("WB SRG", "AUX1", [(T.AUX1[:, 0:16], T.WB[:, 15 - b:143 - b], T.SRG[:, b::16], b == 0, b == 15) for b in range(16)])
+    mms("JT0 JT1 JT2 JT3 JT4 JT5 JT6 JT7 E16", "KEY1", [(T.KEY1[:, 16 * a:16 * a + 16], T.JT[:, a, :], T.E16[:], True, True) for a in range(16)])
+    V("KEEP", "KEEP", "memset", T.KEEP[:, 0::16], 0.0)
+    V("RST", "RST", "memset", T.RST[:, 0::16], 67108864.0)
+    V("IA CF1", "XL", "ts", T.XL[:], T.IA[:], q_c, None, AO.add)
+    V("XL", "XLW", "ts", T.XLW[:, 0:8], T.XL[:, 0:8], 16.0, None, AO.mult)
+    V("XL", "XLW", "ts", T.XLW[:, 8:16], T.XL[:, 0:8], 16.0, None, AO.mult)
+    V("AUX1 XZ", "XZ", "ts", T.XZ[:, 0::16], T.AUX1[:, 0:16], 2.0 ** -21, None, AO.mult)
+    V("AUX1", "ST0", "ts", T.ST0[:, 272:288], T.AUX1[:, 0:16], 2.0 ** -21, None, AO.mult)
+    V("KEEP XZ", "XA", "scan", T.XA[:], T.KEEP[:, 0:256], T.XZ[:], 0.0, AO.mult, AO.add)
+    V("XA QK", "XB", "tt", T.XB[:], T.XA[:], T.QK[:], AO.is_equal)
+    unpack_hi(0)
+    unpack_hi(1)
+    V("KEY1 XB", "XC", "tt", T.XC[:], T.KEY1[:, 0:256], T.XB[:], AO.mult)
+    V("KEY1 PLC", "ST0", "tt", T.ST0[:, 0:256], T.KEY1[:, 0:256], T.PLC[:], AO.add)
+    V("KEEP XC", "XA", "scan", T.XA[:], T.KEEP[:, 0:256], T.XC[:], 0.0, AO.mult, AO.add)
+    V("XA", "ST0", "ts", T.ST0[:, 256:272], T.XA[:, 15::16], 1.0, None, AO.add)
+    send((rank + 1) % nrank, T.ST0[:], T.ST1[:], "aS1", "ST0")
+    send((rank + 2) % nrank, T.ST0[:], T.ST2[:], "aS2", "ST0")
+    Wr["ST1"], Wr["ST2"] = {"aS1": narr}, {"aS2": narr}
+    Wr["FIN1"], Wr["FIN2"] = {"aF1": narr}, {"aF2": narr}
+
+    def a5(buf, X, s):
+        return buf[:, 40 * X + s:40 * X + 40:5]
+
+    def opn(s):
+        return T.OPN[:, s:80:5]
+
+    def win(X):
+        return T.WW[:, 4096 * X:4096 * X + 4096]
+
+    def lists_of_visit(t):
+        V("ST%d" % t, "LU01 LU11", "tc", T.LW[:, 8:24], T["ST%d" % t][:, 256:272])
+
+    unpack_lo(0)
+    unpack_hi(2)
+    unpack_lo(1)
+    unpack_hi(3)
+    unpack_lo(2)
+    lists_of_visit(0)
+    unpack_lo(3)
+    for t in range(3):
+        st, stk = T["ST%d" % t], "ST%d" % t
+        fin, fk = (T.FX0, "FX0") if t == 0 else (T["FIN%d" % t], "FIN%d" % t)
+        fo, fok = T["FO%d" % t], "FO%d" % t
+
+        def pf(X, s):
+            c0, l0 = 256 * s - 256 + 128 * X, 32 * s - 24 + 8 * X
+            V("%s LU%d%d" % (PFA, X, s), "NU%d%d" % (X, s), "tc", T.NU[:, c0:c0 + 128], T.PF[:, 0:4112].indirect(T.LW[:, l0:l0 + 8]))
+
+        def pay(X):
+            mms("IDN " + stk, "KEY%d" % X, [(T["KEY%d" % X][:, 0:128], T.IDN[:], st[:, 128 * X:128 * X + 128], True, False)])
+
+        def fe(X, i):
+            c0, c1 = 256 * FE[i][0], 256 * FE[i][1]
+            if i == "v":
+                V("KEEP FS%d" % X, "WF%dv" % X, "scan", T.WW[:, 4096 * X + c0:4096 * X + c1], T.KEEP[:, 0:c1 - c0],
+                  T.FS[:, 2048 * X + c0:2048 * X + c1], 0.0, AO.mult, AO.add)
+            else:
+                S("XREP FS%d" % X, "WF%d%s" % (X, i), T.WW[:, 4096 * X + c0:4096 * X + c1],
+                  T.FS[:, 2048 * X:2048 * X + 2048].indirect(T.XREP[:, c0 // 16:c1 // 16]), AF.Copy)
+
+        def gather(X, i, s):
+            c0, c1, n0 = 256 * CH[i][0], 256 * CH[i][1], 256 * s - 256 + 128 * X
+            V("R %s NU%d%d" % ("WF%dv WF%da" % (X, X) if i == 0 else "WF%db" % X, X, s), "WD%d%d" % (X, i), "tt",
+              T.WW[:, 4096 * X + 2048 + c0:4096 * X + 2048 + c1],
+              T.R[:, 0:4096].indirect(T.NU[:, n0 + c0 // 16:n0 + c1 // 16]), T.WW[:, 4096 * X + c0:4096 * X + c1], AO.subtract)
+
+        def dist(X, i):
+            a0, a1 = CH[i]
+            S("WD%d%d" % (X, i), "A%d%d" % (X, i), T.A3[:, 8 * X + a0:8 * X + a1, :], T.WW[:, 4096 * X + 2048 + 256 * a0:4096 * X + 2048 + 256 * a1], AF.Abs)
+            mms("WB A%d%d" % (X, i), "KEY%d" % X, [(T["KEY%d" % X][:, 16 * a0:16 * a1], T.WB[:, 15 - b:143 - b],
+                T.A3[:, 8 * X + a0:8 * X + a1, 16 * b:16 * b + 16], False, i == len(CH) - 1 and b == 15) for b in range(16)])
+
+        def nh(s):
+            S("%s LU0%d LU1%d" % (PFA, s, s), "NH%d" % s, T.NHF[:, 256 * s - 256:256 * s], T.PF[:, 0:4112].indirect(T.LW[:, 32 * s - 24:32 * s - 8]), AF.Copy)
+
+        def choose(X, s, fill=(), last=()):
+            k, c0, i0 = "%d%d" % (X, s), 256 * s - 256 + 128 * X, 32 * s - 32
+            fa, cc = (i0, i0 + 8) if X == 0 else (i0 + 24, i0 + 16)
+            key, fill, last = T.SC[:, c0 + 15:c0 + 128:16], list(fill), list(last)
+
+            def some(n):
+                while len(fill) > n:
+                    fill.pop(0)()
+            V("RST KEY%d" % X, "SC" + k, "scan", T.SC[:, c0:c0 + 128], T.RST[:], T["KEY%d" % X][:, 0:128], 0.0, AO.add, AO.min)
+            mixed = len(fill) >= 3
+            some(3 if len(fill) > 3 else 2 if mixed else 0)
+            V("SC" + k, "HK" + k, "ts", a5(T.HK, X, s), key, 13, 15, AO.arith_shift_right, AO.bitwise_and)
+            some(2)
+            if s < 4:
+                V("SC" + k, "CC" + k, "ts", T.CI[:, cc:cc + 8], key, 8191, None, AO.bitwise_and)
+            some(1)
+            for f in last[:1]:
+                f()
+            if mixed:
+                if s < 4:
+                    V("CC" + k, "LU%d%d" % (X, s + 1), "tc", T.LW[:, 32 + cc:40 + cc], T.CI[:, cc:cc + 8])
+                some(0)
+                if s < 4:
+                    pf(X, s + 1)
+            V("OX HK" + k, "FA" + k, "tt", T.CI[:, fa:fa + 8], a5(T.HK, X, s), T.OX[:, 8 * X:8 * X + 8], AO.add)
+            if s < 4 and not mixed:
+                V("CC" + k, "LU%d%d" % (X, s + 1), "tc", T.LW[:, 32 + cc:40 + cc], T.CI[:, cc:cc + 8])
+            for f in last[1:]:
+                f()
+            V("FA" + k, "FL%d" % X, "tc", T.LW[:, 32 + fa:40 + fa], T.CI[:, fa:fa + 8])
+            rd, fl = "FL%d WF%dv WF%da WF%db WD%d0 WD%d1" % (X, X, X, X, X, X), T.LW[:, 32 + fa:40 + fa]
+            if s < 4:
+                S(rd, "FS%d" % X, T.FS[:, 2048 * X:2048 * X + 2048:16], win(X).indirect(fl), AF.Abs)
+                if not mixed:
+                    pf(X, s + 1)
+                pay(X)
+            else:
+                S(rd, fok, fo[:, 128 * X:128 * X + 128], win(X).indirect(fl), AF.Abs)
+
+        def keep(s):
+            H = [T.HK[:, j:80:5] for j in range(5)]
+            hk = ["HK0%d HK1%d" % (j, j) for j in range(5)]
+            todo = []
+
+            def later(*a):
+                todo.append(lambda: V(*a))
+
+            def ne(j, out, key):
+                later(hk[s] + " " + hk[j], key, "tt", out, H[s], H[j], AO.not_equal)
+
+            def mul(out, x, y, ko, kx, ky):
+                later(kx + " " + ky, ko, "tt", out, x, y, AO.mult)
+            t0, t1, t2, t3 = T.T0[:], T.T1[:], T.T2[:], T.T3[:]
+            if s == 1:
+                ne(0, opn(1), "OPN1")
+            else:
+                for j in range(s):
+                    ne(j, T["T%d" % j][:], "T%d" % j)
+                if s == 2:
+                    mul(t0, t0, opn(1), "T0", "T0", "OPN1")
+                    mul(opn(2), t0, t1, "OPN2", "T0", "T1")
+                elif s == 3:
+                    mul(t0, t0, t1, "T0", "T0", "T1")
+                    mul(t2, t2, opn(2), "T2", "T2", "OPN2")
+                    mul(opn(3), t0, t2, "OPN3", "T0", "T2")
+                else:
+                    mul(t0, t0, t1, "T0", "T0", "T1")
+                    mul(t2, t2, t3, "T2", "T2", "T3")
+                    mul(t0, t0, opn(3), "T0", "T0", "OPN3")
+                    mul(opn(4), t0, t2, "OPN4", "T0", "T2")
+            if s < 4:
+                later("OPN%d" % s, "OXT", "ts", T.OXT[:], opn(s), 2048.0, None, AO.mult)
+                later("OXT XLW", "OX", "tt", T.OX[:], T.OXT[:], T.XLW[:], AO.add)
+                later("CC0%d CC1%d OPN%d" % (s, s, s), "LST%d" % (s + 1), "tt", T.LST[:, 16 * s:16 * s + 16], T.CI[:, 32 * s - 24:32 * s - 8], opn(s), AO.mult)
+            later("SC0%d SC1%d" % (s, s), "DP%d" % s, "ts", T.DP[:, s:80:5], T.SC[:, 256 * s - 241:256 * s:16], 17, 1, AO.arith_shift_right, AO.bitwise_and)
+            return todo
+
+        pay(0)
+        pay(1)
+        for X in range(2):
+            S(fk, "FS%d" % X, T.FS[:, 2048 * X:2048 * X + 2048:16], fin[:, 128 * X:128 * X + 128], AF.Copy)
+        mms("WB " + fk, "AUX1", [(T.AUX1[:, 0:16], T.WB[:, 15 - b:143 - b], fin[:, b::16], b == 0, b == 15) for b in range(16)])
+        fe(0, "a")
+        fe(0, "b")
+        fe(1, "a")
+        spare = []
+        for s in range(1, 5):
+            for X in range(2):
+                fe(X, "v")
+                if s == 1 and X == 0:
+                    pf(0, 1)
+                    pf(1, 1)
+                elif s == 1:
+                    V(stk, "LST1", "tc", T.LST[:, 0:16], st[:, 256:272])
+                elif spare:
+                    spare.pop()()
+                gather(X, 0, s)
+                dist(X, 0)
+                if X == 1 and s < 4:
+                    k2 = keep(s - 1) if s > 1 else []
+                    choose(0, s, k2[:-2])
+                    spare.extend(k2[-2:])
+                    fe(0, "a")
+                elif X == 0 and s > 1:
+                    choose(1, s - 1)
+                    fe(1, "a")
+                gather(X, 1, s)
+                dist(X, 1)
+                if X == 0 or s < 4:
+                    fe(1 - X, "b")
+                if X == 0 and s == 1:
+                    V("AUX1", "KF", "tc", T.KF[:], T.AUX1[:, 0:16])
+                    V("HK " + stk, "HK00 HK10", "tc", T.HK[:, 0:80:5], st[:, 272:288])
+                    V("XLW", "OX", "ts", T.OX[:], T.XLW[:], 2048.0, None, AO.add)
+                    V("KF", "DP0", "ts", T.DP[:, 0:80:5], T.KF[:], 17, 1, AO.arith_shift_right, AO.bitwise_and)
+                if X == 1:
+                    nh(s)
+        k3 = keep(3)
+        choose(0, 4, k3[:-2])
+        if t == 0:
+            late_constants()
+        for f in spare + k3[-2:]:
+            f()
+        LSA = "LST1 LST2 LST3 LST4"
+        choose(1, 4, [lambda: V(LSA, "Q0", "ts", T.Q0[:], T.LST[:], 0.0, None, AO.is_equal)],
+               [lambda: V("Q0 TR", "Q1", "tt", T.Q1[:], T.Q0[:], T.TR[:], AO.mult),
+                lambda: V("Q1 " + LSA, "Q2", "tt", T.Q2[:], T.Q1[:], T.LST[:], AO.add)])
+        if t < 2:
+            send((rank + 1) % nrank, fo[:], T["FIN%d" % (t + 1)][:], "aF%d" % (t + 1), fok)
+        else:
+            dma("Y", fok, "yf", T.yf[:], fo[:])
+        HKA = "HK " + " ".join("HK%d%d" % (X, s) for X in range(2) for s in range(5))
+        OPA, NHA = "OPN OPN1 OPN2 OPN3 OPN4", "NH1 NH2 NH3 NH4"
+        Q = [T.QB[:, 80 * i:80 * i + 80] for i in range(5)]
+        k4 = keep(4)
+        for f in k4[:6]:
+            f()
+        V("Q2", "SL", "tc", T.SL[:], T.Q2[:])
+        V(HKA, "H16", "ts", T.H16[:, 0:81], T.HK[:, 0:81], 16.0, None, AO.add)
+        k4[6]()
+        k4[8]()
+        if t < 2:
+            lists_of_visit(t + 1)
+        k4[7]()
+        V("DP0 DP1 DP2 DP3 DP4 AS", "AS", "tt", T.AS[:, 0:79], T.DP[:, 0:79], T.DP[:, 1:80], AO.add)
+        V(OPA, "CLB", "tt", T.CLB[:], T.OPN[:, 0:80], T.OPN[:, 1:81], AO.subtract)
+        if t > 0:
+            V("AS ZA", "AS", "ts", T.AS[:], T.AS[:], T.ZA[:, 0:1], None, AO.add)
+        V("CLB H16", "QB3", "tt", Q[3], T.CLB[:], T.H16[:, 1:81], AO.mult)
+        V("CLB SI", "QB2", "tt", Q[2], T.CLB[:], T.SI[:], AO.mult)
+        V("KEEP5 QB3", "KSS", "scan", T.KSS[:], T.KEEP5[:, 0:80], Q[3], 0.0, AO.mult, AO.add)
+        V("AS", "OD", "ts", T.OD[:], T.AS[:], 1, None, AO.bitwise_and)
+        for j in range(4):
+            V("H16 KSS EQB", "EQ%d" % j, "tt", T.EQB[:, j::5], T.H16[:, j:80:5], T.KSS[:, 3::5], AO.is_equal)
+        if t < 2:
+            V(OPA, "ZR", "red", T.ZR[:, 0:1], T.OPN[:, 4:80:5], AxisListType.X, AO.add)
+        V("EQB EQ0 EQ1 EQ2 EQ3 " + OPA, "GB", "tt", T.GB[:], T.EQB[:], T.OPN[:, 0:80], AO.mult)
+        V("GB SI", "QB0", "tt", Q[0], T.GB[:], T.SI[:], AO.mult)
+        V("GB H16", "QB1", "tt", Q[1], T.GB[:], T.H16[:, 1:81], AO.mult)
+        V("GB OD", "QB4", "tt", Q[4], T.GB[:], T.OD[:], AO.mult)
+        V("KEEP5 GB", "PG", "scan", T.PG[:], T.KEEP5[:, 0:80], T.GB[:], 0.0, AO.mult, AO.add)
+        V("KEEP5 QB0 QB1 QB2 QB3 QB4", "QS", "scan", T.QS[:], T.KEEP5[:], T.QB[:], 0.0, AO.mult, AO.add)
+        V("PG " + OPA, "UB", "tt", T.UB[:], T.PG[:], T.OPN[:, 0:80], AO.mult)
+        V("QS", "DF", "tt", T.DF[:], T.QS[:, 163:320:5], T.QS[:, 3:160:5], AO.subtract)
+        V("UB H16", "KU", "tt", T.KU[:], T.UB[:], T.H16[:, 1:81], AO.mult)
+        V("DF QS", "DG1", "tt", T.DG[:, 16:32], T.DF[:, 16:32], T.QS[:, 323:400:5], AO.mult)
+        V("DF QS", "DG0", "tt", T.DG[:, 0:16], T.DF[:, 0:16], T.QS[:, 323:400:5], AO.mult)
+        V("KU", "LC0", "tc", T.LC[:, 0:16], T.KU[:, 0::5])
+        V("DG0 DG1 QS", "RS", "tt", T.RS[:], T.DG[:], T.QS[:, 3:160:5], AO.add)
+        V("KU", "LC1", "tc", T.LC[:, 16:32], T.KU[:, 1::5])
+        V("RS", "LKD", "tc", T.LKD[:], T.RS[:, 16:32])
+        V("RS XL", "LJA", "tt", T.LJA[:], T.RS[:, 0:16], T.XL[:], AO.add)
+        S("OHW LKD", "OHD", T.OHD[:], T.OHW[:, 0:32].indirect(T.LKD[:, 0:16]), AF.Copy)
+        V("KU", "LC2", "tc", T.LC[:, 32:48], T.KU[:, 2::5])
+        V("LJA", "LJD", "tc", T.LJD[:], T.LJA[:])
+        V("KU", "LC3", "tc", T.LC[:, 48:64], T.KU[:, 3::5])
+        S("OHW LC0 LC1 LC2 LC3", "OHM", T.OHM[:], T.OHW[:, 0:32].indirect(T.LC[:, 0:64]), AF.Copy)
+        V("OHD LJD " + NHA, "SEL", "tt", T.SEL[:], T.NHF[:, 0:1024].indirect(T.LJD[:, 0:16]), T.OHD[:], AO.mult)
+        mms("BO SEL", "AUX0", [(T.AUX0[:, 0:256], T.BO[:], T.SEL[:], True, True)])
+        if t < 2:
+            mms("ONE ZR", "AUX1", [(T.AUX1[:, 0:1], T.ONE[:], T.ZR[:, 0:1], True, True)])
+        V("OHC LC0 LC1 LC2 LC3 " + NHA, "NP", "tt", T.NP[:], T.OHC[:, 0:32].indirect(T.LC[:, 0:64]), T.NHF[:], AO.mult)
+        for s in range(4):
+            V("AUX0 OHM", "BB%d" % s, "tt", T.BB[:, 256 * s:256 * s + 256], T.AUX0[:, 0:256], T.OHM[:, 256 * s:256 * s + 256], AO.mult)
+        if t == 0:
+            V("AUX1", "ZA", "tc", T.ZA[:, 0:1], T.AUX1[:, 0:1])
+        elif t == 1:
+            V("AUX1 ZA", "ZA", "tt", T.ZA[:, 0:1], T.AUX1[:, 0:1], T.ZA[:, 0:1], AO.add)
+        V("NP BB0 BB1 BB2 BB3 SL", PFA, "tt", T.PF[:, 0:5136].indirect(T.SL[:, 0:64]), T.NP[:], T.BB[:], AO.add)
+    for q in range(4):
+        c0, c1, k = 512 * q, 512 * q + 512, str(q)
+        S("PFH" + k, "HP" + k, T["HP" + k][:], T.PF[:, 2049 + c0:2049 + c1], AF.Copy, scale=4096.0)
+        V("HP%s PFL%s" % (k, k), "YO" + k, "tt", T.YO[:, c0:c1], T["HP" + k][:], T.PF[:, 1 + c0:1 + c1], AO.add)
+        dma("Y", "YO" + k, "yp", T.yp[:, c0:c1], T.YO[:, c0:c1])
+    for sem in SEMAPHORES:
+        if cnt[sem] and sem != "ls":
+            need("G", sem, cnt[sem])
+    need("G", "ls", cnt["ls"])
+    for sem in ("aS1", "aS2", "aF1", "aF2"):
+        need("G", sem, narr)

@@ -3,8 +3,11 @@ import comms_topo
 
 AO = AluOpType
 AF = ActivationFunctionType
-CH = [(0, 5), (5, 8)]
-FE = {"v": (0, 3), "a": (3, 5), "b": (5, 8)}
+SHARE = {None: (88, 128), 0: (64, 128), 1: (96, 128), 7: (72, 96)}
+PHASE = {"C": -0.45, "F": -0.40, "T": -0.25, "A": -0.15, "L0": -0.12, "G0": 0.00, "G1": 0.03, "S": 0.06, "G2": 0.09, "P0": 0.12, "Z0": 0.14,
+         "K": 0.16, "L1": 0.20, "P1": 0.25, "L2": 0.30, "P2": 0.35, "G3": 0.40, "Z1": 0.45, "Z2": 0.50, "L3": 0.52, "P3": 0.54,
+         "U0": 0.80, "Z3": 0.90, "U1": 1.18}
+HITS = [(s, j, odd) for s in (4, 3, 2, 1) for j in range(s) for odd in range(2 if j < s - 1 else 1)]
 
 F32, BF, I32, U16 = "float32", "bfloat16", "int32", "uint16"
 SCRATCH = {}
@@ -15,31 +18,37 @@ def _s(name, cols, dtype, where="sbuf"):
 
 
 for _n, _c, _d in [
-        ("R", 4096, BF), ("PF", 5136, F32), ("PK", 2048, I32), ("TI", 2048, I32), ("YO", 2048, F32),
-        ("JI", [16, 16], I32), ("JF", [16, 16], F32), ("JT", [16, 128], F32), ("SRI", 256, I32), ("SRB", 256, BF),
-        ("SRG", 256, BF), ("FX0", 256, BF), ("FIN1", 256, BF), ("FIN2", 256, BF),
-        ("FO0", 256, BF), ("FO1", 256, BF), ("FO2", 256, BF),
-        ("ST0", 288, F32), ("ST1", 288, F32), ("ST2", 288, F32),
-        ("FS", 4096, BF), ("WW", 8192, BF), ("A3", [16, 256], BF),
-        ("NU", 1024, U16), ("NHF", 1024, F32), ("NP", 1024, F32), ("OHM", 1024, F32), ("BB", 1024, F32), ("SEL", 256, F32), ("OHD", 256, F32),
-        ("SC", 1024, I32), ("KF", 16, I32), ("HK", 96, I32), ("OPN", 96, F32), ("LST", 64, F32),
-        ("CI", 128, I32), ("LW", 160, U16), ("OX", 16, F32), ("OXT", 16, F32), ("XLW", 16, F32),
-        ("T0", 16, F32), ("T1", 16, F32), ("T2", 16, F32), ("T3", 16, F32),
-        ("DP", 80, I32), ("AS", 80, I32), ("OD", 80, I32), ("CLB", 80, F32),
-        ("KSS", 80, F32), ("H16", 96, F32), ("EQB", 80, F32), ("GB", 80, F32), ("PG", 80, F32), ("UB", 80, F32),
-        ("QB", 400, F32), ("QS", 400, F32), ("DF", 32, F32), ("DG", 32, F32), ("RS", 32, F32), ("LJA", 16, F32), ("LJD", 16, U16), ("LKD", 16, U16),
-        ("KU", 80, F32), ("LC", 64, U16), ("Q0", 64, F32), ("Q1", 64, F32), ("Q2", 64, F32), ("SL", 64, U16),
+        ("R", 4096, BF), ("PF", 4864, F32), ("PK", 2048, I32), ("TI", 2048, I32), ("YO", 2048, F32),
+        ("JI", 256, I32), ("JQ", [16, 16], F32), ("JT", [16, 128], F32), ("SRI", 256, I32), ("SRB", 256, BF),
+        ("MS", 256, F32), ("JM", 256, F32), ("K0", 16, I32), ("K1", 32, I32),
+        ("FX0", 256, BF), ("FIN1", 256, BF), ("FIN2", 256, BF), ("FO0", 256, BF), ("FO1", 256, BF), ("FO2", 256, BF),
+        ("ST0", 304, F32), ("ST1", 304, F32), ("ST2", 304, F32),
+        ("RG", 8192, BF), ("A", [256, 17], BF), ("FH", 1024, BF), ("FT", 256, BF), ("FD", 256, BF),
+        ("NU", 256, U16), ("SC", 1088, I32), ("H5", 80, I32), ("CB", 64, I32), ("FA", 16, I32), ("LC", 16, U16), ("LF", 16, U16),
+        ("DV", 64, I32), ("AS", 48, I32), ("AZ", 48, I32), ("OD", 48, I32), ("HJ", 48, I32), ("HM", 48, I32), ("C16", 64, F32), ("C16T", 64, F32),
+        ("NE", 272, F32), ("CD", 272, F32), ("CO", 272, I32), ("CW", 64, I32),
+        ("CH", 64, I32), ("DC", 64, I32), ("PP", 64, F32), ("PT", 64, F32), ("PC", 64, F32), ("PD", 64, F32), ("D1", 32, F32),
+        ("YY", 48, F32), ("VV", 64, I32), ("VU", 128, I32), ("LE", 128, U16), ("FI", 16, I32), ("LO", 16, U16),
+        ("OHD", 256, F32), ("SEL", 256, F32), ("OC", 768, F32), ("OM", 768, F32), ("NP", 768, F32), ("BB", 768, F32),
         ("ZR", 1, F32), ("ZA", 1, F32),
-        ("IM", 160, F32), ("IG", 128, F32), ("IPI", 2, I32), ("IQI", 2, I32), ("IGI", 2, I32), ("CF", 4, F32),
-        ("IDN", 128, F32), ("WB", 144, BF), ("BO", 128, F32), ("ONE", 128, F32), ("L8", 128, BF), ("MG", 8, F32), ("E16", 16, F32),
-        ("OHW", 32, F32), ("OHC", 32, F32), ("KEEP", 768, BF), ("RST", 128, F32), ("KEEP5", 400, F32), ("XRI", 128, I32), ("XREP", 128, U16),
-        ("IA", 16, F32), ("XL", 16, F32), ("TRI", 64, F32), ("TR", 64, F32), ("SI", 80, F32), ("PLC", 256, F32),
-        ("QK", 256, F32), ("XZ", 256, F32), ("XA", 256, F32), ("XB", 256, F32), ("XC", 256, F32)]:
+        ("IM", 160, F32), ("IG", 128, F32), ("IPI", 2, I32), ("IQI", 6, I32), ("CF", 8, F32), ("XN", 512, BF), ("ND", 512, BF),
+        ("IDB", 128, BF), ("WB", 144, BF), ("WF", 144, F32), ("BO", 128, F32), ("ONE", 128, F32), ("L8", 128, BF), ("MG", 8, F32),
+        ("OHW", 24, F32), ("OHC", 16, F32), ("E17", 17, F32), ("IA", 16, F32), ("XQ", 16, F32), ("X16", 8, F32),
+        ("TRI", 64, F32), ("TR", 64, F32)]:
     _s(_n, _c, _d)
-for _n in ["KEY0", "KEY1", "AUX0", "AUX1", "HP0", "HP1", "HP2", "HP3"]:
+for _n in ["KEY0", "KEY1", "AUX", "DB0", "DB1", "DB2", "DB3"]:
     _s(_n, 512, F32, "psum")
+_s("FTP", 1024, BF, "psum")
 
-SEMAPHORES = ["sv", "ss", "sp", "sg", "aS1", "aS2", "aF1", "aF2", "ls"] + ["d%d" % i for i in range(12)]
+SEMAPHORES = ["sv", "ss", "sp", "sg", "aS1", "aS2", "aF1", "aF2", "ls"] + ["d%d" % i for i in range(14)]
+
+
+def codes():
+    out = [3 << 16]
+    for s, j, odd in HITS:
+        d = s if odd else j + 1
+        out.append(sum(8 >> (u - 1) for u in range(j + 1, s + 1) if u != d) + (128 >> (d - 1)) + ((s - 1) << 16))
+    return out
 
 
 def rank_program(g, core, T, topo):
@@ -50,6 +59,7 @@ def rank_program(g, core, T, topo):
     ENG = {"V": (g.vector, "sv"), "S": (g.scalar, "ss"), "P": (g.tensor, "sp"), "G": (g, "sg"), "Y": (g.sync, None)}
     cnt = {s: 0 for s in SEMAPHORES}
     waited, Wr, Rd, ndma = {}, {}, {}, [0]
+    DB = [T.DB0, T.DB1, T.DB2, T.DB3]
 
     def need(e, sem, val):
         if waited.get((e, sem), 0) < val:
@@ -57,7 +67,7 @@ def rank_program(g, core, T, topo):
             waited[(e, sem)] = val
 
     def sync(e, reads, writes):
-        own, todo = ENG[e][1], {}
+        todo = {}
         for k in reads:
             for s, v in Wr.get(k, {}).items():
                 todo[s] = max(todo.get(s, 0), v)
@@ -65,8 +75,7 @@ def rank_program(g, core, T, topo):
             for s, v in Wr.get(k, {}).items():
                 todo[s] = max(todo.get(s, 0), v)
             for s, v in Rd.get(k, {}).items():
-                if s != own:
-                    todo[s] = max(todo.get(s, 0), v)
+                todo[s] = max(todo.get(s, 0), v)
         for s, v in todo.items():
             need(e, s, v)
 
@@ -82,7 +91,8 @@ def rank_program(g, core, T, topo):
         q, sem = ENG[e]
         ins = {"tc": lambda: q.tensor_copy(*a, **kw), "tt": lambda: q.tensor_tensor(*a, **kw), "ts": lambda: q.tensor_scalar(*a, **kw),
                "scan": lambda: q.tensor_tensor_scan(*a, **kw), "memset": lambda: q.memset(*a, **kw), "red": lambda: q.tensor_reduce(*a, **kw),
-               "act": lambda: q.activation(*a, **kw), "mm": lambda: q.matmul(*a, **kw), "iota": lambda: q.iota(*a, **kw)}[name]()
+               "act": lambda: q.activation(*a, **kw), "mm": lambda: q.matmul(*a, **kw), "iota": lambda: q.iota(*a, **kw),
+               "tr": lambda: q.transpose(*a, **kw)}[name]()
         cnt[sem] += 1
         ins.then_inc(T.sem[sem], 1)
         note(sem, cnt[sem], reads, writes)
@@ -111,355 +121,302 @@ def rank_program(g, core, T, topo):
     def send(dst_rank, src, dst, arr, key):
         d = T.cores[dst_rank]
         rid, pid, _ = topo.addr(d)
-        sync("G", [key], [])
+        sync("G", key.split(), [])
         g.remote_dma(out_ap=dst, in_ap=src, remote_sem=T.sem[arr], local_sem=T.sem["ls"], pid=pid, routing_id=rid,
                      dma_engine_mask=topo.mask(core, d))
         cnt["ls"] += len(topo.engines(core, d))
 
     narr = len(topo.engines(core, T.cores[(rank + 1) % nrank]))
 
-    dma("Y", "", "JI", T.JI[:, :, :], T.jc[:])
+    dma("Y", "", "JI", T.JI[:], T.jc[:])
     dma("S", "", "SRI", T.SRI[0:8, :], T.sr[:])
     dma("Y", "", "PK0", T.PK[:, 0:1024], T.pk[:, 0:1024])
     dma("S", "", "FX0", T.FX0[:], T.fx[:])
     dma("Y", "", "PK1", T.PK[:, 1024:2048], T.pk[:, 1024:2048])
     dma("Y", "", "R", T.R[:], T.rt[:])
 
-    def iota(name, pat, base, cm, key=None):
-        run("G", "", key or name, "iota", T[name][:], pat, base, cm,
-            **({} if SCRATCH[name][2] == I32 else {"allow_small_or_imprecise_dtypes": True}))
-    iota("IPI", [[0, 2]], 0, 1)
-    iota("IM", [[1, 160]], 0, 0)
-    iota("IG", [[1, 8], [0, 16]], 0, 0)
-    iota("XZ", [[0, 256]], 0, 0)
-    iota("KEEP", [[0, 768]], 1, 0)
-    iota("QK", [[0, 16], [1, 16]], 0, 0)
-    iota("PLC", [[0, 16], [8192, 16]], -16777215, 0)
-    iota("XRI", [[16, 128]], 0, 0)
-    iota("IA", [[16, 16]], 0, 0)
-    iota("RST", [[0, 128]], 0, 0)
-    iota("FS", [[0, 4096]], 0, 0, "FS0 FS1")
-    iota("OPN", [[0, 96]], 1, 0)
-    iota("HK", [[0, 96]], 0, 0)
-    iota("TRI", [[256, 4], [16, 16]], 4097, 0)
-    iota("SI", [[0, 16], [256, 5]], 0, 0)
-    iota("KEEP5", [[0, 400]], 1, 0)
-    iota("ONE", [[0, 128]], 1, 0)
-    iota("AS", [[0, 80]], 0, 0)
-    iota("EQB", [[0, 80]], 0, 0)
-    iota("OHW", [[0, 32]], 0, 0)
-    iota("OHC", [[0, 32]], 1, 0)
-    V("IPI", "IQI", "ts", T.IQI[:], T.IPI[:], 15, None, AO.bitwise_and)
-    V("IPI", "IGI", "ts", T.IGI[:], T.IPI[:], 4, None, AO.arith_shift_right)
+    def iota(key, out, pat, base, cm=0):
+        run("G", "", key, "iota", out, pat, base, cm, allow_small_or_imprecise_dtypes=True)
+    run("G", "", "IPI", "iota", T.IPI[:], [[0, 2]], 0, 1)
+    iota("IM", T.IM[:], [[1, 160]], 0)
+    iota("IG", T.IG[:], [[1, 8], [0, 16]], 0)
+    iota("IA", T.IA[:], [[16, 16]], 0)
+    iota("XN", T.XN[:], [[1, 32], [0, 16]], 0)
+    iota("A17", T.A[:, :, 16], [[0, 256]], 255)
+    V("IPI", "IQ0", "ts", T.IQI[:, 0:2], T.IPI[:], 15, None, AO.bitwise_and)
+    V("IPI", "IQ1", "ts", T.IQI[:, 2:4], T.IPI[:], 4, None, AO.arith_shift_right)
+    V("IPI", "IQ2", "ts", T.IQI[:, 4:6], T.IPI[:], 31, None, AO.bitwise_and)
     V("IPI", "CF0", "tc", T.CF[:, 0:1], T.IPI[:, 0:1])
-    V("IQI", "CF1", "tc", T.CF[:, 1:2], T.IQI[:, 0:1])
-    V("IGI", "CF2", "tc", T.CF[:, 2:3], T.IGI[:, 0:1])
-    V("IGI", "CF3", "ts", T.CF[:, 3:4], T.IGI[:, 0:1], 16.0, 15.0, AO.mult, AO.add)
-    p_c, q_c, g_c, e_c = [T.CF[:, i:i + 1] for i in range(4)]
-    V("IM CF2", "MG", "ts", T.MG[:], T.IM[:, 0:8], g_c, None, AO.is_equal)
-    V("IM CF3", "WB", "ts", T.WB[:, 0:143], T.IM[:, 0:143], e_c, 131072.0, AO.is_equal, AO.mult)
-    V("IM CF1", "E16", "ts", T.E16[:], T.IM[:, 0:16], q_c, None, AO.is_equal)
+    V("IQ0 IQ1 IQ2", "CF1", "tc", T.CF[:, 1:4], T.IQI[:, 0:6:2])
+    V("IQ1", "CF4", "ts", T.CF[:, 4:5], T.IQI[:, 2:3], 16.0, 15.0, AO.mult, AO.add)
+    V("IQ0", "CF5", "ts", T.CF[:, 5:6], T.IQI[:, 0:1], 4096.0, None, AO.mult)
+    p_c, q_c, g_c, r_c, e_c, k_c = [T.CF[:, i:i + 1] for i in range(6)]
+    V("IM CF1", "MG", "ts", T.MG[:], T.IM[:, 0:8], g_c, None, AO.is_equal)
     V("IG CF0", "L8", "ts", T.L8[0:8, :], T.IG[0:8, :], T.CF[0:8, 0:1], None, AO.is_equal)
-    V("IM CF0", "IDN", "ts", T.IDN[:], T.IM[:, 0:128], p_c, None, AO.is_equal)
+    V("IM CF1", "OHW", "ts", T.OHW[:], T.IM[:, 0:24], q_c, None, AO.is_equal)
+    V("IM CF4", "WF", "ts", T.WF[:, 0:143], T.IM[:, 0:143], e_c, None, AO.is_equal)
+    V("OHW", "E17a", "tt", T.E17[:, 1:17], T.OHW[:, 0:16], T.OHW[:, 1:17], AO.subtract)
+    V("OHW", "E17b", "ts", T.E17[:, 0:1], T.OHW[:, 15:16], 1024.0, None, AO.mult)
+    V("IM CF4", "WB", "ts", T.WB[:, 0:143], T.IM[:, 0:143], e_c, 65536.0, AO.is_equal, AO.mult)
+    V("IM CF0", "IDB", "ts", T.IDB[:], T.IM[:, 0:128], p_c, None, AO.is_equal)
+    V("IA CF1", "XQ", "ts", T.XQ[:], T.IA[:], q_c, None, AO.add)
+    V("XN CF1", "ND", "ts", T.ND[:], T.XN[:], r_c, -1.0, AO.is_equal, AO.mult)
+    V("XQ", "X16", "ts", T.X16[:], T.XQ[:, 0:8], 16.0, None, AO.mult)
 
     def late_constants():
-        V("IG CF2", "BO", "ts", T.BO[:], T.IG[:], g_c, None, AO.is_equal)
-        V("IM CF1", "OHW", "ts", T.OHW[:, 16:32], T.IM[:, 0:16], q_c, None, AO.is_equal)
-        V("IM CF1", "OHC", "ts", T.OHC[:, 16:32], T.IM[:, 0:16], q_c, None, AO.not_equal)
-        V("TRI CF1", "TR", "ts", T.TR[:], T.TRI[:], q_c, None, AO.add)
-        V("", "KEEP5", "memset", T.KEEP5[:, 0::5], 0.0)
+        iota("PFT", T.PF[:, 4096:4864], [[0, 768]], 0)
+        iota("TRIa", T.TRI[:, 0:48], [[16, 48]], 4096)
+        iota("TRIb", T.TRI[:, 48:64], [[16, 16]], 4096)
+        iota("ONE", T.ONE[:], [[0, 128]], 1)
+        iota("NE", T.NE[:, 0::17], [[0, 16]], 0)
+        c = codes()
+        for i in range(16):
+            iota("CD%d" % i, T.CD[:, i::17], [[0, 16]], c[i] - c[i + 1])
+
+    def late_constants_v():
+        return [lambda: V("IG CF1", "BO", "ts", T.BO[:], T.IG[:], g_c, None, AO.is_equal),
+                lambda: V("IM CF1", "OHC", "ts", T.OHC[:], T.IM[:, 0:16], q_c, None, AO.not_equal),
+                lambda: V("TRIa TRIb CF1", "TR", "ts", T.TR[:], T.TRI[:], q_c, 16.0, AO.add, AO.mult),
+                lambda: V("XQ", "CD16", "ts", T.CD[:, 16::17], T.XQ[:], 256.0, float(codes()[16]), AO.mult, AO.add),
+                lambda: V("TR", "YY", "tc", T.YY[:], T.TR[:, 0:48])]
+    CDA = " ".join("CD%d" % i for i in range(17))
 
     def unpack_hi(q):
         c0, c1, k = 512 * q, 512 * q + 512, str(q)
         V("PK%d" % (q // 2), "TI" + k, "ts", T.TI[:, c0:c1], T.PK[:, c0:c1], 12, None, AO.arith_shift_right)
-        V("PFT TI" + k, "PFH" + k, "tc", T.PF[:, 2049 + c0:2049 + c1], T.TI[:, c0:c1])
-        S("PFH" + k, "HP" + k, T["HP" + k][:], T.PF[:, 2049 + c0:2049 + c1], AF.Copy, scale=4096.0)
+        V("TI" + k, "PFH" + k, "tc", T.PF[:, 2048 + c0:2048 + c1], T.TI[:, c0:c1])
+        S("PFH" + k, "DB" + k, DB[q][:], T.PF[:, 2048 + c0:2048 + c1], AF.Copy, scale=4096.0)
 
     def unpack_lo(q):
         c0, c1, k = 512 * q, 512 * q + 512, str(q)
-        V("PFT PK%d HP%s" % (q // 2, k), "PFL" + k, "tt", T.PF[:, 1 + c0:1 + c1], T.PK[:, c0:c1], T["HP" + k][:], AO.subtract)
-    PFA = "PFT " + " ".join("PFH%d PFL%d" % (q, q) for q in range(4))
+        V("PK%d DB%s" % (q // 2, k), "PFL" + k, "tt", T.PF[:, c0:c1], T.PK[:, c0:c1], DB[q][:], AO.subtract)
+    PFA = " ".join("PFH%d PFL%d" % (q, q) for q in range(4))
 
-    V("JI", "JF", "tc", T.JF[:, :, :], T.JI[:, :, :])
+    V("JI CF5", "JQ", "ts", T.JQ[:, :, :], T.JI[:], k_c, None, AO.add)
     for h in range(8):
-        S("JF MG", "JT%d" % h, T.JT[:, :, 16 * h:16 * h + 16], T.JF[:, :, :], AF.Identity, scale=T.MG[:, h:h + 1])
+        S("JQ MG", "JT%d" % h, T.JT[:, :, 16 * h:16 * h + 16], T.JQ[:, :, :], AF.Identity, scale=T.MG[:, h:h + 1])
     V("SRI", "SRB", "tc", T.SRB[0:8, :], T.SRI[0:8, :])
-    mms("L8 SRB", "AUX0", [(T.AUX0[:, 0:256], T.L8[0:8, :], T.SRB[0:8, :], True, True)])
-    V("", "PFT", "memset", T.PF[:, 0:16], 4096.0)
-    V("", "PFT", "memset", T.PF[:, 4096:4112], 0.0)
-    V("XRI", "XREP", "tc", T.XREP[:], T.XRI[:])
-    V("AUX0", "SRG", "tc", T.SRG[:], T.AUX0[:, 0:256])
-    mms("WB SRG", "AUX1", [(T.AUX1[:, 0:16], T.WB[:, 15 - b:143 - b], T.SRG[:, b::16], b == 0, b == 15) for b in range(16)])
-    mms("JT0 JT1 JT2 JT3 JT4 JT5 JT6 JT7 E16", "KEY1", [(T.KEY1[:, 16 * a:16 * a + 16], T.JT[:, a, :], T.E16[:], True, True) for a in range(16)])
-    V("KEEP", "KEEP", "memset", T.KEEP[:, 0::16], 0.0)
-    V("RST", "RST", "memset", T.RST[:, 0::16], 67108864.0)
-    V("IA CF1", "XL", "ts", T.XL[:], T.IA[:], q_c, None, AO.add)
-    V("XL", "XLW", "ts", T.XLW[:, 0:8], T.XL[:, 0:8], 16.0, None, AO.mult)
-    V("XL", "XLW", "ts", T.XLW[:, 8:16], T.XL[:, 0:8], 16.0, None, AO.mult)
-    V("AUX1 XZ", "XZ", "ts", T.XZ[:, 0::16], T.AUX1[:, 0:16], 2.0 ** -21, None, AO.mult)
-    V("AUX1", "ST0", "ts", T.ST0[:, 272:288], T.AUX1[:, 0:16], 2.0 ** -21, None, AO.mult)
-    V("KEEP XZ", "XA", "scan", T.XA[:], T.KEEP[:, 0:256], T.XZ[:], 0.0, AO.mult, AO.add)
-    V("XA QK", "XB", "tt", T.XB[:], T.XA[:], T.QK[:], AO.is_equal)
+    mms("L8 SRB", "AUX", [(T.AUX[:, 0:256], T.L8[0:8, :], T.SRB[0:8, :], True, True)])
+    V("AUX CF1", "MS", "ts", T.MS[:], T.AUX[:, 0:256], q_c, None, AO.is_equal)
+    V("MS JQ", "JM", "tt", T.JM[:], T.MS[:], T.JQ[:, :, :], AO.mult)
+    mms("WF JM", "KEY0a KEY0b", [(T.KEY0[:, 0:16], T.WF[:, 15 - b:143 - b], T.JM[:, b::16], b == 0, b == 15) for b in range(16)])
+    mms("JT0 JT1 JT2 JT3 JT4 JT5 JT6 JT7 E17a E17b", "KEY1a KEY1b",
+        [(T.KEY1[:, 17 * a:17 * a + 17], T.JT[:, a, :], T.E17[:], True, True) for a in range(16)])
     unpack_hi(0)
     unpack_hi(1)
-    V("KEY1 XB", "XC", "tt", T.XC[:], T.KEY1[:, 0:256], T.XB[:], AO.mult)
-    V("KEY1 PLC", "ST0", "tt", T.ST0[:, 0:256], T.KEY1[:, 0:256], T.PLC[:], AO.add)
-    V("KEEP XC", "XA", "scan", T.XA[:], T.KEEP[:, 0:256], T.XC[:], 0.0, AO.mult, AO.add)
-    V("XA", "ST0", "ts", T.ST0[:, 256:272], T.XA[:, 15::16], 1.0, None, AO.add)
-    send((rank + 1) % nrank, T.ST0[:], T.ST1[:], "aS1", "ST0")
-    send((rank + 2) % nrank, T.ST0[:], T.ST2[:], "aS2", "ST0")
-    Wr["ST1"], Wr["ST2"] = {"aS1": narr}, {"aS2": narr}
+    S("KEY1a KEY1b", "ST0", T.ST0[:, 0:272], T.KEY1[:, 0:272], AF.Copy)
+    V("KEY0a KEY0b", "K0", "tc", T.K0[:], T.KEY0[:, 0:16])
+    unpack_lo(0)
+    V("K0", "K1a", "ts", T.K1[:, 0:16], T.K0[:], 4095, None, AO.bitwise_and)
+    V("K0", "K1b", "ts", T.K1[:, 16:32], T.K0[:], 12, None, AO.arith_shift_right)
+    unpack_lo(1)
+    V("K1a K1b", "SU0", "tc", T.ST0[:, 272:304], T.K1[:])
+    send((rank + 1) % nrank, T.ST0[:], T.ST1[:], "aS1", "ST0 SU0")
+    send((rank + 2) % nrank, T.ST0[:], T.ST2[:], "aS2", "ST0 SU0")
+    late_constants()
+    Wr["ST1"], Wr["ST2"], Wr["SU1"], Wr["SU2"] = {"aS1": narr}, {"aS2": narr}, {"aS1": narr}, {"aS2": narr}
     Wr["FIN1"], Wr["FIN2"] = {"aF1": narr}, {"aF2": narr}
 
-    def a5(buf, X, s):
-        return buf[:, 40 * X + s:40 * X + 40:5]
+    def first_courts(t):
+        V("SU%d" % t, "LC0 LC1", "tc", T.LC[:], T["ST%d" % t][:, 272:288])
 
-    def opn(s):
-        return T.OPN[:, s:80:5]
+    def turn(X, src, key):
+        run("P", "IDB " + key, "FTP", "tr", T.FTP[:, 0:128], src[:, 128 * X:128 * X + 128], T.IDB[:])
 
-    def win(X):
-        return T.WW[:, 4096 * X:4096 * X + 4096]
+    def turned(X):
+        S("FTP", "FT%d" % X, T.FT[:, 128 * X:128 * X + 128], T.FTP[:, 0:128], AF.Abs)
 
-    def lists_of_visit(t):
-        V("ST%d" % t, "LU01 LU11", "tc", T.LW[:, 8:24], T["ST%d" % t][:, 256:272])
+    def first_facts(fin, fk):
+        for X in range(2):
+            turn(X, fin, fk)
+            turned(X)
+        mms("WB " + fk, "AUX", [(T.AUX[:, 0:16], T.WB[:, 15 - b:143 - b], fin[:, b::16], b == 0, b == 15) for b in range(16)])
 
-    unpack_lo(0)
+    first_facts(T.FX0, "FX0")
     unpack_hi(2)
-    unpack_lo(1)
     unpack_hi(3)
     unpack_lo(2)
-    lists_of_visit(0)
+    first_courts(0)
     unpack_lo(3)
     for t in range(3):
-        st, stk = T["ST%d" % t], "ST%d" % t
+        st, stk, suk = T["ST%d" % t], "ST%d" % t, "SU%d" % t
         fin, fk = (T.FX0, "FX0") if t == 0 else (T["FIN%d" % t], "FIN%d" % t)
         fo, fok = T["FO%d" % t], "FO%d" % t
 
-        def pf(X, s):
-            c0, l0 = 256 * s - 256 + 128 * X, 32 * s - 24 + 8 * X
-            V("%s LU%d%d" % (PFA, X, s), "NU%d%d" % (X, s), "tc", T.NU[:, c0:c0 + 128], T.PF[:, 0:4112].indirect(T.LW[:, l0:l0 + 8]))
+        def pf(X):
+            V("%s LC%d" % (PFA, X), "NU%d" % X, "tc", T.NU[:, 128 * X:128 * X + 128], T.PF[:, 0:4096].indirect(T.LC[:, 8 * X:8 * X + 8]))
 
-        def pay(X):
-            mms("IDN " + stk, "KEY%d" % X, [(T["KEY%d" % X][:, 0:128], T.IDN[:], st[:, 128 * X:128 * X + 128], True, False)])
-
-        def fe(X, i):
-            c0, c1 = 256 * FE[i][0], 256 * FE[i][1]
-            if i == "v":
-                V("KEEP FS%d" % X, "WF%dv" % X, "scan", T.WW[:, 4096 * X + c0:4096 * X + c1], T.KEEP[:, 0:c1 - c0],
-                  T.FS[:, 2048 * X + c0:2048 * X + c1], 0.0, AO.mult, AO.add)
+        def rules(e, n, x0, x1):
+            if x0 >= x1:
+                return
+            X, w = n % 2, n % 4
+            wr = " ".join("RG%d%d%s" % (w, j, e) for j in range(x0 // 32, (x1 + 31) // 32))
+            out, src = T.RG[:, 2048 * w + 16 * x0:2048 * w + 16 * x1], T.R[:, 0:4096].indirect(T.NU[:, 128 * X + x0:128 * X + x1])
+            if e == "V":
+                V("R NU%d" % X, wr, "tc", out, src)
             else:
-                S("XREP FS%d" % X, "WF%d%s" % (X, i), T.WW[:, 4096 * X + c0:4096 * X + c1],
-                  T.FS[:, 2048 * X:2048 * X + 2048].indirect(T.XREP[:, c0 // 16:c1 // 16]), AF.Copy)
+                S("R NU%d" % X, wr, out, src, AF.Copy)
 
-        def gather(X, i, s):
-            c0, c1, n0 = 256 * CH[i][0], 256 * CH[i][1], 256 * s - 256 + 128 * X
-            V("R %s NU%d%d" % ("WF%dv WF%da" % (X, X) if i == 0 else "WF%db" % X, X, s), "WD%d%d" % (X, i), "tt",
-              T.WW[:, 4096 * X + 2048 + c0:4096 * X + 2048 + c1],
-              T.R[:, 0:4096].indirect(T.NU[:, n0 + c0 // 16:n0 + c1 // 16]), T.WW[:, 4096 * X + c0:4096 * X + c1], AO.subtract)
+        def less(X, j):
+            sync("P", ["FT%d" % X, "ND"], ["DB%d" % j])
+            g.tensor.matmul(DB[j][:], T.FT[32 * j:32 * j + 32, 128 * X:128 * X + 128], T.ND[32 * j:32 * j + 32, :], True, False)
 
-        def dist(X, i):
-            a0, a1 = CH[i]
-            S("WD%d%d" % (X, i), "A%d%d" % (X, i), T.A3[:, 8 * X + a0:8 * X + a1, :], T.WW[:, 4096 * X + 2048 + 256 * a0:4096 * X + 2048 + 256 * a1], AF.Abs)
-            mms("WB A%d%d" % (X, i), "KEY%d" % X, [(T["KEY%d" % X][:, 16 * a0:16 * a1], T.WB[:, 15 - b:143 - b],
-                T.A3[:, 8 * X + a0:8 * X + a1, 16 * b:16 * b + 16], False, i == len(CH) - 1 and b == 15) for b in range(16)])
+        def plus(w, j):
+            run("P", "FT%d ND IDB RG%d%dV RG%d%dS" % (w % 2, w, j, w, j), "DB%d" % j, "mm",
+                DB[j][:], T.IDB[:], T.RG[:, 2048 * w + 512 * j:2048 * w + 512 * j + 512], False, True)
 
-        def nh(s):
-            S("%s LU0%d LU1%d" % (PFA, s, s), "NH%d" % s, T.NHF[:, 256 * s - 256:256 * s], T.PF[:, 0:4112].indirect(T.LW[:, 32 * s - 24:32 * s - 8]), AF.Copy)
+        def size(X, j):
+            S("DB%d" % j, "A%d%d" % (X, j), T.A[:, 128 * X + 32 * j:128 * X + 32 * j + 32, 0:16], DB[j][:], AF.Abs)
 
-        def choose(X, s, fill=(), last=()):
-            k, c0, i0 = "%d%d" % (X, s), 256 * s - 256 + 128 * X, 32 * s - 32
-            fa, cc = (i0, i0 + 8) if X == 0 else (i0 + 24, i0 + 16)
-            key, fill, last = T.SC[:, c0 + 15:c0 + 128:16], list(fill), list(last)
+        def sums(X, h):
+            x0 = 128 * X + 64 * h
+            mms("WB A17 A%d%d A%d%d" % (X, 2 * h, X, 2 * h + 1), "KEY%d%s" % (X, "ab"[h]),
+                [(T["KEY%d" % X][:, 68 * h:68 * h + 68], T.WB[:, 15 - b:143 - b], T.A[:, x0 + b:x0 + 64:16, :], b == 0, b == 15) for b in range(16)])
 
-            def some(n):
-                while len(fill) > n:
-                    fill.pop(0)()
-            V("RST KEY%d" % X, "SC" + k, "scan", T.SC[:, c0:c0 + 128], T.RST[:], T["KEY%d" % X][:, 0:128], 0.0, AO.add, AO.min)
-            mixed = len(fill) >= 3
-            some(3 if len(fill) > 3 else 2 if mixed else 0)
-            V("SC" + k, "HK" + k, "ts", a5(T.HK, X, s), key, 13, 15, AO.arith_shift_right, AO.bitwise_and)
-            some(2)
+        def choose(X, s, fill=(), mid=(), tail=()):
+            k, c0, fill = "%d%d" % (X, s), 272 * (s - 1) + 136 * X, list(fill)
+            key, a, sa = T.SC[:, c0 + 16:c0 + 136:17], slice(8 * X, 8 * X + 8), slice(16 * s + 8 * X, 16 * s + 8 * X + 8)
+            V("%s KEY%da KEY%db" % (stk, X, X), "SC" + k, "scan", T.SC[:, c0:c0 + 136], st[:, 136 * X:136 * X + 136],
+              T["KEY%d" % X][:, 0:136], 0.0, AO.add, AO.min)
+            if fill:
+                fill.pop(0)()
+            V("SC" + k, "H" + k, "ts", T.H5[:, sa], key, 12, 15, AO.arith_shift_right, AO.bitwise_and)
             if s < 4:
-                V("SC" + k, "CC" + k, "ts", T.CI[:, cc:cc + 8], key, 8191, None, AO.bitwise_and)
-            some(1)
-            for f in last[:1]:
-                f()
-            if mixed:
-                if s < 4:
-                    V("CC" + k, "LU%d%d" % (X, s + 1), "tc", T.LW[:, 32 + cc:40 + cc], T.CI[:, cc:cc + 8])
-                some(0)
-                if s < 4:
-                    pf(X, s + 1)
-            V("OX HK" + k, "FA" + k, "tt", T.CI[:, fa:fa + 8], a5(T.HK, X, s), T.OX[:, 8 * X:8 * X + 8], AO.add)
-            if s < 4 and not mixed:
-                V("CC" + k, "LU%d%d" % (X, s + 1), "tc", T.LW[:, 32 + cc:40 + cc], T.CI[:, cc:cc + 8])
-            for f in last[1:]:
-                f()
-            V("FA" + k, "FL%d" % X, "tc", T.LW[:, 32 + fa:40 + fa], T.CI[:, fa:fa + 8])
-            rd, fl = "FL%d WF%dv WF%da WF%db WD%d0 WD%d1" % (X, X, X, X, X, X), T.LW[:, 32 + fa:40 + fa]
+                V("SC" + k, "C%d%d" % (X, s + 1), "ts", T.CB[:, sa], key, 4095, None, AO.bitwise_and)
+            if fill:
+                fill.pop(0)()
+            V("X16 H" + k, "FA%d" % X, "tt", T.FA[:, a], T.H5[:, sa], T.X16[:], AO.add)
             if s < 4:
-                S(rd, "FS%d" % X, T.FS[:, 2048 * X:2048 * X + 2048:16], win(X).indirect(fl), AF.Abs)
-                if not mixed:
-                    pf(X, s + 1)
-                pay(X)
-            else:
-                S(rd, fok, fo[:, 128 * X:128 * X + 128], win(X).indirect(fl), AF.Abs)
+                V("C%d%d" % (X, s + 1), "LC%d" % X, "tc", T.LC[:, a], T.CB[:, sa])
+            for f in fill + list(mid):
+                f()
+            V("FA%d" % X, "LF%d" % X, "tc", T.LF[:, a], T.FA[:, a])
+            if s < 4:
+                pf(X)
+            for f in tail:
+                f()
 
-        def keep(s):
-            H = [T.HK[:, j:80:5] for j in range(5)]
-            hk = ["HK0%d HK1%d" % (j, j) for j in range(5)]
-            todo = []
+        def facts(X, s):
+            f0 = 256 * (s - 1) + 128 * X
+            old, ok = (fin[:, 128 * X:128 * X + 128], fk) if s == 1 else (T.FH[:, f0 - 256:f0 - 128], "FH%d%d" % (X, s - 1))
+            out, key = (T.FD[:, 128 * X:128 * X + 128], "FD%d" % X) if s < 4 else (T.FH[:, f0:f0 + 128], "FH%d4" % X)
+            w = (2 * s - 2 + X) % 4
+            V("LF%d %s " % (X, ok) + " ".join("RG%d%d%s" % (w, j, e) for j in range(4) for e in "VS"), key, "tt", out,
+              T.RG[:, 2048 * w:2048 * w + 2048].indirect(T.LF[:, 8 * X:8 * X + 8]), old, AO.subtract)
 
-            def later(*a):
-                todo.append(lambda: V(*a))
+        def kept(X, s):
+            f0 = 256 * (s - 1) + 128 * X
+            S("FD%d" % X, "FH%d%d" % (X, s), T.FH[:, f0:f0 + 128], T.FD[:, 128 * X:128 * X + 128], AF.Abs)
 
-            def ne(j, out, key):
-                later(hk[s] + " " + hk[j], key, "tt", out, H[s], H[j], AO.not_equal)
+        def both(k, s):
+            return "%s0%d %s1%d" % (k, s, k, s)
 
-            def mul(out, x, y, ko, kx, ky):
-                later(kx + " " + ky, ko, "tt", out, x, y, AO.mult)
-            t0, t1, t2, t3 = T.T0[:], T.T1[:], T.T2[:], T.T3[:]
-            if s == 1:
-                ne(0, opn(1), "OPN1")
-            else:
-                for j in range(s):
-                    ne(j, T["T%d" % j][:], "T%d" % j)
-                if s == 2:
-                    mul(t0, t0, opn(1), "T0", "T0", "OPN1")
-                    mul(opn(2), t0, t1, "OPN2", "T0", "T1")
-                elif s == 3:
-                    mul(t0, t0, t1, "T0", "T0", "T1")
-                    mul(t2, t2, opn(2), "T2", "T2", "OPN2")
-                    mul(opn(3), t0, t2, "OPN3", "T0", "T2")
+        def miss(i):
+            s, j, odd = HITS[i]
+            row, key = (T.H5, both("H", j)) if j == s - 1 else (T.HM, "HM") if odd else (T.HJ, "HJ")
+            return lambda: V("NE %s %s" % (both("H", s), key), "NE%d" % i, "tt", T.NE[:, i + 1::17],
+                             row[:, 16 * j:16 * j + 16], T.H5[:, 16 * s:16 * s + 16], AO.not_equal)
+        HA = " ".join(both("H", s) for s in range(3))
+        CA = " ".join(both("C", s) for s in range(1, 5))
+        loops = [i for i, (s, j, odd) in enumerate(HITS) if j == s - 1 and s < 4]
+        early = [lambda: V(" ".join(both("SC", s) for s in (1, 2, 3)), "DV1", "ts", T.DV[:, 16:64], T.SC[:, 16:816:17], 16, None, AO.arith_shift_right),
+                 lambda: V("DV0 DV1", "AS", "tt", T.AS[:], T.DV[:, 0:48], T.DV[:, 16:64], AO.add),
+                 lambda: V("AS ZA", "AZ", "ts", T.AZ[:], T.AS[:], T.ZA[:, 0:1] if t else 0.0, 16.0, AO.add, AO.mult),
+                 lambda: V("AZ", "OD", "ts", T.OD[:], T.AZ[:], 16, None, AO.bitwise_and),
+                 lambda: V(CA, "C16", "ts", T.C16[:], T.CB[:], 16.0, None, AO.mult), miss(loops[0]),
+                 lambda: V("OD " + HA, "HJ", "tt", T.HJ[:], T.H5[:, 0:48], T.OD[:], AO.add),
+                 lambda: V("C16 TR", "C16T", "tt", T.C16T[:], T.C16[:], T.TR[:], AO.subtract),
+                 lambda: V("HJ", "HM", "ts", T.HM[:], T.HJ[:], 16.0, None, AO.subtract), miss(loops[1]), miss(loops[2])]
+        early += [miss(i) for i in range(7, 16) if i not in loops]
+        late = [miss(i) for i in range(7)]
+        lc = late_constants_v() if t == 0 else []
+        fills = {(0, 1): [lambda: V(suk, both("H", 0), "tc", T.H5[:, 0:16], st[:, 288:304])],
+                 (1, 1): [lambda: V(suk, both("C", 1), "tc", T.CB[:, 0:16], st[:, 272:288])],
+                 (0, 2): [lambda: V("AUX", "DV0", "ts", T.DV[:, 0:16], T.AUX[:, 0:16], 2.0 ** -16, None, AO.mult)],
+                 (1, 2): lc[0:1], (0, 3): lc[1:3], (1, 3): lc[3:]}
+
+        def call(name, n):
+            X, s, j = n % 2, n // 2 + 1, int(name[1:] or 0)
+            s0, s1 = SHARE.get(n, SHARE[None])
+            if name == "C":
+                if n < 2:
+                    pf(X)
                 else:
-                    mul(t0, t0, t1, "T0", "T0", "T1")
-                    mul(t2, t2, t3, "T2", "T2", "T3")
-                    mul(t0, t0, opn(3), "T0", "T0", "OPN3")
-                    mul(opn(4), t0, t2, "OPN4", "T0", "T2")
-            if s < 4:
-                later("OPN%d" % s, "OXT", "ts", T.OXT[:], opn(s), 2048.0, None, AO.mult)
-                later("OXT XLW", "OX", "tt", T.OX[:], T.OXT[:], T.XLW[:], AO.add)
-                later("CC0%d CC1%d OPN%d" % (s, s, s), "LST%d" % (s + 1), "tt", T.LST[:, 16 * s:16 * s + 16], T.CI[:, 32 * s - 24:32 * s - 8], opn(s), AO.mult)
-            later("SC0%d SC1%d" % (s, s), "DP%d" % s, "ts", T.DP[:, s:80:5], T.SC[:, 256 * s - 241:256 * s:16], 17, 1, AO.arith_shift_right, AO.bitwise_and)
-            return todo
-
-        pay(0)
-        pay(1)
-        for X in range(2):
-            S(fk, "FS%d" % X, T.FS[:, 2048 * X:2048 * X + 2048:16], fin[:, 128 * X:128 * X + 128], AF.Copy)
-        mms("WB " + fk, "AUX1", [(T.AUX1[:, 0:16], T.WB[:, 15 - b:143 - b], fin[:, b::16], b == 0, b == 15) for b in range(16)])
-        fe(0, "a")
-        fe(0, "b")
-        fe(1, "a")
-        spare = []
-        for s in range(1, 5):
-            for X in range(2):
-                fe(X, "v")
-                if s == 1 and X == 0:
-                    pf(0, 1)
-                    pf(1, 1)
-                elif s == 1:
-                    V(stk, "LST1", "tc", T.LST[:, 0:16], st[:, 256:272])
-                elif spare:
-                    spare.pop()()
-                gather(X, 0, s)
-                dist(X, 0)
-                if X == 1 and s < 4:
-                    k2 = keep(s - 1) if s > 1 else []
-                    choose(0, s, k2[:-2])
-                    spare.extend(k2[-2:])
-                    fe(0, "a")
-                elif X == 0 and s > 1:
-                    choose(1, s - 1)
-                    fe(1, "a")
-                gather(X, 1, s)
-                dist(X, 1)
-                if X == 0 or s < 4:
-                    fe(1 - X, "b")
-                if X == 0 and s == 1:
-                    V("AUX1", "KF", "tc", T.KF[:], T.AUX1[:, 0:16])
-                    V("HK " + stk, "HK00 HK10", "tc", T.HK[:, 0:80:5], st[:, 272:288])
-                    V("XLW", "OX", "ts", T.OX[:], T.XLW[:], 2048.0, None, AO.add)
-                    V("KF", "DP0", "ts", T.DP[:, 0:80:5], T.KF[:], 17, 1, AO.arith_shift_right, AO.bitwise_and)
-                if X == 1:
-                    nh(s)
-        k3 = keep(3)
-        choose(0, 4, k3[:-2])
-        if t == 0:
-            late_constants()
-        for f in spare + k3[-2:]:
+                    choose(X, s - 1, fills[(X, s - 1)])
+            elif name in "FKTA":
+                if n >= 2:
+                    {"F": lambda: facts(X, s - 1), "K": lambda: kept(X, s - 1), "T": lambda: turn(X, T.FD, "FD%d" % X), "A": lambda: turned(X)}[name]()
+            elif name == "S":
+                rules("S", n, s0, s1)
+            elif name[0] == "G":
+                rules("V", n, 32 * j, min(s0, 32 * j + 32))
+                rules("V", n, max(s1, 32 * j), 32 * j + 32)
+            elif name[0] == "P":
+                plus(n % 4, j)
+            else:
+                {"L": less, "Z": size, "U": sums}[name[0]](X, j)
+        for _, name, n in sorted((n + ph, name, n) for n in range(8) for name, ph in PHASE.items()):
+            call(name, n)
+        choose(0, 4, early[:3])
+        facts(0, 4)
+        for f in early[3:]:
             f()
-        LSA = "LST1 LST2 LST3 LST4"
-        choose(1, 4, [lambda: V(LSA, "Q0", "ts", T.Q0[:], T.LST[:], 0.0, None, AO.is_equal)],
-               [lambda: V("Q0 TR", "Q1", "tt", T.Q1[:], T.Q0[:], T.TR[:], AO.mult),
-                lambda: V("Q1 " + LSA, "Q2", "tt", T.Q2[:], T.Q1[:], T.LST[:], AO.add)])
+        choose(1, 4, [], late[:2], late[2:])
+        H4 = " ".join(both("H", s) for s in range(1, 5))
+        V("C16 " + H4, "PP", "tt", T.PP[:], T.H5[:, 16:80], T.C16[:], AO.add)
+        V("NE %s %s" % (" ".join("NE%d" % i for i in range(16)), CDA), "CO", "scan", T.CO[:], T.NE[:], T.CD[:], 0.0, AO.mult, AO.add)
+        facts(1, 4)
+        V("CO", "FI", "ts", T.FI[:], T.CO[:, 16::17], 8, None, AO.arith_shift_right)
+        for u in range(4):
+            V("CO", "CW%d" % u, "ts", T.CW[:, 16 * u:16 * u + 16], T.CO[:, 16::17], 2.0 ** u, None, AO.mult)
+        V("FI", "LO", "tc", T.LO[:], T.FI[:])
+        V("C16T " + H4, "PT", "tt", T.PT[:], T.H5[:, 16:80], T.C16T[:], AO.add)
+        V("CW0 CW1 CW2 CW3", "DC", "ts", T.DC[:], T.CW[:], 7, 1, AO.arith_shift_right, AO.bitwise_and)
+        V("CW0 CW1 CW2 CW3", "CH", "ts", T.CH[:], T.CW[:], 3, 1, AO.arith_shift_right, AO.bitwise_and)
+        S("LO " + " ".join(both("FH", s) for s in range(1, 5)), fok, fo[:], T.FH[:, 0:1024].indirect(T.LO[:]), AF.Abs)
         if t < 2:
             send((rank + 1) % nrank, fo[:], T["FIN%d" % (t + 1)][:], "aF%d" % (t + 1), fok)
+            first_courts(t + 1)
         else:
             dma("Y", fok, "yf", T.yf[:], fo[:])
-        HKA = "HK " + " ".join("HK%d%d" % (X, s) for X in range(2) for s in range(5))
-        OPA, NHA = "OPN OPN1 OPN2 OPN3 OPN4", "NH1 NH2 NH3 NH4"
-        Q = [T.QB[:, 80 * i:80 * i + 80] for i in range(5)]
-        k4 = keep(4)
-        for f in k4[:6]:
-            f()
-        V("Q2", "SL", "tc", T.SL[:], T.Q2[:])
-        V(HKA, "H16", "ts", T.H16[:, 0:81], T.HK[:, 0:81], 16.0, None, AO.add)
-        k4[6]()
-        k4[8]()
+        V("DC PP", "PD", "tt", T.PD[:], T.DC[:], T.PP[:], AO.mult)
+        V("CH PT", "PC", "tt", T.PC[:], T.CH[:], T.PT[:], AO.mult)
+        V("PD", "D1", "tt", T.D1[:], T.PD[:, 0:32], T.PD[:, 32:64], AO.add)
+        V("PC TR YY", "YY", "tt", T.YY[:, 0:16], T.PC[:, 48:64], T.TR[:, 0:16], AO.add)
         if t < 2:
-            lists_of_visit(t + 1)
-        k4[7]()
-        V("DP0 DP1 DP2 DP3 DP4 AS", "AS", "tt", T.AS[:, 0:79], T.DP[:, 0:79], T.DP[:, 1:80], AO.add)
-        V(OPA, "CLB", "tt", T.CLB[:], T.OPN[:, 0:80], T.OPN[:, 1:81], AO.subtract)
-        if t > 0:
-            V("AS ZA", "AS", "ts", T.AS[:], T.AS[:], T.ZA[:, 0:1], None, AO.add)
-        V("CLB H16", "QB3", "tt", Q[3], T.CLB[:], T.H16[:, 1:81], AO.mult)
-        V("CLB SI", "QB2", "tt", Q[2], T.CLB[:], T.SI[:], AO.mult)
-        V("KEEP5 QB3", "KSS", "scan", T.KSS[:], T.KEEP5[:, 0:80], Q[3], 0.0, AO.mult, AO.add)
-        V("AS", "OD", "ts", T.OD[:], T.AS[:], 1, None, AO.bitwise_and)
-        for j in range(4):
-            V("H16 KSS EQB", "EQ%d" % j, "tt", T.EQB[:, j::5], T.H16[:, j:80:5], T.KSS[:, 3::5], AO.is_equal)
+            V("DC", "ZR", "red", T.ZR[:, 0:1], T.DC[:], AxisListType.X, AO.add)
+        V("D1", "VVa", "tt", T.VV[:, 0:16], T.D1[:, 0:16], T.D1[:, 16:32], AO.add)
+        V("PC YY", "VVb", "tt", T.VV[:, 16:64], T.PC[:, 0:48], T.YY[:], AO.add)
+        V("VVa VVb", "VUb", "ts", T.VU[:, 64:128], T.VV[:], 15, None, AO.bitwise_and)
+        V("VVa VVb", "VUa", "ts", T.VU[:, 0:64], T.VV[:], 4, None, AO.arith_shift_right)
+        V("VUb", "LEb", "tc", T.LE[:, 64:128], T.VU[:, 64:128])
+        V("VUa", "LEa", "tc", T.LE[:, 0:64], T.VU[:, 0:64])
+        V("OHW LEb", "OHD", "tc", T.OHD[:], T.OHW[:, 0:16].indirect(T.LE[:, 64:80]))
+        for i in range(3):
+            S("OHC LEb", "OC%d" % i, T.OC[:, 256 * i:256 * i + 256], T.OHC[:, 0:16].indirect(T.LE[:, 80 + 16 * i:96 + 16 * i]), AF.Copy)
+        V("OHD LEa " + PFA, "SEL", "tt", T.SEL[:], T.PF[:, 0:4096].indirect(T.LE[:, 0:16]), T.OHD[:], AO.mult)
+        mms("BO SEL", "AUX", [(T.AUX[:, 0:256], T.BO[:], T.SEL[:], True, True)])
         if t < 2:
-            V(OPA, "ZR", "red", T.ZR[:, 0:1], T.OPN[:, 4:80:5], AxisListType.X, AO.add)
-        V("EQB EQ0 EQ1 EQ2 EQ3 " + OPA, "GB", "tt", T.GB[:], T.EQB[:], T.OPN[:, 0:80], AO.mult)
-        V("GB SI", "QB0", "tt", Q[0], T.GB[:], T.SI[:], AO.mult)
-        V("GB H16", "QB1", "tt", Q[1], T.GB[:], T.H16[:, 1:81], AO.mult)
-        V("GB OD", "QB4", "tt", Q[4], T.GB[:], T.OD[:], AO.mult)
-        V("KEEP5 GB", "PG", "scan", T.PG[:], T.KEEP5[:, 0:80], T.GB[:], 0.0, AO.mult, AO.add)
-        V("KEEP5 QB0 QB1 QB2 QB3 QB4", "QS", "scan", T.QS[:], T.KEEP5[:], T.QB[:], 0.0, AO.mult, AO.add)
-        V("PG " + OPA, "UB", "tt", T.UB[:], T.PG[:], T.OPN[:, 0:80], AO.mult)
-        V("QS", "DF", "tt", T.DF[:], T.QS[:, 163:320:5], T.QS[:, 3:160:5], AO.subtract)
-        V("UB H16", "KU", "tt", T.KU[:], T.UB[:], T.H16[:, 1:81], AO.mult)
-        V("DF QS", "DG1", "tt", T.DG[:, 16:32], T.DF[:, 16:32], T.QS[:, 323:400:5], AO.mult)
-        V("DF QS", "DG0", "tt", T.DG[:, 0:16], T.DF[:, 0:16], T.QS[:, 323:400:5], AO.mult)
-        V("KU", "LC0", "tc", T.LC[:, 0:16], T.KU[:, 0::5])
-        V("DG0 DG1 QS", "RS", "tt", T.RS[:], T.DG[:], T.QS[:, 3:160:5], AO.add)
-        V("KU", "LC1", "tc", T.LC[:, 16:32], T.KU[:, 1::5])
-        V("RS", "LKD", "tc", T.LKD[:], T.RS[:, 16:32])
-        V("RS XL", "LJA", "tt", T.LJA[:], T.RS[:, 0:16], T.XL[:], AO.add)
-        S("OHW LKD", "OHD", T.OHD[:], T.OHW[:, 0:32].indirect(T.LKD[:, 0:16]), AF.Copy)
-        V("KU", "LC2", "tc", T.LC[:, 32:48], T.KU[:, 2::5])
-        V("LJA", "LJD", "tc", T.LJD[:], T.LJA[:])
-        V("KU", "LC3", "tc", T.LC[:, 48:64], T.KU[:, 3::5])
-        S("OHW LC0 LC1 LC2 LC3", "OHM", T.OHM[:], T.OHW[:, 0:32].indirect(T.LC[:, 0:64]), AF.Copy)
-        V("OHD LJD " + NHA, "SEL", "tt", T.SEL[:], T.NHF[:, 0:1024].indirect(T.LJD[:, 0:16]), T.OHD[:], AO.mult)
-        mms("BO SEL", "AUX0", [(T.AUX0[:, 0:256], T.BO[:], T.SEL[:], True, True)])
-        if t < 2:
-            mms("ONE ZR", "AUX1", [(T.AUX1[:, 0:1], T.ONE[:], T.ZR[:, 0:1], True, True)])
-        V("OHC LC0 LC1 LC2 LC3 " + NHA, "NP", "tt", T.NP[:], T.OHC[:, 0:32].indirect(T.LC[:, 0:64]), T.NHF[:], AO.mult)
-        for s in range(4):
-            V("AUX0 OHM", "BB%d" % s, "tt", T.BB[:, 256 * s:256 * s + 256], T.AUX0[:, 0:256], T.OHM[:, 256 * s:256 * s + 256], AO.mult)
+            mms("ONE ZR", "KEY0a", [(T.KEY0[:, 0:1], T.ONE[:], T.ZR[:, 0:1], True, True)])
+        for i in range(3):
+            c = slice(256 * i, 256 * i + 256)
+            S("OC%d" % i, "OM%d" % i, T.OM[:, c], T.OC[:, c], AF.Identity, scale=-1.0, bias=T.ONE[:, 0:1])
+            V("PFT OC%d LEa %s" % (i, PFA), "NP%d" % i, "tt", T.NP[:, c], T.PF[:, 0:4864].indirect(T.LE[:, 16 + 16 * i:32 + 16 * i]), T.OC[:, c], AO.mult)
+        for i in range(3):
+            c = slice(256 * i, 256 * i + 256)
+            V("AUX OM%d" % i, "BB%d" % i, "tt", T.BB[:, c], T.AUX[:, 0:256], T.OM[:, c], AO.mult)
         if t == 0:
-            V("AUX1", "ZA", "tc", T.ZA[:, 0:1], T.AUX1[:, 0:1])
+            V("KEY0a", "ZA", "tc", T.ZA[:, 0:1], T.KEY0[:, 0:1])
         elif t == 1:
-            V("AUX1 ZA", "ZA", "tt", T.ZA[:, 0:1], T.AUX1[:, 0:1], T.ZA[:, 0:1], AO.add)
-        V("NP BB0 BB1 BB2 BB3 SL", PFA, "tt", T.PF[:, 0:5136].indirect(T.SL[:, 0:64]), T.NP[:], T.BB[:], AO.add)
+            V("KEY0a ZA", "ZA", "tt", T.ZA[:, 0:1], T.KEY0[:, 0:1], T.ZA[:, 0:1], AO.add)
+        V("NP0 NP1 NP2 BB0 BB1 BB2 LEa", "PFT " + PFA, "tt", T.PF[:, 0:4864].indirect(T.LE[:, 16:64]), T.NP[:], T.BB[:], AO.add)
+        if t < 2:
+            first_facts(T["FIN%d" % (t + 1)], "FIN%d" % (t + 1))
     for q in range(4):
         c0, c1, k = 512 * q, 512 * q + 512, str(q)
-        S("PFH" + k, "HP" + k, T["HP" + k][:], T.PF[:, 2049 + c0:2049 + c1], AF.Copy, scale=4096.0)
-        V("HP%s PFL%s" % (k, k), "YO" + k, "tt", T.YO[:, c0:c1], T["HP" + k][:], T.PF[:, 1 + c0:1 + c1], AO.add)
-        dma("Y", "YO" + k, "yp", T.yp[:, c0:c1], T.YO[:, c0:c1])
+        S("PFH" + k, "DB" + k, DB[q][:], T.PF[:, 2048 + c0:2048 + c1], AF.Copy, scale=4096.0)
+        V("DB%s PFL%s" % (k, k), "YO" + k, "tt", T.YO[:, c0:c1], DB[q][:], T.PF[:, c0:c1], AO.add)
+        dma("Y", "YO" + k, "yp" + k, T.yp[:, c0:c1], T.YO[:, c0:c1])
     for sem in SEMAPHORES:
         if cnt[sem] and sem != "ls":
             need("G", sem, cnt[sem])

@@ -3,11 +3,22 @@ import comms_topo
 
 AO = AluOpType
 AF = ActivationFunctionType
-SHARE = {None: (88, 128), 0: (64, 128), 1: (96, 128), 7: (72, 96)}
-PHASE = {"C": -0.45, "F": -0.40, "T": -0.25, "A": -0.15, "L0": -0.12, "G0": 0.00, "G1": 0.03, "S": 0.06, "G2": 0.09, "P0": 0.12, "Z0": 0.14,
-         "K": 0.16, "L1": 0.20, "P1": 0.25, "L2": 0.30, "P2": 0.35, "G3": 0.40, "Z1": 0.45, "Z2": 0.50, "L3": 0.52, "P3": 0.54,
-         "U0": 0.80, "Z3": 0.90, "U1": 1.18}
-HITS = [(s, j, odd) for s in (4, 3, 2, 1) for j in range(s) for odd in range(2 if j < s - 1 else 1)]
+SHARE = {None: (88, 128), 0: (32, 80), 1: (80, 128), 7: (68, 96)}
+CUTS = (0, 32, 64, 96, 128)
+PHASE = {"M": -0.92, "H": -0.86, "I": -0.67, "J": -0.50, "E": -0.49, "F": -0.34, "T": -0.26, "G0": -0.20, "A": -0.18, "P0": -0.14, "L0": -0.06,
+         "G1": -0.045, "G2": -0.03, "G3": 0.04, "S": 0.07, "L1": 0.09, "K": 0.165, "P1": 0.23, "P2": 0.51, "L2": 0.56, "Z0": 0.57, "P3": 0.59,
+         "Z1": 0.68, "L3": 0.72, "Z2": 0.77, "U0": 0.84, "Z3": 0.91, "U1": 1.01}
+OTHER = {("L0", 0): -1.0, ("L1", 0): -0.99, ("L2", 0): -0.98, ("L3", 0): -0.97, ("U1", 6): 1.3, ("K", 7): 0.95}
+START = ("WF OHW XQ WB X16 SRB L8 SRG JQ JT0 JT1 JT2 JT3 JT4 JT5 JT6 JT7 E17a E17b MS IDB JM KA KB TW0 TW1 TW2 TW3 HP0 HP1 HP2 HP3 ND PH3 "
+         "K0 PL0 K1a K1b PL1 SU PH0 PH1 PH2 PL2 LC PL3 FF ST IL LW").split()
+END = ("DV LV AS N4 AZ N5 OD C16 M0 N6 H0 PPa I0 C16T J0 N7 N8 N9 Y0 Y1 Y2 Y4 Y5 Y7 PTa F0 "
+       "OL1 OM1 OC1 OM2 OL2 OC2 NP1 "
+       "M1 H1 N0 N1 N2 N3 I1 CO J1 FI CW FJ F1 DC LO FO NP2 CH PPb PTb PD PC D1 YY VVa VVb VUa VUb LE "
+       "OHD0 OM0 OL0 OC0 SEL0 DEC0 OHD1 ZR SEL1 DEC1 LC BB00 BB10 BB20 NP0 BB01 BB11 BB21 ZP PUT ZA").split()
+ON_V = ("PH3",)
+LOADS = ((0, 1), (1, 2), (2, 3), (3, 4))
+OUT = ((384,), (512,), (512,), (384,), (256,))
+HITS = [(s, j) for s in (4, 3, 2, 1) for j in range(s)]
 
 F32, BF, I32, U16 = "float32", "bfloat16", "int32", "uint16"
 SCRATCH = {}
@@ -18,36 +29,41 @@ def _s(name, cols, dtype, where="sbuf"):
 
 
 for _n, _c, _d in [
-        ("R", 4096, BF), ("PF", 4864, F32), ("PK", 2048, I32), ("TI", 2048, I32), ("YO", 2048, F32),
+        ("R", 4096, BF), ("PF", 4864, F32), ("PK", 2048, I32), ("TW", 2048, F32), ("YO", 2048, F32),
         ("JI", 256, I32), ("JQ", [16, 16], F32), ("JT", [16, 128], F32), ("SRI", 256, I32), ("SRB", 256, BF),
         ("MS", 256, F32), ("JM", 256, F32), ("K0", 16, I32), ("K1", 32, I32),
         ("FX0", 256, BF), ("FIN1", 256, BF), ("FIN2", 256, BF), ("FO0", 256, BF), ("FO1", 256, BF), ("FO2", 256, BF),
         ("ST0", 304, F32), ("ST1", 304, F32), ("ST2", 304, F32),
         ("RG", 8192, BF), ("A", [256, 17], BF), ("FH", 1024, BF), ("FT", 256, BF), ("FD", 256, BF),
-        ("NU", 256, U16), ("SC", 1088, I32), ("H5", 80, I32), ("CB", 64, I32), ("FA", 16, I32), ("LC", 16, U16), ("LF", 16, U16),
-        ("DV", 64, I32), ("AS", 48, I32), ("AZ", 48, I32), ("OD", 48, I32), ("HJ", 48, I32), ("HM", 48, I32), ("C16", 64, F32), ("C16T", 64, F32),
-        ("NE", 272, F32), ("CD", 272, F32), ("CO", 272, I32), ("CW", 64, I32),
+        ("NU", 256, U16), ("SC", 1088, I32), ("H5", 80, I32), ("CB", 64, I32), ("FA", 16, I32), ("LC", 64, U16), ("LF", 16, U16), ("LV", 32, U16),
+        ("DV", 64, I32), ("AS", 48, I32), ("AZ", 48, I32), ("OD", 48, I32), ("C16", 64, F32), ("C16T", 64, F32),
+        ("NE", 176, F32), ("CD", 176, F32), ("CO", 176, I32), ("CW", 64, I32), ("FJ", 16, F32),
         ("CH", 64, I32), ("DC", 64, I32), ("PP", 64, F32), ("PT", 64, F32), ("PC", 64, F32), ("PD", 64, F32), ("D1", 32, F32),
-        ("YY", 48, F32), ("VV", 64, I32), ("VU", 128, I32), ("LE", 128, U16), ("FI", 16, I32), ("LO", 16, U16),
-        ("OHD", 256, F32), ("SEL", 256, F32), ("OC", 768, F32), ("OM", 768, F32), ("NP", 768, F32), ("BB", 768, F32),
+        ("YY", 48, F32), ("VV", 64, I32), ("VU", 96, I32), ("LE", 96, U16), ("FI", 16, I32), ("LO", 16, U16),
+        ("OHD", 256, F32), ("SEL", 256, F32), ("OL", 768, F32), ("OM", 768, BF), ("NP", 768, F32), ("BB", 768, F32),
         ("ZR", 1, F32), ("ZA", 1, F32),
         ("IM", 160, F32), ("IG", 128, F32), ("IPI", 2, I32), ("IQI", 6, I32), ("CF", 8, F32), ("XN", 512, BF), ("ND", 512, BF),
-        ("IDB", 128, BF), ("WB", 144, BF), ("WF", 144, F32), ("BO", 128, F32), ("ONE", 128, F32), ("L8", 128, BF), ("MG", 8, F32),
-        ("OHW", 24, F32), ("OHC", 16, F32), ("E17", 17, F32), ("IA", 16, F32), ("XQ", 16, F32), ("X16", 8, F32),
-        ("TRI", 64, F32), ("TR", 64, F32)]:
+        ("IDB", 128, BF), ("IDF", 128, F32), ("NB", 128, BF), ("WB", 144, BF), ("WF", 144, F32), ("BO", 128, F32), ("ONE", 128, F32),
+        ("L8", 128, BF), ("MG", 8, F32), ("OHW", 24, F32), ("E17", 17, F32), ("IA", 16, F32), ("XQ", 16, F32), ("X16", 8, F32), ("BI", 2, F32),
+        ("POW", 64, F32), ("IL", 4, F32), ("LW", 4, U16), ("TRI", 64, F32), ("TR", 64, F32)]:
     _s(_n, _c, _d)
-for _n in ["KEY0", "KEY1", "AUX", "DB0", "DB1", "DB2", "DB3"]:
+_s("DB", 2048, F32, "psum")
+for _n in ["KEY0", "KEY1", "AUX"]:
     _s(_n, 512, F32, "psum")
 _s("FTP", 1024, BF, "psum")
 
-SEMAPHORES = ["sv", "ss", "sp", "sg", "aS1", "aS2", "aF1", "aF2", "ls"] + ["d%d" % i for i in range(14)]
+SEMAPHORES = ["sv", "ss", "sp", "sg", "aS1", "aS2", "aF1", "aF2", "ls"] + ["d%d" % i for i in range(16)]
 
 
-def codes():
-    out = [3 << 16]
-    for s, j, odd in HITS:
+def at(name, n):
+    return n + OTHER.get((name, n), PHASE[name])
+
+
+def codes(odd):
+    out = [(3 << 16) + (11 << 20)]
+    for i, (s, j) in enumerate(HITS):
         d = s if odd else j + 1
-        out.append(sum(8 >> (u - 1) for u in range(j + 1, s + 1) if u != d) + (128 >> (d - 1)) + ((s - 1) << 16))
+        out.append(sum(8 >> (u - 1) for u in range(j + 1, s + 1) if u != d) + (128 >> (d - 1)) + ((s - 1) << 16) + ((10 - i) << 20))
     return out
 
 
@@ -59,7 +75,9 @@ def rank_program(g, core, T, topo):
     ENG = {"V": (g.vector, "sv"), "S": (g.scalar, "ss"), "P": (g.tensor, "sp"), "G": (g, "sg"), "Y": (g.sync, None)}
     cnt = {s: 0 for s in SEMAPHORES}
     waited, Wr, Rd, ndma = {}, {}, {}, [0]
-    DB = [T.DB0, T.DB1, T.DB2, T.DB3]
+
+    def bank(j, n=512):
+        return T.DB[:, 512 * j:512 * j + n]
 
     def need(e, sem, val):
         if waited.get((e, sem), 0) < val:
@@ -109,6 +127,12 @@ def rank_program(g, core, T, topo):
             g.tensor.matmul(*c)
         run("P", reads, writes, "mm", *calls[-1])
 
+    def turns(reads, calls):
+        sync("P", reads.split() + ["IDB"], ["FTP"])
+        for c in calls[:-1]:
+            g.tensor.transpose(*c)
+        run("P", reads + " IDB", "FTP", "tr", *calls[-1])
+
     def dma(e, reads, writes, out, in_):
         reads, writes = reads.split(), writes.split()
         sync(e, reads, writes)
@@ -130,9 +154,9 @@ def rank_program(g, core, T, topo):
 
     dma("Y", "", "JI", T.JI[:], T.jc[:])
     dma("S", "", "SRI", T.SRI[0:8, :], T.sr[:])
-    dma("Y", "", "PK0", T.PK[:, 0:1024], T.pk[:, 0:1024])
-    dma("S", "", "FX0", T.FX0[:], T.fx[:])
-    dma("Y", "", "PK1", T.PK[:, 1024:2048], T.pk[:, 1024:2048])
+    for q0, q1 in LOADS:
+        dma("Y", "", " ".join("PK%d" % q for q in range(q0, q1)), T.PK[:, 512 * q0:512 * q1], T.pk[:, 512 * q0:512 * q1])
+    dma("Y", "", "FX0", T.FX0[:], T.fx[:])
     dma("Y", "", "R", T.R[:], T.rt[:])
 
     def iota(key, out, pat, base, cm=0):
@@ -143,108 +167,114 @@ def rank_program(g, core, T, topo):
     iota("IA", T.IA[:], [[16, 16]], 0)
     iota("XN", T.XN[:], [[1, 32], [0, 16]], 0)
     iota("A17", T.A[:, :, 16], [[0, 256]], 255)
+    CUT, BIG = 4096.0 * 2047 + 2047.5, 1.5 * 2.0 ** 35
+    V("", "BI0", "memset", T.BI[:, 0:1], 2047 - BIG / 4096)
+    V("", "BI1", "memset", T.BI[:, 1:2], 4096.0 * 2047 - BIG)
     V("IPI", "IQ0", "ts", T.IQI[:, 0:2], T.IPI[:], 15, None, AO.bitwise_and)
     V("IPI", "IQ1", "ts", T.IQI[:, 2:4], T.IPI[:], 4, None, AO.arith_shift_right)
     V("IPI", "IQ2", "ts", T.IQI[:, 4:6], T.IPI[:], 31, None, AO.bitwise_and)
+    V("IQ0", "CF5", "ts", T.CF[:, 5:6], T.IQI[:, 0:1], 4096.0, None, AO.mult)
     V("IPI", "CF0", "tc", T.CF[:, 0:1], T.IPI[:, 0:1])
     V("IQ0 IQ1 IQ2", "CF1", "tc", T.CF[:, 1:4], T.IQI[:, 0:6:2])
     V("IQ1", "CF4", "ts", T.CF[:, 4:5], T.IQI[:, 2:3], 16.0, 15.0, AO.mult, AO.add)
-    V("IQ0", "CF5", "ts", T.CF[:, 5:6], T.IQI[:, 0:1], 4096.0, None, AO.mult)
     p_c, q_c, g_c, r_c, e_c, k_c = [T.CF[:, i:i + 1] for i in range(6)]
     V("IM CF1", "MG", "ts", T.MG[:], T.IM[:, 0:8], g_c, None, AO.is_equal)
-    V("IG CF0", "L8", "ts", T.L8[0:8, :], T.IG[0:8, :], T.CF[0:8, 0:1], None, AO.is_equal)
-    V("IM CF1", "OHW", "ts", T.OHW[:], T.IM[:, 0:24], q_c, None, AO.is_equal)
-    V("IM CF4", "WF", "ts", T.WF[:, 0:143], T.IM[:, 0:143], e_c, None, AO.is_equal)
-    V("OHW", "E17a", "tt", T.E17[:, 1:17], T.OHW[:, 0:16], T.OHW[:, 1:17], AO.subtract)
-    V("OHW", "E17b", "ts", T.E17[:, 0:1], T.OHW[:, 15:16], 1024.0, None, AO.mult)
-    V("IM CF4", "WB", "ts", T.WB[:, 0:143], T.IM[:, 0:143], e_c, 65536.0, AO.is_equal, AO.mult)
-    V("IM CF0", "IDB", "ts", T.IDB[:], T.IM[:, 0:128], p_c, None, AO.is_equal)
-    V("IA CF1", "XQ", "ts", T.XQ[:], T.IA[:], q_c, None, AO.add)
-    V("XN CF1", "ND", "ts", T.ND[:], T.XN[:], r_c, -1.0, AO.is_equal, AO.mult)
-    V("XQ", "X16", "ts", T.X16[:], T.XQ[:, 0:8], 16.0, None, AO.mult)
+
+    EVEN, ODD = codes(0), codes(1)
 
     def late_constants():
         iota("PFT", T.PF[:, 4096:4864], [[0, 768]], 0)
         iota("TRIa", T.TRI[:, 0:48], [[16, 48]], 4096)
         iota("TRIb", T.TRI[:, 48:64], [[16, 16]], 4096)
         iota("ONE", T.ONE[:], [[0, 128]], 1)
-        iota("NE", T.NE[:, 0::17], [[0, 16]], 0)
-        c = codes()
-        for i in range(16):
-            iota("CD%d" % i, T.CD[:, i::17], [[0, 16]], c[i] - c[i + 1])
+        iota("NE", T.NE[:, 0::11], [[0, 16]], 0)
+        for u in range(4):
+            iota("POW", T.POW[:, 16 * u:16 * u + 16], [[0, 16]], 2 ** u)
+        for i in range(11):
+            if EVEN[i] == ODD[i]:
+                iota("CD%d" % i, T.CD[:, i::11], [[0, 16]], EVEN[i])
 
     def late_constants_v():
-        return [lambda: V("IG CF1", "BO", "ts", T.BO[:], T.IG[:], g_c, None, AO.is_equal),
-                lambda: V("IM CF1", "OHC", "ts", T.OHC[:], T.IM[:, 0:16], q_c, None, AO.not_equal),
-                lambda: V("TRIa TRIb CF1", "TR", "ts", T.TR[:], T.TRI[:], q_c, 16.0, AO.add, AO.mult),
-                lambda: V("XQ", "CD16", "ts", T.CD[:, 16::17], T.XQ[:], 256.0, float(codes()[16]), AO.mult, AO.add),
-                lambda: V("TR", "YY", "tc", T.YY[:], T.TR[:, 0:48])]
-    CDA = " ".join("CD%d" % i for i in range(17))
-
-    def unpack_hi(q):
-        c0, c1, k = 512 * q, 512 * q + 512, str(q)
-        V("PK%d" % (q // 2), "TI" + k, "ts", T.TI[:, c0:c1], T.PK[:, c0:c1], 12, None, AO.arith_shift_right)
-        V("TI" + k, "PFH" + k, "tc", T.PF[:, 2048 + c0:2048 + c1], T.TI[:, c0:c1])
-        S("PFH" + k, "DB" + k, DB[q][:], T.PF[:, 2048 + c0:2048 + c1], AF.Copy, scale=4096.0)
-
-    def unpack_lo(q):
-        c0, c1, k = 512 * q, 512 * q + 512, str(q)
-        V("PK%d DB%s" % (q // 2, k), "PFL" + k, "tt", T.PF[:, c0:c1], T.PK[:, c0:c1], DB[q][:], AO.subtract)
+        return [lambda: V("TRIa TRIb CF1", "TR", "ts", T.TR[:], T.TRI[:], q_c, 16.0, AO.add, AO.mult),
+                lambda: V("TR", "YY", "tc", T.YY[:], T.TR[:, 0:48]),
+                lambda: V("IM CF0", "IDF", "ts", T.IDF[:], T.IM[:, 0:128], p_c, None, AO.is_equal),
+                lambda: V("IDB", "NB", "ts", T.NB[:], T.IDB[:], -4096.0, None, AO.mult),
+                lambda: V("IG CF1", "BO", "ts", T.BO[:], T.IG[:], g_c, None, AO.is_equal)]
+    CDA = " ".join("CD%d" % i for i in range(11))
     PFA = " ".join("PFH%d PFL%d" % (q, q) for q in range(4))
 
-    V("JI CF5", "JQ", "ts", T.JQ[:, :, :], T.JI[:], k_c, None, AO.add)
+    def first_courts(t):
+        V("SU%d" % t, "LC01 LC11", "tc", T.LC[:, 0:16], T["ST%d" % t][:, 272:288])
+
+    def first_facts(fin, fk):
+        turns(fk, [(T.FTP[:, 128 * X:128 * X + 128], fin[:, 128 * X:128 * X + 128], T.IDB[:]) for X in range(2)])
+        S("FTP", "FT0 FT1", T.FT[:], T.FTP[:, 0:256], AF.Copy)
+        mms("WB " + fk, "AUX", [(T.AUX[:, 0:16], T.WB[:, 15 - b:143 - b], fin[:, b::16], b == 0, b == 15) for b in range(16)])
+
+    def unpack(q):
+        c, h, k = slice(512 * q, 512 * q + 512), slice(2048 + 512 * q, 2560 + 512 * q), str(q)
+        return {"TW" + k: lambda: V("PK" + k, "TW" + k, "ts", T.TW[:, c], T.PK[:, c], CUT, BIG, AO.subtract, AO.add),
+                "HP" + k: lambda: S("TW%s BI1" % k, "DB" + k, bank(q), T.TW[:, c], AF.Identity, bias=T.BI[:, 1:2]),
+                "PH" + k: (lambda: V("TW" + k, "PFH" + k, "ts", T.PF[:, h], T.TW[:, c], 2.0 ** -12, 2047 - BIG / 4096, AO.mult, AO.add))
+                if "PH" + k in ON_V else
+                (lambda: S("TW%s BI0" % k, "PFH" + k, T.PF[:, h], T.TW[:, c], AF.Identity, scale=2.0 ** -12, bias=T.BI[:, 0:1])),
+                "PL" + k: lambda: V("PK%s DB%s" % (k, k), "PFL" + k, "tt", T.PF[:, c], T.PK[:, c], bank(q), AO.subtract)}
+
+    def block(h):
+        if "JT%d" % h in ON_V:
+            return lambda: V("JQ MG", "JT%d" % h, "ts", T.JT[:, :, 16 * h:16 * h + 16], T.JQ[:, :, :], T.MG[:, h:h + 1], None, AO.mult)
+        return lambda: S("JQ MG", "JT%d" % h, T.JT[:, :, 16 * h:16 * h + 16], T.JQ[:, :, :], AF.Identity, scale=T.MG[:, h:h + 1])
+
+    start = {
+        "WF": lambda: V("IM CF4", "WF", "ts", T.WF[:, 0:143], T.IM[:, 0:143], e_c, None, AO.is_equal),
+        "E17a": lambda: V("OHW", "E17a", "tt", T.E17[:, 1:17], T.OHW[:, 0:16], T.OHW[:, 1:17], AO.subtract),
+        "E17b": lambda: V("OHW", "E17b", "ts", T.E17[:, 0:1], T.OHW[:, 15:16], 1024.0, None, AO.mult),
+        "OHW": lambda: V("IM CF1", "OHW", "ts", T.OHW[:], T.IM[:, 0:24], q_c, None, AO.is_equal),
+        "L8": lambda: V("IG CF0", "L8", "ts", T.L8[0:8, :], T.IG[0:8, :], T.CF[0:8, 0:1], None, AO.is_equal),
+        "WB": lambda: S("WF", "WB", T.WB[:, 0:143], T.WF[:, 0:143], AF.Copy, scale=65536.0),
+        "IDB": lambda: V("IM CF0", "IDB", "ts", T.IDB[:], T.IM[:, 0:128], p_c, None, AO.is_equal),
+        "XQ": lambda: S("IA CF1", "XQ", T.XQ[:], T.IA[:], AF.Identity, bias=q_c),
+        "ND": lambda: V("XN CF1", "ND", "ts", T.ND[:], T.XN[:], r_c, -1.0, AO.is_equal, AO.mult),
+        "X16": lambda: S("XQ", "X16", T.X16[:], T.XQ[:, 0:8], AF.Copy, scale=16.0),
+        "IL": lambda: V("IM CF1", "IL", "ts", T.IL[:], T.IM[:, 0:4], 0.0, q_c, AO.mult, AO.add),
+        "LW": lambda: V("IL", "LW", "ts", T.LW[:], T.IL[:], 11.0, 10.0, AO.mult, AO.add),
+        "JQ": lambda: V("JI CF5", "JQ", "ts", T.JQ[:, :, :], T.JI[:], k_c, None, AO.add),
+        "SRB": lambda: V("SRI", "SRB", "tc", T.SRB[0:8, :], T.SRI[0:8, :]),
+        "SRG": lambda: mms("L8 SRB", "AUX", [(T.AUX[:, 0:256], T.L8[0:8, :], T.SRB[0:8, :], True, True)]),
+        "MS": lambda: V("AUX CF1", "MS", "ts", T.MS[:], T.AUX[:, 0:256], q_c, None, AO.is_equal),
+        "JM": lambda: V("MS JQ", "JM", "tt", T.JM[:], T.MS[:], T.JQ[:, :, :], AO.mult),
+        "KA": lambda: mms("WF JM", "KEY0a KEY0b",
+                          [(T.KEY0[:, 0:16], T.WF[:, 15 - b:143 - b], T.JM[:, b::16], b == 0, b == 15) for b in range(16)]),
+        "KB": lambda: mms("JT0 JT1 JT2 JT3 JT4 JT5 JT6 JT7 E17a E17b", "KEY1a KEY1b",
+                          [(T.KEY1[:, 17 * a:17 * a + 17], T.JT[:, a, :], T.E17[:], True, True) for a in range(16)]),
+        "K0": lambda: V("KEY0a KEY0b", "K0", "tc", T.K0[:], T.KEY0[:, 0:16]),
+        "K1a": lambda: V("K0", "K1a", "ts", T.K1[:, 0:16], T.K0[:], 4095, None, AO.bitwise_and),
+        "K1b": lambda: V("K0", "K1b", "ts", T.K1[:, 16:32], T.K0[:], 12, None, AO.arith_shift_right),
+        "SU": lambda: V("K1a K1b", "SU0", "tc", T.ST0[:, 272:304], T.K1[:]),
+        "ST": (lambda: V("KEY1a KEY1b", "ST0", "tc", T.ST0[:, 0:272], T.KEY1[:, 0:272])) if "ST" in ON_V else
+              (lambda: S("KEY1a KEY1b", "ST0", T.ST0[:, 0:272], T.KEY1[:, 0:272], AF.Copy)),
+        "LC": lambda: first_courts(0),
+        "FF": lambda: first_facts(T.FX0, "FX0")}
+    for q in range(4):
+        start.update(unpack(q))
     for h in range(8):
-        S("JQ MG", "JT%d" % h, T.JT[:, :, 16 * h:16 * h + 16], T.JQ[:, :, :], AF.Identity, scale=T.MG[:, h:h + 1])
-    V("SRI", "SRB", "tc", T.SRB[0:8, :], T.SRI[0:8, :])
-    mms("L8 SRB", "AUX", [(T.AUX[:, 0:256], T.L8[0:8, :], T.SRB[0:8, :], True, True)])
-    V("AUX CF1", "MS", "ts", T.MS[:], T.AUX[:, 0:256], q_c, None, AO.is_equal)
-    V("MS JQ", "JM", "tt", T.JM[:], T.MS[:], T.JQ[:, :, :], AO.mult)
-    mms("WF JM", "KEY0a KEY0b", [(T.KEY0[:, 0:16], T.WF[:, 15 - b:143 - b], T.JM[:, b::16], b == 0, b == 15) for b in range(16)])
-    mms("JT0 JT1 JT2 JT3 JT4 JT5 JT6 JT7 E17a E17b", "KEY1a KEY1b",
-        [(T.KEY1[:, 17 * a:17 * a + 17], T.JT[:, a, :], T.E17[:], True, True) for a in range(16)])
-    unpack_hi(0)
-    unpack_hi(1)
-    S("KEY1a KEY1b", "ST0", T.ST0[:, 0:272], T.KEY1[:, 0:272], AF.Copy)
-    V("KEY0a KEY0b", "K0", "tc", T.K0[:], T.KEY0[:, 0:16])
-    unpack_lo(0)
-    V("K0", "K1a", "ts", T.K1[:, 0:16], T.K0[:], 4095, None, AO.bitwise_and)
-    V("K0", "K1b", "ts", T.K1[:, 16:32], T.K0[:], 12, None, AO.arith_shift_right)
-    unpack_lo(1)
-    V("K1a K1b", "SU0", "tc", T.ST0[:, 272:304], T.K1[:])
+        start["JT%d" % h] = block(h)
+    for name in START:
+        start[name]()
     send((rank + 1) % nrank, T.ST0[:], T.ST1[:], "aS1", "ST0 SU0")
     send((rank + 2) % nrank, T.ST0[:], T.ST2[:], "aS2", "ST0 SU0")
     late_constants()
     Wr["ST1"], Wr["ST2"], Wr["SU1"], Wr["SU2"] = {"aS1": narr}, {"aS2": narr}, {"aS1": narr}, {"aS2": narr}
     Wr["FIN1"], Wr["FIN2"] = {"aF1": narr}, {"aF2": narr}
 
-    def first_courts(t):
-        V("SU%d" % t, "LC0 LC1", "tc", T.LC[:], T["ST%d" % t][:, 272:288])
-
-    def turn(X, src, key):
-        run("P", "IDB " + key, "FTP", "tr", T.FTP[:, 0:128], src[:, 128 * X:128 * X + 128], T.IDB[:])
-
-    def turned(X):
-        S("FTP", "FT%d" % X, T.FT[:, 128 * X:128 * X + 128], T.FTP[:, 0:128], AF.Abs)
-
-    def first_facts(fin, fk):
-        for X in range(2):
-            turn(X, fin, fk)
-            turned(X)
-        mms("WB " + fk, "AUX", [(T.AUX[:, 0:16], T.WB[:, 15 - b:143 - b], fin[:, b::16], b == 0, b == 15) for b in range(16)])
-
-    first_facts(T.FX0, "FX0")
-    unpack_hi(2)
-    unpack_hi(3)
-    unpack_lo(2)
-    first_courts(0)
-    unpack_lo(3)
     for t in range(3):
         st, stk, suk = T["ST%d" % t], "ST%d" % t, "SU%d" % t
         fin, fk = (T.FX0, "FX0") if t == 0 else (T["FIN%d" % t], "FIN%d" % t)
         fo, fok = T["FO%d" % t], "FO%d" % t
 
-        def pf(X):
-            V("%s LC%d" % (PFA, X), "NU%d" % X, "tc", T.NU[:, 128 * X:128 * X + 128], T.PF[:, 0:4096].indirect(T.LC[:, 8 * X:8 * X + 8]))
+        def entries(X, s):
+            l0 = 16 * s - 16 + 8 * X
+            V("%s LC%d%d" % (PFA, X, s), "NU%d" % X, "tc", T.NU[:, 128 * X:128 * X + 128], T.PF[:, 0:4096].indirect(T.LC[:, l0:l0 + 8]))
 
         def rules(e, n, x0, x1):
             if x0 >= x1:
@@ -257,50 +287,48 @@ def rank_program(g, core, T, topo):
             else:
                 S("R NU%d" % X, wr, out, src, AF.Copy)
 
-        def less(X, j):
-            sync("P", ["FT%d" % X, "ND"], ["DB%d" % j])
-            g.tensor.matmul(DB[j][:], T.FT[32 * j:32 * j + 32, 128 * X:128 * X + 128], T.ND[32 * j:32 * j + 32, :], True, False)
+        def less(n, j):
+            first, X = at("L%d" % j, n) < at("P%d" % j, n), n % 2
+            run("P", "FT%d ND" % X, "DB%d" % j if first else "DC%d" % j, "mm",
+                bank(j), T.FT[32 * j:32 * j + 32, 128 * X:128 * X + 128], T.ND[32 * j:32 * j + 32, :], first, not first)
 
-        def plus(w, j):
-            run("P", "FT%d ND IDB RG%d%dV RG%d%dS" % (w % 2, w, j, w, j), "DB%d" % j, "mm",
-                DB[j][:], T.IDB[:], T.RG[:, 2048 * w + 512 * j:2048 * w + 512 * j + 512], False, True)
+        def plus(n, j):
+            first, w = at("P%d" % j, n) < at("L%d" % j, n), n % 4
+            run("P", "IDB RG%d%dV RG%d%dS" % (w, j, w, j), "DB%d" % j if first else "DC%d" % j, "mm",
+                bank(j), T.IDB[:], T.RG[:, 2048 * w + 512 * j:2048 * w + 512 * j + 512], first, not first)
 
         def size(X, j):
-            S("DB%d" % j, "A%d%d" % (X, j), T.A[:, 128 * X + 32 * j:128 * X + 32 * j + 32, 0:16], DB[j][:], AF.Abs)
+            S("DB%d DC%d" % (j, j), "A%d%d" % (X, j), T.A[:, 128 * X + 32 * j:128 * X + 32 * j + 32, 0:16], bank(j), AF.Abs)
 
         def sums(X, h):
             x0 = 128 * X + 64 * h
             mms("WB A17 A%d%d A%d%d" % (X, 2 * h, X, 2 * h + 1), "KEY%d%s" % (X, "ab"[h]),
                 [(T["KEY%d" % X][:, 68 * h:68 * h + 68], T.WB[:, 15 - b:143 - b], T.A[:, x0 + b:x0 + 64:16, :], b == 0, b == 15) for b in range(16)])
 
-        def choose(X, s, fill=(), mid=(), tail=()):
-            k, c0, fill = "%d%d" % (X, s), 272 * (s - 1) + 136 * X, list(fill)
-            key, a, sa = T.SC[:, c0 + 16:c0 + 136:17], slice(8 * X, 8 * X + 8), slice(16 * s + 8 * X, 16 * s + 8 * X + 8)
-            V("%s KEY%da KEY%db" % (stk, X, X), "SC" + k, "scan", T.SC[:, c0:c0 + 136], st[:, 136 * X:136 * X + 136],
+        def least(X, s):
+            c0 = 272 * (s - 1) + 136 * X
+            V("%s KEY%da KEY%db" % (stk, X, X), "SC%d%d" % (X, s), "scan", T.SC[:, c0:c0 + 136], st[:, 136 * X:136 * X + 136],
               T["KEY%d" % X][:, 0:136], 0.0, AO.add, AO.min)
-            if fill:
-                fill.pop(0)()
-            V("SC" + k, "H" + k, "ts", T.H5[:, sa], key, 12, 15, AO.arith_shift_right, AO.bitwise_and)
-            if s < 4:
-                V("SC" + k, "C%d%d" % (X, s + 1), "ts", T.CB[:, sa], key, 4095, None, AO.bitwise_and)
-            if fill:
-                fill.pop(0)()
-            V("X16 H" + k, "FA%d" % X, "tt", T.FA[:, a], T.H5[:, sa], T.X16[:], AO.add)
-            if s < 4:
-                V("C%d%d" % (X, s + 1), "LC%d" % X, "tc", T.LC[:, a], T.CB[:, sa])
-            for f in fill + list(mid):
-                f()
-            V("FA%d" % X, "LF%d" % X, "tc", T.LF[:, a], T.FA[:, a])
-            if s < 4:
-                pf(X)
-            for f in tail:
-                f()
 
-        def facts(X, s):
-            f0 = 256 * (s - 1) + 128 * X
+        def row(X, s):
+            k, c0, a0 = "%d%d" % (X, s), 272 * (s - 1) + 136 * X, 16 * s + 8 * X
+            V("SC" + k, "H" + k, "ts", T.H5[:, a0:a0 + 8], T.SC[:, c0 + 16:c0 + 136:17], 12, 15, AO.arith_shift_right, AO.bitwise_and)
+            if s < 4:
+                V("SC" + k, "C%d%d" % (X, s + 1), "ts", T.CB[:, a0:a0 + 8], T.SC[:, c0 + 16:c0 + 136:17], 4095, None, AO.bitwise_and)
+
+        def place(X, s):
+            a0 = 16 * s + 8 * X
+            V("X16 H%d%d" % (X, s), "FA%d" % X, "tt", T.FA[:, 8 * X:8 * X + 8], T.H5[:, a0:a0 + 8], T.X16[:], AO.add)
+            if s < 4:
+                V("C%d%d" % (X, s + 1), "LC%d%d" % (X, s + 1), "tc", T.LC[:, a0:a0 + 8], T.CB[:, a0:a0 + 8])
+
+        def places(X, s):
+            V("FA%d" % X, "LF%d" % X, "tc", T.LF[:, 8 * X:8 * X + 8], T.FA[:, 8 * X:8 * X + 8])
+
+        def chosen(X, s):
+            f0, w = 256 * (s - 1) + 128 * X, (2 * s - 2 + X) % 4
             old, ok = (fin[:, 128 * X:128 * X + 128], fk) if s == 1 else (T.FH[:, f0 - 256:f0 - 128], "FH%d%d" % (X, s - 1))
             out, key = (T.FD[:, 128 * X:128 * X + 128], "FD%d" % X) if s < 4 else (T.FH[:, f0:f0 + 128], "FH%d4" % X)
-            w = (2 * s - 2 + X) % 4
             V("LF%d %s " % (X, ok) + " ".join("RG%d%d%s" % (w, j, e) for j in range(4) for e in "VS"), key, "tt", out,
               T.RG[:, 2048 * w:2048 * w + 2048].indirect(T.LF[:, 8 * X:8 * X + 8]), old, AO.subtract)
 
@@ -308,115 +336,165 @@ def rank_program(g, core, T, topo):
             f0 = 256 * (s - 1) + 128 * X
             S("FD%d" % X, "FH%d%d" % (X, s), T.FH[:, f0:f0 + 128], T.FD[:, 128 * X:128 * X + 128], AF.Abs)
 
+        def turn(X, s):
+            f0 = 256 * (s - 1) + 128 * X
+            if "A" in ON_V:
+                turns("FH%d%d" % (X, s), [(T.FTP[:, 0:128], T.FH[:, f0:f0 + 128], T.IDB[:])])
+            else:
+                turns("FD%d" % X, [(T.FTP[:, 0:128], T.FD[:, 128 * X:128 * X + 128], T.IDB[:])])
+
+        def turned(X, s):
+            if "A" in ON_V:
+                V("FTP", "FT%d" % X, "tc", T.FT[:, 128 * X:128 * X + 128], T.FTP[:, 0:128])
+            else:
+                S("FTP", "FT%d" % X, T.FT[:, 128 * X:128 * X + 128], T.FTP[:, 0:128], AF.Abs)
+
         def both(k, s):
             return "%s0%d %s1%d" % (k, s, k, s)
-
-        def miss(i):
-            s, j, odd = HITS[i]
-            row, key = (T.H5, both("H", j)) if j == s - 1 else (T.HM, "HM") if odd else (T.HJ, "HJ")
-            return lambda: V("NE %s %s" % (both("H", s), key), "NE%d" % i, "tt", T.NE[:, i + 1::17],
-                             row[:, 16 * j:16 * j + 16], T.H5[:, 16 * s:16 * s + 16], AO.not_equal)
-        HA = " ".join(both("H", s) for s in range(3))
-        CA = " ".join(both("C", s) for s in range(1, 5))
-        loops = [i for i, (s, j, odd) in enumerate(HITS) if j == s - 1 and s < 4]
-        early = [lambda: V(" ".join(both("SC", s) for s in (1, 2, 3)), "DV1", "ts", T.DV[:, 16:64], T.SC[:, 16:816:17], 16, None, AO.arith_shift_right),
-                 lambda: V("DV0 DV1", "AS", "tt", T.AS[:], T.DV[:, 0:48], T.DV[:, 16:64], AO.add),
-                 lambda: V("AS ZA", "AZ", "ts", T.AZ[:], T.AS[:], T.ZA[:, 0:1] if t else 0.0, 16.0, AO.add, AO.mult),
-                 lambda: V("AZ", "OD", "ts", T.OD[:], T.AZ[:], 16, None, AO.bitwise_and),
-                 lambda: V(CA, "C16", "ts", T.C16[:], T.CB[:], 16.0, None, AO.mult), miss(loops[0]),
-                 lambda: V("OD " + HA, "HJ", "tt", T.HJ[:], T.H5[:, 0:48], T.OD[:], AO.add),
-                 lambda: V("C16 TR", "C16T", "tt", T.C16T[:], T.C16[:], T.TR[:], AO.subtract),
-                 lambda: V("HJ", "HM", "ts", T.HM[:], T.HJ[:], 16.0, None, AO.subtract), miss(loops[1]), miss(loops[2])]
-        early += [miss(i) for i in range(7, 16) if i not in loops]
-        late = [miss(i) for i in range(7)]
         lc = late_constants_v() if t == 0 else []
-        fills = {(0, 1): [lambda: V(suk, both("H", 0), "tc", T.H5[:, 0:16], st[:, 288:304])],
-                 (1, 1): [lambda: V(suk, both("C", 1), "tc", T.CB[:, 0:16], st[:, 272:288])],
-                 (0, 2): [lambda: V("AUX", "DV0", "ts", T.DV[:, 0:16], T.AUX[:, 0:16], 2.0 ** -16, None, AO.mult)],
-                 (1, 2): lc[0:1], (0, 3): lc[1:3], (1, 3): lc[3:]}
+        fills = {2: [lambda: V("AUX", "DV0", "ts", T.DV[:, 0:16], T.AUX[:, 0:16], 2.0 ** -16, None, AO.mult)],
+                 3: [lambda: V(suk, both("C", 1), "tc", T.CB[:, 0:16], st[:, 272:288])],
+                 4: [lambda: V(suk, both("H", 0), "tc", T.H5[:, 0:16], st[:, 288:304])],
+                 5: lc[0:1], 6: lc[1:3], 7: lc[3:5]}
+
+        last = {"M": least, "H": row, "I": place, "J": places, "F": chosen, "K": kept, "T": turn, "A": turned}
 
         def call(name, n):
             X, s, j = n % 2, n // 2 + 1, int(name[1:] or 0)
             s0, s1 = SHARE.get(n, SHARE[None])
-            if name == "C":
-                if n < 2:
-                    pf(X)
-                else:
-                    choose(X, s - 1, fills[(X, s - 1)])
-            elif name in "FKTA":
+            if name == "E":
+                entries(X, s)
+            elif name in last:
                 if n >= 2:
-                    {"F": lambda: facts(X, s - 1), "K": lambda: kept(X, s - 1), "T": lambda: turn(X, T.FD, "FD%d" % X), "A": lambda: turned(X)}[name]()
+                    last[name](X, s - 1)
+                    for f in fills[n] if name == "M" else []:
+                        f()
             elif name == "S":
                 rules("S", n, s0, s1)
             elif name[0] == "G":
-                rules("V", n, 32 * j, min(s0, 32 * j + 32))
-                rules("V", n, max(s1, 32 * j), 32 * j + 32)
-            elif name[0] == "P":
-                plus(n % 4, j)
+                rules("V", n, CUTS[j], min(s0, CUTS[j + 1]))
+                rules("V", n, max(s1, CUTS[j]), CUTS[j + 1])
+            elif name[0] in "LP":
+                {"L": less, "P": plus}[name[0]](n, j)
             else:
-                {"L": less, "Z": size, "U": sums}[name[0]](X, j)
-        for _, name, n in sorted((n + ph, name, n) for n in range(8) for name, ph in PHASE.items()):
+                {"Z": size, "U": sums}[name[0]](X, j)
+        for _, name, n in sorted((at(name, n), name, n) for n in range(8) for name in PHASE):
             call(name, n)
-        choose(0, 4, early[:3])
-        facts(0, 4)
-        for f in early[3:]:
-            f()
-        choose(1, 4, [], late[:2], late[2:])
-        H4 = " ".join(both("H", s) for s in range(1, 5))
-        V("C16 " + H4, "PP", "tt", T.PP[:], T.H5[:, 16:80], T.C16[:], AO.add)
-        V("NE %s %s" % (" ".join("NE%d" % i for i in range(16)), CDA), "CO", "scan", T.CO[:], T.NE[:], T.CD[:], 0.0, AO.mult, AO.add)
-        facts(1, 4)
-        V("CO", "FI", "ts", T.FI[:], T.CO[:, 16::17], 8, None, AO.arith_shift_right)
-        for u in range(4):
-            V("CO", "CW%d" % u, "ts", T.CW[:, 16 * u:16 * u + 16], T.CO[:, 16::17], 2.0 ** u, None, AO.mult)
-        V("FI", "LO", "tc", T.LO[:], T.FI[:])
-        V("C16T " + H4, "PT", "tt", T.PT[:], T.H5[:, 16:80], T.C16T[:], AO.add)
-        V("CW0 CW1 CW2 CW3", "DC", "ts", T.DC[:], T.CW[:], 7, 1, AO.arith_shift_right, AO.bitwise_and)
-        V("CW0 CW1 CW2 CW3", "CH", "ts", T.CH[:], T.CW[:], 3, 1, AO.arith_shift_right, AO.bitwise_and)
-        S("LO " + " ".join(both("FH", s) for s in range(1, 5)), fok, fo[:], T.FH[:, 0:1024].indirect(T.LO[:]), AF.Abs)
-        if t < 2:
-            send((rank + 1) % nrank, fo[:], T["FIN%d" % (t + 1)][:], "aF%d" % (t + 1), fok)
-            first_courts(t + 1)
-        else:
-            dma("Y", fok, "yf", T.yf[:], fo[:])
-        V("DC PP", "PD", "tt", T.PD[:], T.DC[:], T.PP[:], AO.mult)
-        V("CH PT", "PC", "tt", T.PC[:], T.CH[:], T.PT[:], AO.mult)
-        V("PD", "D1", "tt", T.D1[:], T.PD[:, 0:32], T.PD[:, 32:64], AO.add)
-        V("PC TR YY", "YY", "tt", T.YY[:, 0:16], T.PC[:, 48:64], T.TR[:, 0:16], AO.add)
-        if t < 2:
-            V("DC", "ZR", "red", T.ZR[:, 0:1], T.DC[:], AxisListType.X, AO.add)
-        V("D1", "VVa", "tt", T.VV[:, 0:16], T.D1[:, 0:16], T.D1[:, 16:32], AO.add)
-        V("PC YY", "VVb", "tt", T.VV[:, 16:64], T.PC[:, 0:48], T.YY[:], AO.add)
-        V("VVa VVb", "VUb", "ts", T.VU[:, 64:128], T.VV[:], 15, None, AO.bitwise_and)
-        V("VVa VVb", "VUa", "ts", T.VU[:, 0:64], T.VV[:], 4, None, AO.arith_shift_right)
-        V("VUb", "LEb", "tc", T.LE[:, 64:128], T.VU[:, 64:128])
-        V("VUa", "LEa", "tc", T.LE[:, 0:64], T.VU[:, 0:64])
-        V("OHW LEb", "OHD", "tc", T.OHD[:], T.OHW[:, 0:16].indirect(T.LE[:, 64:80]))
+
+        def miss(i):
+            s, j = HITS[i]
+            return lambda: V("NE %s %s" % (both("H", s), both("H", j)), "NE%d" % i, "tt", T.NE[:, i + 1::11],
+                             T.H5[:, 16 * j:16 * j + 16], T.H5[:, 16 * s:16 * s + 16], AO.not_equal)
+
+        def meaning(i):
+            j = HITS[i][1]
+            return lambda: V("OD", "CD%d" % (i + 1), "ts", T.CD[:, i + 1::11], T.OD[:, 16 * j:16 * j + 16],
+                             float(ODD[i + 1] - EVEN[i + 1]), float(EVEN[i + 1]), AO.mult, AO.add)
+
+        def slot(i):
+            c, k, b = slice(256 * i, 256 * i + 256), str(i), "DB%d DC%d" % (i, i)
+            vl, vk = (T.LE[:, 80:96], "LE") if i == 0 else (T.LV[:, 16 * i - 16:16 * i], "LV")
+            cl, ck = (T.LE[:, 16:32], "LE PFT") if i == 0 else (T.LC[:, 16 * i:16 * i + 16], both("LC", i + 1))
+            out = {"OM" + k: (lambda: V("OHW " + vk, "OM" + k, "tc", T.OM[:, c], T.OHW[:, 0:16].indirect(vl))) if "OM" + k in ON_V else
+                             (lambda: S("OHW " + vk, "OM" + k, T.OM[:, c], T.OHW[:, 0:16].indirect(vl), AF.Copy)),
+                   "OL" + k: lambda: S("%s %s" % (ck, PFA), "OL" + k, T.OL[:, c], T.PF[:, 0:4864 if i == 0 else 4096].indirect(cl), AF.Copy)}
+            if i == 0:
+                out["OC0"] = lambda: S("OM0 ONE", b, bank(0, 256), T.OM[:, c], AF.Identity, scale=-1.0, bias=T.ONE[:, 0:1])
+                out["NP0"] = lambda: V("OL0 " + b, "NP0", "tt", T.NP[:, c], T.OL[:, c], bank(0, 256), AO.mult)
+            else:
+                out["OC" + k] = lambda: mms("IDF NB OL%s OM%s" % (k, k), b, [(bank(i, 256), T.NB[:], T.OM[:, c], True, False),
+                                                                             (bank(i, 256), T.IDF[:], T.OL[:, c], False, True)])
+                out["NP" + k] = lambda: S(b, "NP" + k, T.NP[:, c], bank(i, 256), AF.Relu)
+            return out
+
+        def decider(h):
+            c = slice(128 * h, 128 * h + 128)
+
+            def new(i):
+                d = slice(256 * i + 128 * h, 256 * i + 128 * h + 128)
+                return lambda: V("KEY%da KEY%db OM%d" % (h, h, i), "BB%d%d" % (i, h), "tt", T.BB[:, d], T["KEY%d" % h][:, 0:128], T.OM[:, d], AO.mult)
+            out = {"BB%d%d" % (i, h): new(i) for i in range(3)}
+            out.update({"OHD%d" % h: lambda: V("OHW LE", "OHD%d" % h, "tc", T.OHD[:, c], T.OHW[:, 0:16].indirect(T.LE[:, 64 + 8 * h:72 + 8 * h])),
+                        "SEL%d" % h: lambda: V("OHD%d LE %s" % (h, PFA), "SEL%d" % h, "tt", T.SEL[:, c],
+                                               T.PF[:, 0:4096].indirect(T.LE[:, 8 * h:8 * h + 8]), T.OHD[:, c], AO.mult),
+                        "DEC%d" % h: lambda: mms("BO SEL%d" % h, "KEY%da KEY%db" % (h, h), [(T["KEY%d" % h][:, 0:128], T.BO[:], T.SEL[:, c], True, True)])})
+            return out
+
+        def finish(name, X):
+            return lambda: last[name](X, 4)
+
+        def hand_on():
+            S("LO " + " ".join(both("FH", s) for s in range(1, 5)), fok, fo[:], T.FH[:, 0:1024].indirect(T.LO[:]), AF.Abs)
+            if t < 2:
+                send((rank + 1) % nrank, fo[:], T["FIN%d" % (t + 1)][:], "aF%d" % (t + 1), fok)
+            else:
+                dma("Y", fok, "yf", T.yf[:], fo[:])
+
+        def closed():
+            if t == 0:
+                V("DB3 DC3", "ZA", "tc", T.ZA[:, 0:1], bank(3, 1))
+            else:
+                V("DB3 DC3 ZA", "ZA", "tt", T.ZA[:, 0:1], bank(3, 1), T.ZA[:, 0:1], AO.add)
+        H13, CA = [" ".join(both(k, s) for s in ss) for k, ss in (("H", (1, 2, 3)), ("C", (1, 2, 3, 4)))]
+        H4 = both("H", 4)
+        end = {
+            "DV": lambda: V(" ".join(both("SC", s) for s in (1, 2, 3)), "DV1", "ts", T.DV[:, 16:64], T.SC[:, 16:816:17], 16, None, AO.arith_shift_right),
+            "AS": lambda: V("DV0 DV1", "AS", "tt", T.AS[:], T.DV[:, 0:48], T.DV[:, 16:64], AO.add),
+            "AZ": lambda: V("AS ZA", "AZ", "ts", T.AZ[:], T.AS[:], T.ZA[:, 0:1] if t else 0.0, None, AO.add),
+            "OD": lambda: V("AZ", "OD", "ts", T.OD[:], T.AZ[:], 1, None, AO.bitwise_and),
+            "C16": lambda: V(CA, "C16", "ts", T.C16[:], T.CB[:], 16.0, None, AO.mult),
+            "C16T": lambda: V("C16 TR", "C16T", "tt", T.C16T[:], T.C16[:], T.TR[:], AO.subtract),
+            "LV": lambda: V(both("H", 2) + " " + both("H", 3), "LV", "tc", T.LV[:], T.H5[:, 32:64]),
+            "PPa": lambda: V("C16 " + H13, "PPa", "tt", T.PP[:, 0:48], T.H5[:, 16:64], T.C16[:, 0:48], AO.add),
+            "PTa": lambda: V("C16T " + H13, "PTa", "tt", T.PT[:, 0:48], T.H5[:, 16:64], T.C16T[:, 0:48], AO.add),
+            "PPb": lambda: V("C16 " + H4, "PPb", "tt", T.PP[:, 48:64], T.H5[:, 64:80], T.C16[:, 48:64], AO.add),
+            "PTb": lambda: V("C16T " + H4, "PTb", "tt", T.PT[:, 48:64], T.H5[:, 64:80], T.C16T[:, 48:64], AO.add),
+            "CO": lambda: V("NE %s %s" % (" ".join("NE%d" % i for i in range(10)), CDA), "CO", "scan", T.CO[:], T.NE[:], T.CD[:], 0.0, AO.mult, AO.max),
+            "CW": lambda: V("CO LW POW", "CW", "tt", T.CW[:], T.CO[:, 0:176].indirect(T.LW[:]), T.POW[:], AO.mult),
+            "FI": lambda: V("CO", "FI", "ts", T.FI[:], T.CO[:, 10::11], 8, 1023, AO.arith_shift_right, AO.bitwise_and),
+            "FJ": lambda: V("FI XQ", "FJ", "tt", T.FJ[:], T.FI[:], T.XQ[:], AO.add),
+            "LO": lambda: V("FJ", "LO", "tc", T.LO[:], T.FJ[:]),
+            "FO": hand_on,
+            "DC": lambda: V("CW", "DC", "ts", T.DC[:], T.CW[:], 7, 1, AO.arith_shift_right, AO.bitwise_and),
+            "CH": lambda: V("CW", "CH", "ts", T.CH[:], T.CW[:], 3, 1, AO.arith_shift_right, AO.bitwise_and),
+            "PD": lambda: V("DC PPa PPb", "PD", "tt", T.PD[:], T.DC[:], T.PP[:], AO.mult),
+            "PC": lambda: V("CH PTa PTb", "PC", "tt", T.PC[:], T.CH[:], T.PT[:], AO.mult),
+            "D1": lambda: V("PD", "D1", "tt", T.D1[:], T.PD[:, 0:32], T.PD[:, 32:64], AO.add),
+            "YY": lambda: V("PC TR YY", "YY", "tt", T.YY[:, 0:16], T.PC[:, 48:64], T.TR[:, 0:16], AO.add),
+            "VVa": lambda: V("D1", "VVa", "tt", T.VV[:, 0:16], T.D1[:, 0:16], T.D1[:, 16:32], AO.add),
+            "VVb": lambda: V("PC YY", "VVb", "tt", T.VV[:, 16:64], T.PC[:, 0:48], T.YY[:], AO.add),
+            "VUa": lambda: V("VVa VVb", "VUa", "ts", T.VU[:, 0:64], T.VV[:], 4, None, AO.arith_shift_right),
+            "VUb": lambda: V("VVa VVb", "VUb", "ts", T.VU[:, 64:96], T.VV[:, 0:32], 15, None, AO.bitwise_and),
+            "LE": lambda: V("VUa VUb", "LE", "tc", T.LE[:], T.VU[:]),
+            "PUT": lambda: V("NP0 NP1 NP2 BB00 BB01 BB10 BB11 BB20 BB21 LE", "PFT " + PFA, "tt",
+                             T.PF[:, 0:4864].indirect(T.LE[:, 16:64]), T.NP[:], T.BB[:], AO.add)}
+        for i in range(10):
+            end.update({"N%d" % i: miss(i), "Y%d" % i: meaning(i)})
         for i in range(3):
-            S("OHC LEb", "OC%d" % i, T.OC[:, 256 * i:256 * i + 256], T.OHC[:, 0:16].indirect(T.LE[:, 80 + 16 * i:96 + 16 * i]), AF.Copy)
-        V("OHD LEa " + PFA, "SEL", "tt", T.SEL[:], T.PF[:, 0:4096].indirect(T.LE[:, 0:16]), T.OHD[:], AO.mult)
-        mms("BO SEL", "AUX", [(T.AUX[:, 0:256], T.BO[:], T.SEL[:], True, True)])
+            end.update(slot(i))
+        for X in range(2):
+            end.update(decider(X))
+            end.update({name + str(X): finish(name, X) for name in "MHIJF"})
         if t < 2:
-            mms("ONE ZR", "KEY0a", [(T.KEY0[:, 0:1], T.ONE[:], T.ZR[:, 0:1], True, True)])
-        for i in range(3):
-            c = slice(256 * i, 256 * i + 256)
-            S("OC%d" % i, "OM%d" % i, T.OM[:, c], T.OC[:, c], AF.Identity, scale=-1.0, bias=T.ONE[:, 0:1])
-            V("PFT OC%d LEa %s" % (i, PFA), "NP%d" % i, "tt", T.NP[:, c], T.PF[:, 0:4864].indirect(T.LE[:, 16 + 16 * i:32 + 16 * i]), T.OC[:, c], AO.mult)
-        for i in range(3):
-            c = slice(256 * i, 256 * i + 256)
-            V("AUX OM%d" % i, "BB%d" % i, "tt", T.BB[:, c], T.AUX[:, 0:256], T.OM[:, c], AO.mult)
-        if t == 0:
-            V("KEY0a", "ZA", "tc", T.ZA[:, 0:1], T.KEY0[:, 0:1])
-        elif t == 1:
-            V("KEY0a ZA", "ZA", "tt", T.ZA[:, 0:1], T.KEY0[:, 0:1], T.ZA[:, 0:1], AO.add)
-        V("NP0 NP1 NP2 BB0 BB1 BB2 LEa", "PFT " + PFA, "tt", T.PF[:, 0:4864].indirect(T.LE[:, 16:64]), T.NP[:], T.BB[:], AO.add)
+            end.update({"ZR": lambda: V("DC", "ZR", "red", T.ZR[:, 0:1], T.DC[:], AxisListType.X, AO.add),
+                        "ZP": lambda: mms("ONE ZR", "DB3 DC3", [(bank(3, 1), T.ONE[:], T.ZR[:, 0:1], True, True)]),
+                        "ZA": closed, "LC": lambda: first_courts(t + 1)})
+        for name in END:
+            if name in end:
+                end[name]()
         if t < 2:
             first_facts(T["FIN%d" % (t + 1)], "FIN%d" % (t + 1))
-    for q in range(4):
-        c0, c1, k = 512 * q, 512 * q + 512, str(q)
-        S("PFH" + k, "DB" + k, DB[q][:], T.PF[:, 2048 + c0:2048 + c1], AF.Copy, scale=4096.0)
-        V("DB%s PFL%s" % (k, k), "YO" + k, "tt", T.YO[:, c0:c1], DB[q][:], T.PF[:, c0:c1], AO.add)
-        dma("Y", "YO" + k, "yp" + k, T.yp[:, c0:c1], T.YO[:, c0:c1])
+    c0, q = 0, 0
+    for pieces in OUT:
+        d0, keys = c0, ""
+        for n in pieces:
+            if q == 0:
+                V(PFA, "DB0", "ts", bank(0, n), T.PF[:, 2048:2048 + n], 4096.0, None, AO.mult)
+            else:
+                S(PFA, "DB%d" % (q % 4), bank(q % 4, n), T.PF[:, 2048 + c0:2048 + c0 + n], AF.Copy, scale=4096.0)
+            V("DB%d %s" % (q % 4, PFA), "YO%d" % q, "tt", T.YO[:, c0:c0 + n], bank(q % 4, n), T.PF[:, c0:c0 + n], AO.add)
+            c0, q, keys = c0 + n, q + 1, keys + " YO%d" % q
+        dma("Y", keys, "yp%d" % q, T.yp[:, d0:c0], T.YO[:, d0:c0])
     for sem in SEMAPHORES:
         if cnt[sem] and sem != "ls":
             need("G", sem, cnt[sem])

@@ -3,19 +3,21 @@ import comms_topo
 
 AO = AluOpType
 AF = ActivationFunctionType
-SHARE = {None: (88, 128), 0: (32, 80), 1: (80, 128), 7: (68, 96)}
-CUTS = (0, 32, 64, 96, 128)
-PHASE = {"M": -0.92, "H": -0.86, "I": -0.67, "J": -0.50, "E": -0.49, "F": -0.34, "T": -0.26, "G0": -0.20, "A": -0.18, "P0": -0.14, "L0": -0.06,
-         "G1": -0.045, "G2": -0.03, "G3": 0.04, "S": 0.07, "L1": 0.09, "K": 0.165, "P1": 0.23, "P2": 0.51, "L2": 0.56, "Z0": 0.57, "P3": 0.59,
-         "Z1": 0.68, "L3": 0.72, "Z2": 0.77, "U0": 0.84, "Z3": 0.91, "U1": 1.01}
-OTHER = {("L0", 0): -1.0, ("L1", 0): -0.99, ("L2", 0): -0.98, ("L3", 0): -0.97, ("U1", 6): 1.3, ("K", 7): 0.95}
-START = ("WF OHW XQ WB X16 SRB L8 SRG JQ JT0 JT1 JT2 JT3 JT4 JT5 JT6 JT7 E17a E17b MS IDB JM KA KB TW0 TW1 TW2 TW3 HP0 HP1 HP2 HP3 ND PH3 "
-         "K0 PL0 K1a K1b PL1 SU PH0 PH1 PH2 PL2 LC PL3 FF ST IL LW").split()
-END = ("DV LV AS N4 AZ N5 OD C16 M0 N6 H0 PPa I0 C16T J0 N7 N8 N9 Y0 Y1 Y2 Y4 Y5 Y7 PTa F0 "
-       "OL1 OM1 OC1 OM2 OL2 OC2 NP1 "
-       "M1 H1 N0 N1 N2 N3 I1 CO J1 FI CW FJ F1 DC LO FO NP2 CH PPb PTb PD PC D1 YY VVa VVb VUa VUb LE "
-       "OHD0 OM0 OL0 OC0 SEL0 DEC0 OHD1 ZR SEL1 DEC1 LC BB00 BB10 BB20 NP0 BB01 BB11 BB21 ZP PUT ZA").split()
-ON_V = ("PH3",)
+SHARE = {None: (32, 80, 96), 0: (32, 32, 96)}
+PHASE = {"M": -1.15, "H": -1.12, "B": -1.036, "D1": -1.021, "P1": -0.961, "D0": -0.928, "J": -0.853, "P0": -0.789, "L": -0.641, "F": -0.638,
+         "E": -0.596, "K": -0.522, "S1": -0.491, "T": -0.398, "G": -0.285, "C": -0.28, "R1": -0.195, "S0": -0.063, "S2": -0.052, "R0": -0.014,
+         "Y": 0.045, "N1": 0.104, "N0": 0.194, "R3": 0.387, "R2": 0.413, "N3": 0.484, "U": 0.501, "N2": 0.507, "W": 0.799}
+OTHER = {("E", 0): -2.104, ("K", 0): -1.786, ("T", 0): -1.0, ("C", 0): -0.861, ("G", 0): -0.596, ("R1", 0): -0.456, ("N0", 0): 0.012,
+         ("R2", 0): 0.378, ("N3", 0): 0.527, ("U", 0): 0.586, ("W", 0): 0.624, ("K", 1): -1.214, ("T", 1): -0.664, ("C", 1): -0.467,
+         ("R0", 1): -0.033, ("P0", 6): -0.869, ("R1", 6): -0.197, ("N3", 6): 0.677, ("J", 7): -0.784, ("T", 7): -0.287, ("C", 7): -0.215,
+         ("R1", 7): -0.189, ("N1", 7): 0.18, ("N3", 7): 0.564, ("N2", 7): 0.576}
+START = ("L8 IDF IL SRB LR JQ XQ MK SRG WF XM AI KB MS JM TW0 HP0 IDB TW1 OHW KA GU TW2 TW3 SH SL PH3 K0 CB HP1 LW HP2 PH2 HP3 PL0 LC GW "
+         "PL1 HS PH1 WB PH0 PL3 PL2").split()
+END = ("@6.395 C16 @6.446 HA @6.593 SUM N4 @6.750 DV @6.874 AS @6.942 N5 C16T @7.112 M0 N8 H0 @7.291 N9 @7.400 PTa @7.457 D10 P10 "
+       "@7.687 HR0 K0 N6 AZ @9 J0 OL1 OD Y2 Y5 N7 PPa M1 Y7 OM2 H1 D11 Y4 CB P11 F0 OL2 Y1 HR1 J1 Y0 N2 N0 N1 N3 PPb CO F1 CW FI PTb CH DC "
+       "PC PD YY FJ OC2 D1 OM1 VVb OC1 NP1 VVa LO VUb VUa LE OHD0 OHD1 FO SEL0 OM0 SEL1 OL0 LC ZR DEC0 OC0 DEC1 BB00 NP2 BB10 ZP BB01 BB11 "
+       "BB20 NP0 BB21 ZA PUT HS").split()
+ON_V = ("PH3", "C")
 LOADS = ((0, 1), (1, 2), (2, 3), (3, 4))
 OUT = ((384,), (512,), (512,), (384,), (256,))
 HITS = [(s, j) for s in (4, 3, 2, 1) for j in range(s)]
@@ -30,27 +32,29 @@ def _s(name, cols, dtype, where="sbuf"):
 
 for _n, _c, _d in [
         ("R", 4096, BF), ("PF", 4864, F32), ("PK", 2048, I32), ("TW", 2048, F32), ("YO", 2048, F32),
-        ("JI", 256, I32), ("JQ", [16, 16], F32), ("JT", [16, 128], F32), ("SRI", 256, I32), ("SRB", 256, BF),
-        ("MS", 256, F32), ("JM", 256, F32), ("K0", 16, I32), ("K1", 32, I32),
+        ("JI", 256, I32), ("JQ", 256, F32), ("SRI", 256, I32), ("SRB", 256, BF),
+        ("MS", 256, F32), ("JM", 256, F32), ("K0", 16, I32), ("CB", 16, I32),
         ("FX0", 256, BF), ("FIN1", 256, BF), ("FIN2", 256, BF), ("FO0", 256, BF), ("FO1", 256, BF), ("FO2", 256, BF),
-        ("ST0", 304, F32), ("ST1", 304, F32), ("ST2", 304, F32),
-        ("RG", 8192, BF), ("A", [256, 17], BF), ("FH", 1024, BF), ("FT", 256, BF), ("FD", 256, BF),
-        ("NU", 256, U16), ("SC", 1088, I32), ("H5", 80, I32), ("CB", 64, I32), ("FA", 16, I32), ("LC", 64, U16), ("LF", 16, U16), ("LV", 32, U16),
-        ("DV", 64, I32), ("AS", 48, I32), ("AZ", 48, I32), ("OD", 48, I32), ("C16", 64, F32), ("C16T", 64, F32),
+        ("ST0", 544, BF), ("ST1", 544, BF), ("ST2", 544, BF),
+        ("RG", 8192, BF), ("A", 4096, BF), ("FH", 2560, BF), ("FT", 512, BF), ("FD", 256, BF),
+        ("NU", 256, U16), ("SC", 256, I32), ("HC", 32, I32), ("KC", 256, F32), ("KH", 256, BF), ("LL", [3, 80], U16), ("H5", 80, I32),
+        ("DV", 64, F32), ("AS", 48, F32), ("AZ", 48, I32), ("OD", 48, I32), ("C16", 64, F32), ("C16T", 64, F32),
         ("NE", 176, F32), ("CD", 176, F32), ("CO", 176, I32), ("CW", 64, I32), ("FJ", 16, F32),
         ("CH", 64, I32), ("DC", 64, I32), ("PP", 64, F32), ("PT", 64, F32), ("PC", 64, F32), ("PD", 64, F32), ("D1", 32, F32),
         ("YY", 48, F32), ("VV", 64, I32), ("VU", 96, I32), ("LE", 96, U16), ("FI", 16, I32), ("LO", 16, U16),
         ("OHD", 256, F32), ("SEL", 256, F32), ("OL", 768, F32), ("OM", 768, BF), ("NP", 768, F32), ("BB", 768, F32),
         ("ZR", 1, F32), ("ZA", 1, F32),
-        ("IM", 160, F32), ("IG", 128, F32), ("IPI", 2, I32), ("IQI", 6, I32), ("CF", 8, F32), ("XN", 512, BF), ("ND", 512, BF),
+        ("IM", 160, F32), ("IG", 128, F32), ("IB", 128, F32), ("IPI", 2, I32), ("IQI", 4, I32), ("CF", 8, F32), ("RS", 128, F32),
         ("IDB", 128, BF), ("IDF", 128, F32), ("NB", 128, BF), ("WB", 144, BF), ("WF", 144, F32), ("BO", 128, F32), ("ONE", 128, F32),
-        ("L8", 128, BF), ("MG", 8, F32), ("OHW", 24, F32), ("E17", 17, F32), ("IA", 16, F32), ("XQ", 16, F32), ("X16", 8, F32), ("BI", 2, F32),
+        ("GU", 8, BF), ("GW", 8, BF), ("AI", 8, BF), ("MK", 128, F32), ("XM", 128, BF), ("LR", 8, U16),
+        ("L8", 128, BF), ("MG", 8, F32), ("OHW", 24, F32), ("IA", 16, F32), ("XQ", 16, F32), ("BI", 2, F32),
         ("POW", 64, F32), ("IL", 4, F32), ("LW", 4, U16), ("TRI", 64, F32), ("TR", 64, F32)]:
     _s(_n, _c, _d)
-_s("DB", 2048, F32, "psum")
-for _n in ["KEY0", "KEY1", "AUX"]:
+for _n in ["DB0", "DB1", "DB2", "KEY0", "KEY1"]:
     _s(_n, 512, F32, "psum")
 _s("FTP", 1024, BF, "psum")
+for _n in ["FP0", "FP1"]:
+    _s(_n, [64, 16], BF, "psum")
 
 SEMAPHORES = ["sv", "ss", "sp", "sg", "aS1", "aS2", "aF1", "aF2", "ls"] + ["d%d" % i for i in range(16)]
 
@@ -59,11 +63,16 @@ def at(name, n):
     return n + OTHER.get((name, n), PHASE[name])
 
 
+def shares(n):
+    c0, c1, c2 = SHARE.get(n, SHARE[None])
+    return {"S0": (0, c0), "S1": (c0, c1), "G": (c1, c2), "S2": (c2, 128)}
+
+
 def codes(odd):
-    out = [(3 << 16) + (11 << 20)]
+    out = [(4 << 16) + (11 << 20)]
     for i, (s, j) in enumerate(HITS):
         d = s if odd else j + 1
-        out.append(sum(8 >> (u - 1) for u in range(j + 1, s + 1) if u != d) + (128 >> (d - 1)) + ((s - 1) << 16) + ((10 - i) << 20))
+        out.append(sum(8 >> (u - 1) for u in range(j + 1, s + 1) if u != d) + (128 >> (d - 1)) + (s << 16) + ((10 - i) << 20))
     return out
 
 
@@ -75,9 +84,10 @@ def rank_program(g, core, T, topo):
     ENG = {"V": (g.vector, "sv"), "S": (g.scalar, "ss"), "P": (g.tensor, "sp"), "G": (g, "sg"), "Y": (g.sync, None)}
     cnt = {s: 0 for s in SEMAPHORES}
     waited, Wr, Rd, ndma = {}, {}, {}, [0]
+    BANKS = ("DB0", "DB1", "DB2", "KEY1", "KEY0")
 
     def bank(j, n=512):
-        return T.DB[:, 512 * j:512 * j + n]
+        return T[BANKS[j]][:, 0:n]
 
     def need(e, sem, val):
         if waited.get((e, sem), 0) < val:
@@ -94,6 +104,8 @@ def rank_program(g, core, T, topo):
                 todo[s] = max(todo.get(s, 0), v)
             for s, v in Rd.get(k, {}).items():
                 todo[s] = max(todo.get(s, 0), v)
+        if e == "P":
+            todo.pop("sp", None)
         for s, v in todo.items():
             need(e, s, v)
 
@@ -127,11 +139,11 @@ def rank_program(g, core, T, topo):
             g.tensor.matmul(*c)
         run("P", reads, writes, "mm", *calls[-1])
 
-    def turns(reads, calls):
-        sync("P", reads.split() + ["IDB"], ["FTP"])
+    def turns(reads, writes, calls):
+        sync("P", reads.split() + ["IDB"], writes.split())
         for c in calls[:-1]:
             g.tensor.transpose(*c)
-        run("P", reads + " IDB", "FTP", "tr", *calls[-1])
+        run("P", reads + " IDB", writes, "tr", *calls[-1])
 
     def dma(e, reads, writes, out, in_):
         reads, writes = reads.split(), writes.split()
@@ -164,26 +176,29 @@ def rank_program(g, core, T, topo):
     run("G", "", "IPI", "iota", T.IPI[:], [[0, 2]], 0, 1)
     iota("IM", T.IM[:], [[1, 160]], 0)
     iota("IG", T.IG[:], [[1, 8], [0, 16]], 0)
-    iota("IA", T.IA[:], [[16, 16]], 0)
-    iota("XN", T.XN[:], [[1, 32], [0, 16]], 0)
-    iota("A17", T.A[:, :, 16], [[0, 256]], 255)
+    iota("IA", T.IA[:], [[32, 16]], 0)
+    iota("IB", T.IB[:], [[0, 8], [1, 16]], 0)
+    iota("RS", T.RS[:], [[0, 128]], 1 - 2 ** 24)
+    iota("RS", T.RS[:, 0::16], [[0, 8]], 2 ** 24 - 1)
     CUT, BIG = 4096.0 * 2047 + 2047.5, 1.5 * 2.0 ** 35
     V("", "BI0", "memset", T.BI[:, 0:1], 2047 - BIG / 4096)
     V("", "BI1", "memset", T.BI[:, 1:2], 4096.0 * 2047 - BIG)
     V("IPI", "IQ0", "ts", T.IQI[:, 0:2], T.IPI[:], 15, None, AO.bitwise_and)
     V("IPI", "IQ1", "ts", T.IQI[:, 2:4], T.IPI[:], 4, None, AO.arith_shift_right)
-    V("IPI", "IQ2", "ts", T.IQI[:, 4:6], T.IPI[:], 31, None, AO.bitwise_and)
     V("IQ0", "CF5", "ts", T.CF[:, 5:6], T.IQI[:, 0:1], 4096.0, None, AO.mult)
     V("IPI", "CF0", "tc", T.CF[:, 0:1], T.IPI[:, 0:1])
-    V("IQ0 IQ1 IQ2", "CF1", "tc", T.CF[:, 1:4], T.IQI[:, 0:6:2])
+    V("IQ0 IQ1", "CF1", "tc", T.CF[:, 1:3], T.IQI[:, 0:4:2])
+    V("IQ0", "CF3", "ts", T.CF[:, 3:4], T.IQI[:, 0:1], 2.0, None, AO.mult)
     V("IQ1", "CF4", "ts", T.CF[:, 4:5], T.IQI[:, 2:3], 16.0, 15.0, AO.mult, AO.add)
-    p_c, q_c, g_c, r_c, e_c, k_c = [T.CF[:, i:i + 1] for i in range(6)]
+    V("IPI", "CF6", "ts", T.CF[:, 6:7], T.IPI[:, 0:1], 16.0, None, AO.mult)
+    p_c, q_c, g_c, r_c, e_c, k_c, x_c = [T.CF[:, i:i + 1] for i in range(7)]
     V("IM CF1", "MG", "ts", T.MG[:], T.IM[:, 0:8], g_c, None, AO.is_equal)
 
     EVEN, ODD = codes(0), codes(1)
 
     def late_constants():
         iota("PFT", T.PF[:, 4096:4864], [[0, 768]], 0)
+        iota("FHT", T.FH[:, 2049:2560:2], [[0, 256]], 0)
         iota("TRIa", T.TRI[:, 0:48], [[16, 48]], 4096)
         iota("TRIb", T.TRI[:, 48:64], [[16, 16]], 4096)
         iota("ONE", T.ONE[:], [[0, 128]], 1)
@@ -197,189 +212,200 @@ def rank_program(g, core, T, topo):
     def late_constants_v():
         return [lambda: V("TRIa TRIb CF1", "TR", "ts", T.TR[:], T.TRI[:], q_c, 16.0, AO.add, AO.mult),
                 lambda: V("TR", "YY", "tc", T.YY[:], T.TR[:, 0:48]),
-                lambda: V("IM CF0", "IDF", "ts", T.IDF[:], T.IM[:, 0:128], p_c, None, AO.is_equal),
                 lambda: V("IDB", "NB", "ts", T.NB[:], T.IDB[:], -4096.0, None, AO.mult),
                 lambda: V("IG CF1", "BO", "ts", T.BO[:], T.IG[:], g_c, None, AO.is_equal)]
     CDA = " ".join("CD%d" % i for i in range(11))
     PFA = " ".join("PFH%d PFL%d" % (q, q) for q in range(4))
 
-    def first_courts(t):
-        V("SU%d" % t, "LC01 LC11", "tc", T.LC[:, 0:16], T["ST%d" % t][:, 272:288])
+    def both(k, s):
+        return "%s0%d %s1%d" % (k, s, k, s)
 
-    def first_facts(fin, fk):
-        turns(fk, [(T.FTP[:, 128 * X:128 * X + 128], fin[:, 128 * X:128 * X + 128], T.IDB[:]) for X in range(2)])
-        S("FTP", "FT0 FT1", T.FT[:], T.FTP[:, 0:256], AF.Copy)
-        mms("WB " + fk, "AUX", [(T.AUX[:, 0:16], T.WB[:, 15 - b:143 - b], fin[:, b::16], b == 0, b == 15) for b in range(16)])
+    def first(t):
+        st = T["ST%d" % t]
+        return {"K0": lambda: V("SH%d SL%d" % (t, t), "K0", "tt", T.K0[:], st[:, 256:272], st[:, 528:544], AO.add),
+                "CB": lambda: V("K0", "CB", "ts", T.CB[:], T.K0[:], 4095, None, AO.bitwise_and),
+                "LC": lambda: V("CB", both("LC", 1), "tc", T.LL[:, 0, 0:16], T.CB[:]),
+                "HS": lambda: V("K0", both("H", 0), "ts", T.H5[:, 0:16], T.K0[:], 12, None, AO.arith_shift_right)}
 
     def unpack(q):
-        c, h, k = slice(512 * q, 512 * q + 512), slice(2048 + 512 * q, 2560 + 512 * q), str(q)
+        c, h, k, j = slice(512 * q, 512 * q + 512), slice(2048 + 512 * q, 2560 + 512 * q), str(q), (q + 3) % 5
         return {"TW" + k: lambda: V("PK" + k, "TW" + k, "ts", T.TW[:, c], T.PK[:, c], CUT, BIG, AO.subtract, AO.add),
-                "HP" + k: lambda: S("TW%s BI1" % k, "DB" + k, bank(q), T.TW[:, c], AF.Identity, bias=T.BI[:, 1:2]),
+                "HP" + k: lambda: S("TW%s BI1" % k, BANKS[j], bank(j), T.TW[:, c], AF.Identity, bias=T.BI[:, 1:2]),
                 "PH" + k: (lambda: V("TW" + k, "PFH" + k, "ts", T.PF[:, h], T.TW[:, c], 2.0 ** -12, 2047 - BIG / 4096, AO.mult, AO.add))
                 if "PH" + k in ON_V else
                 (lambda: S("TW%s BI0" % k, "PFH" + k, T.PF[:, h], T.TW[:, c], AF.Identity, scale=2.0 ** -12, bias=T.BI[:, 0:1])),
-                "PL" + k: lambda: V("PK%s DB%s" % (k, k), "PFL" + k, "tt", T.PF[:, c], T.PK[:, c], bank(q), AO.subtract)}
-
-    def block(h):
-        if "JT%d" % h in ON_V:
-            return lambda: V("JQ MG", "JT%d" % h, "ts", T.JT[:, :, 16 * h:16 * h + 16], T.JQ[:, :, :], T.MG[:, h:h + 1], None, AO.mult)
-        return lambda: S("JQ MG", "JT%d" % h, T.JT[:, :, 16 * h:16 * h + 16], T.JQ[:, :, :], AF.Identity, scale=T.MG[:, h:h + 1])
+                "PL" + k: lambda: V("PK%s %s" % (k, BANKS[j]), "PFL" + k, "tt", T.PF[:, c], T.PK[:, c], bank(j), AO.subtract)}
 
     start = {
         "WF": lambda: V("IM CF4", "WF", "ts", T.WF[:, 0:143], T.IM[:, 0:143], e_c, None, AO.is_equal),
-        "E17a": lambda: V("OHW", "E17a", "tt", T.E17[:, 1:17], T.OHW[:, 0:16], T.OHW[:, 1:17], AO.subtract),
-        "E17b": lambda: V("OHW", "E17b", "ts", T.E17[:, 0:1], T.OHW[:, 15:16], 1024.0, None, AO.mult),
         "OHW": lambda: V("IM CF1", "OHW", "ts", T.OHW[:], T.IM[:, 0:24], q_c, None, AO.is_equal),
         "L8": lambda: V("IG CF0", "L8", "ts", T.L8[0:8, :], T.IG[0:8, :], T.CF[0:8, 0:1], None, AO.is_equal),
-        "WB": lambda: S("WF", "WB", T.WB[:, 0:143], T.WF[:, 0:143], AF.Copy, scale=65536.0),
+        "WB": lambda: S("WF", "WB", T.WB[:, 0:143], T.WF[:, 0:143], AF.Copy),
+        "GU": lambda: S("MG", "GU", T.GU[:], T.MG[:], AF.Copy, scale=65536.0),
+        "GW": lambda: S("MG", "GW", T.GW[:], T.MG[:], AF.Copy, scale=-131072.0),
+        "AI": lambda: S("MG", "AI", T.AI[:], T.MG[:], AF.Copy),
+        "IDF": lambda: V("IM CF0", "IDF", "ts", T.IDF[:], T.IM[:, 0:128], p_c, None, AO.is_equal),
+        "LR": lambda: V("IM", "LR", "tc", T.LR[:], T.IM[:, 0:8]),
+        "MK": lambda: V("IB CF1", "MK", "ts", T.MK[:], T.IB[:], q_c, None, AO.is_equal),
+        "XM": lambda: S("MK CF6", "XM", T.XM[:], T.MK[:], AF.Identity, scale=x_c),
         "IDB": lambda: V("IM CF0", "IDB", "ts", T.IDB[:], T.IM[:, 0:128], p_c, None, AO.is_equal),
-        "XQ": lambda: S("IA CF1", "XQ", T.XQ[:], T.IA[:], AF.Identity, bias=q_c),
-        "ND": lambda: V("XN CF1", "ND", "ts", T.ND[:], T.XN[:], r_c, -1.0, AO.is_equal, AO.mult),
-        "X16": lambda: S("XQ", "X16", T.X16[:], T.XQ[:, 0:8], AF.Copy, scale=16.0),
+        "XQ": lambda: S("IA CF3", "XQ", T.XQ[:], T.IA[:], AF.Identity, bias=r_c),
         "IL": lambda: V("IM CF1", "IL", "ts", T.IL[:], T.IM[:, 0:4], 0.0, q_c, AO.mult, AO.add),
         "LW": lambda: V("IL", "LW", "ts", T.LW[:], T.IL[:], 11.0, 10.0, AO.mult, AO.add),
-        "JQ": lambda: V("JI CF5", "JQ", "ts", T.JQ[:, :, :], T.JI[:], k_c, None, AO.add),
+        "JQ": lambda: V("JI CF5", "JQ", "ts", T.JQ[:], T.JI[:], k_c, None, AO.add),
         "SRB": lambda: V("SRI", "SRB", "tc", T.SRB[0:8, :], T.SRI[0:8, :]),
-        "SRG": lambda: mms("L8 SRB", "AUX", [(T.AUX[:, 0:256], T.L8[0:8, :], T.SRB[0:8, :], True, True)]),
-        "MS": lambda: V("AUX CF1", "MS", "ts", T.MS[:], T.AUX[:, 0:256], q_c, None, AO.is_equal),
-        "JM": lambda: V("MS JQ", "JM", "tt", T.JM[:], T.MS[:], T.JQ[:, :, :], AO.mult),
-        "KA": lambda: mms("WF JM", "KEY0a KEY0b",
-                          [(T.KEY0[:, 0:16], T.WF[:, 15 - b:143 - b], T.JM[:, b::16], b == 0, b == 15) for b in range(16)]),
-        "KB": lambda: mms("JT0 JT1 JT2 JT3 JT4 JT5 JT6 JT7 E17a E17b", "KEY1a KEY1b",
-                          [(T.KEY1[:, 17 * a:17 * a + 17], T.JT[:, a, :], T.E17[:], True, True) for a in range(16)]),
-        "K0": lambda: V("KEY0a KEY0b", "K0", "tc", T.K0[:], T.KEY0[:, 0:16]),
-        "K1a": lambda: V("K0", "K1a", "ts", T.K1[:, 0:16], T.K0[:], 4095, None, AO.bitwise_and),
-        "K1b": lambda: V("K0", "K1b", "ts", T.K1[:, 16:32], T.K0[:], 12, None, AO.arith_shift_right),
-        "SU": lambda: V("K1a K1b", "SU0", "tc", T.ST0[:, 272:304], T.K1[:]),
-        "ST": (lambda: V("KEY1a KEY1b", "ST0", "tc", T.ST0[:, 0:272], T.KEY1[:, 0:272])) if "ST" in ON_V else
-              (lambda: S("KEY1a KEY1b", "ST0", T.ST0[:, 0:272], T.KEY1[:, 0:272], AF.Copy)),
-        "LC": lambda: first_courts(0),
-        "FF": lambda: first_facts(T.FX0, "FX0")}
+        "SRG": lambda: mms("L8 SRB", "DB1", [(T.DB1[:, 0:256], T.L8[0:8, :], T.SRB[0:8, :], True, True)]),
+        "MS": lambda: V("DB1 CF1", "MS", "ts", T.MS[:], T.DB1[:, 0:256], q_c, None, AO.is_equal),
+        "JM": lambda: V("MS JQ", "JM", "tt", T.JM[:], T.MS[:], T.JQ[:], AO.mult),
+        "KA": lambda: mms("WF JM", "DB2",
+                          [(T.DB2[:, 256:272], T.WF[:, 15 - b:143 - b], T.JM[:, b::16], b == 0, b == 15) for b in range(16)]),
+        "KB": lambda: mms("JQ IDF", "DB2", [(T.DB2[:, 128 * X:128 * X + 128], T.JQ[:, 128 * X:128 * X + 128], T.IDF[:], True, True) for X in range(2)]),
+        "SH": lambda: S("DB2", "SH0", T.ST0[:, 0:272], T.DB2[:, 0:272], AF.Copy),
+        "SL": lambda: V("DB2 SH0", "SL0", "tt", T.ST0[:, 272:544], T.DB2[:, 0:272], T.ST0[:, 0:272], AO.subtract)}
+    start.update(first(0))
     for q in range(4):
         start.update(unpack(q))
-    for h in range(8):
-        start["JT%d" % h] = block(h)
     for name in START:
         start[name]()
-    send((rank + 1) % nrank, T.ST0[:], T.ST1[:], "aS1", "ST0 SU0")
-    send((rank + 2) % nrank, T.ST0[:], T.ST2[:], "aS2", "ST0 SU0")
+    send((rank + 1) % nrank, T.ST0[:], T.ST1[:], "aS1", "SH0 SL0")
+    send((rank + 2) % nrank, T.ST0[:], T.ST2[:], "aS2", "SH0 SL0")
     late_constants()
-    Wr["ST1"], Wr["ST2"], Wr["SU1"], Wr["SU2"] = {"aS1": narr}, {"aS2": narr}, {"aS1": narr}, {"aS2": narr}
-    Wr["FIN1"], Wr["FIN2"] = {"aF1": narr}, {"aF2": narr}
+    for t in (1, 2):
+        Wr["SH%d" % t], Wr["SL%d" % t], Wr["FIN%d" % t] = {"aS%d" % t: narr}, {"aS%d" % t: narr}, {"aF%d" % t: narr}
 
     for t in range(3):
-        st, stk, suk = T["ST%d" % t], "ST%d" % t, "SU%d" % t
+        st, stk = T["ST%d" % t], "SH%d SL%d" % (t, t)
         fin, fk = (T.FX0, "FX0") if t == 0 else (T["FIN%d" % t], "FIN%d" % t)
         fo, fok = T["FO%d" % t], "FO%d" % t
 
         def entries(X, s):
             l0 = 16 * s - 16 + 8 * X
-            V("%s LC%d%d" % (PFA, X, s), "NU%d" % X, "tc", T.NU[:, 128 * X:128 * X + 128], T.PF[:, 0:4096].indirect(T.LC[:, l0:l0 + 8]))
+            V("%s LC%d%d" % (PFA, X, s), "NU%d" % X, "tc", T.NU[:, 128 * X:128 * X + 128], T.PF[:, 0:4096].indirect(T.LL[:, 0, l0:l0 + 8]))
+
+        def got(w, rows):
+            return " ".join("RG%d%d%s" % (w, r, e) for r in rows for e in "VS")
 
         def rules(e, n, x0, x1):
             if x0 >= x1:
                 return
             X, w = n % 2, n % 4
-            wr = " ".join("RG%d%d%s" % (w, j, e) for j in range(x0 // 32, (x1 + 31) // 32))
+            wr = " ".join("RG%d%d%s" % (w, r, e) for r in range(x0 // 32, (x1 + 31) // 32))
             out, src = T.RG[:, 2048 * w + 16 * x0:2048 * w + 16 * x1], T.R[:, 0:4096].indirect(T.NU[:, 128 * X + x0:128 * X + x1])
             if e == "V":
                 V("R NU%d" % X, wr, "tc", out, src)
             else:
                 S("R NU%d" % X, wr, out, src, AF.Copy)
 
-        def less(n, j):
-            first, X = at("L%d" % j, n) < at("P%d" % j, n), n % 2
-            run("P", "FT%d ND" % X, "DB%d" % j if first else "DC%d" % j, "mm",
-                bank(j), T.FT[32 * j:32 * j + 32, 128 * X:128 * X + 128], T.ND[32 * j:32 * j + 32, :], first, not first)
+        def smaller(n, r):
+            X, w, f0 = n % 2, n % 4, 32 * (r // 2)
+            a0, r0 = 2048 * X + 512 * r, 2048 * w + 512 * r
+            V("FP%d %s" % (r % 2, got(w, [r])), "A%d%d" % (X, r), "tt", T.A[:, a0:a0 + 512], T.RG[:, r0:r0 + 512],
+              T["FP%d" % (r % 2)][:, f0:f0 + 32, :], AO.min)
 
-        def plus(n, j):
-            first, w = at("P%d" % j, n) < at("L%d" % j, n), n % 4
-            run("P", "IDB RG%d%dV RG%d%dS" % (w, j, w, j), "DB%d" % j if first else "DC%d" % j, "mm",
-                bank(j), T.IDB[:], T.RG[:, 2048 * w + 512 * j:2048 * w + 512 * j + 512], first, not first)
+        def payloads(n):
+            X = n % 2
+            k = T["KEY%d" % X][:, 0:128]
+            mms("IDB " + stk, "KEY%d" % X, [(k, T.IDB[:], st[:, 128 * X:128 * X + 128], True, False),
+                                            (k, T.IDB[:], st[:, 272 + 128 * X:400 + 128 * X], False, False)])
 
-        def size(X, j):
-            S("DB%d DC%d" % (j, j), "A%d%d" % (X, j), T.A[:, 128 * X + 32 * j:128 * X + 32 * j + 32, 0:16], bank(j), AF.Abs)
-
-        def sums(X, h):
-            x0 = 128 * X + 64 * h
-            mms("WB A17 A%d%d A%d%d" % (X, 2 * h, X, 2 * h + 1), "KEY%d%s" % (X, "ab"[h]),
-                [(T["KEY%d" % X][:, 68 * h:68 * h + 68], T.WB[:, 15 - b:143 - b], T.A[:, x0 + b:x0 + 64:16, :], b == 0, b == 15) for b in range(16)])
+        def sums(n, of):
+            X, w = n % 2, n % 4
+            rd, src, c0, m = (("GU " + got(w, range(4)), T.RG, 2048 * w, T.GU) if of == "U" else
+                              ("GW " + " ".join("A%d%d" % (X, r) for r in range(4)), T.A, 2048 * X, T.GW))
+            mms(rd, "KEY%d" % X, [(T["KEY%d" % X][:, k:128:16], src[:, c0 + k:c0 + 2048:16], m[:], False, of == "W" and k == 15) for k in range(16)])
 
         def least(X, s):
-            c0 = 272 * (s - 1) + 136 * X
-            V("%s KEY%da KEY%db" % (stk, X, X), "SC%d%d" % (X, s), "scan", T.SC[:, c0:c0 + 136], st[:, 136 * X:136 * X + 136],
-              T["KEY%d" % X][:, 0:136], 0.0, AO.add, AO.min)
+            V("RS KEY%d" % X, "SC%d" % X, "scan", T.SC[:, 128 * X:128 * X + 128], T.RS[:], T["KEY%d" % X][:, 0:128], 0.0, AO.max, AO.min)
 
         def row(X, s):
-            k, c0, a0 = "%d%d" % (X, s), 272 * (s - 1) + 136 * X, 16 * s + 8 * X
-            V("SC" + k, "H" + k, "ts", T.H5[:, a0:a0 + 8], T.SC[:, c0 + 16:c0 + 136:17], 12, 15, AO.arith_shift_right, AO.bitwise_and)
-            if s < 4:
-                V("SC" + k, "C%d%d" % (X, s + 1), "ts", T.CB[:, a0:a0 + 8], T.SC[:, c0 + 16:c0 + 136:17], 4095, None, AO.bitwise_and)
+            V("SC%d" % X, "HX%d" % X, "ts", T.HC[:, 16 * X + 8:16 * X + 16], T.SC[:, 128 * X + 15:128 * X + 128:16], 12, 15,
+              AO.arith_shift_right, AO.bitwise_and)
 
-        def place(X, s):
+        def court(X, s):
+            V("SC%d" % X, "CX%d" % X, "ts", T.HC[:, 16 * X:16 * X + 8], T.SC[:, 128 * X + 15:128 * X + 128:16], 4095, None, AO.bitwise_and)
+
+        def spread(X, j):
+            c0 = 16 * X + 8 * j
+            V("LR MK %sX%d" % ("CH"[j], X), "K%s%d" % ("CH"[j], X), "tt", (T.KC, T.KH)[j][:, 128 * X:128 * X + 128],
+              T.HC[:, c0:c0 + 8].indirect(T.LR[:]), T.MK[:], AO.mult)
+
+        def route(X, j):
+            c = slice(128 * X, 128 * X + 128)
+            if j == 0:
+                mms("MG KC%d" % X, "DB1", [(T.DB1[:, 0:8], T.KC[:, c], T.MG[:], True, True)])
+            else:
+                mms("AI XM KH%d" % X, "DB2", [(T.DB2[:, 0:8], T.XM[:], T.AI[:], True, False), (T.DB2[:, 0:8], T.KH[:, c], T.AI[:], False, True),
+                                              (T.DB2[:, 8:16], T.KH[:, c], T.AI[:], True, True)])
+
+        def courts(X, s):
             a0 = 16 * s + 8 * X
-            V("X16 H%d%d" % (X, s), "FA%d" % X, "tt", T.FA[:, 8 * X:8 * X + 8], T.H5[:, a0:a0 + 8], T.X16[:], AO.add)
-            if s < 4:
-                V("C%d%d" % (X, s + 1), "LC%d%d" % (X, s + 1), "tc", T.LC[:, a0:a0 + 8], T.CB[:, a0:a0 + 8])
+            V("DB1", "LC%d%d" % (X, s + 1), "tc", T.LL[:, 0, a0:a0 + 8], T.DB1[:, 0:8])
 
         def places(X, s):
-            V("FA%d" % X, "LF%d" % X, "tc", T.LF[:, 8 * X:8 * X + 8], T.FA[:, 8 * X:8 * X + 8])
+            a0 = 16 * s + 8 * X
+            V("DB2", "LF%d%d" % (X, s), "tc", T.LL[:, 1:3, a0:a0 + 8], T.DB2[:, 0:16])
 
         def chosen(X, s):
-            f0, w = 256 * (s - 1) + 128 * X, (2 * s - 2 + X) % 4
-            old, ok = (fin[:, 128 * X:128 * X + 128], fk) if s == 1 else (T.FH[:, f0 - 256:f0 - 128], "FH%d%d" % (X, s - 1))
-            out, key = (T.FD[:, 128 * X:128 * X + 128], "FD%d" % X) if s < 4 else (T.FH[:, f0:f0 + 128], "FH%d4" % X)
-            V("LF%d %s " % (X, ok) + " ".join("RG%d%d%s" % (w, j, e) for j in range(4) for e in "VS"), key, "tt", out,
-              T.RG[:, 2048 * w:2048 * w + 2048].indirect(T.LF[:, 8 * X:8 * X + 8]), old, AO.subtract)
+            f0, w, a0 = 512 * s + 256 * X, (2 * s - 2 + X) % 4, 16 * s + 8 * X
+            out, key = (T.FD[:, 128 * X:128 * X + 128], "FD%d" % X) if s < 4 else (T.FH[:, f0:f0 + 256:2], "FH%d4a" % X)
+            V("LF%d%d FH%d%da %s" % (X, s, X, s - 1, got(w, range(4))), key, "tt", out,
+              T.RG[:, 2048 * w:2048 * w + 2048].indirect(T.LL[:, 1, a0:a0 + 8]), T.FH[:, f0 - 512:f0 - 256:2], AO.subtract)
 
         def kept(X, s):
-            f0 = 256 * (s - 1) + 128 * X
-            S("FD%d" % X, "FH%d%d" % (X, s), T.FH[:, f0:f0 + 128], T.FD[:, 128 * X:128 * X + 128], AF.Abs)
+            f0 = 512 * s + 256 * X
+            src, key = (T.FD, "FD%d" % X) if s else (fin, fk)
+            for c in range(2):
+                S(key, "FH%d%d%s" % (X, s, "ab"[c]), T.FH[:, f0 + c:f0 + 256:2], src[:, 128 * X:128 * X + 128], AF.Abs)
 
         def turn(X, s):
-            f0 = 256 * (s - 1) + 128 * X
-            if "A" in ON_V:
-                turns("FH%d%d" % (X, s), [(T.FTP[:, 0:128], T.FH[:, f0:f0 + 128], T.IDB[:])])
-            else:
-                turns("FD%d" % X, [(T.FTP[:, 0:128], T.FD[:, 128 * X:128 * X + 128], T.IDB[:])])
+            f0 = 512 * s + 256 * X
+            turns("FH%d%da FH%d%db" % (X, s, X, s), "FTP",
+                  [(T.FTP[:, 128 * h:128 * h + 128], T.FH[:, f0 + 128 * h:f0 + 128 * h + 128], T.IDB[:]) for h in range(2)])
 
         def turned(X, s):
-            if "A" in ON_V:
-                V("FTP", "FT%d" % X, "tc", T.FT[:, 128 * X:128 * X + 128], T.FTP[:, 0:128])
+            if "C" in ON_V:
+                V("FTP", "FT%d" % X, "tc", T.FT[:, 256 * X:256 * X + 256], T.FTP[:, 0:256])
             else:
-                S("FTP", "FT%d" % X, T.FT[:, 128 * X:128 * X + 128], T.FTP[:, 0:128], AF.Abs)
+                S("FTP", "FT%d" % X, T.FT[:, 256 * X:256 * X + 256], T.FTP[:, 0:256], AF.Copy)
 
-        def both(k, s):
-            return "%s0%d %s1%d" % (k, s, k, s)
+        def repeat(X, r):
+            p, f0, c0 = slice(64 * (r % 2), 64 * (r % 2) + 64), 32 * (r // 2), 256 * X + 128 * (r // 2)
+            turns("FT%d" % X, "FP%d" % (r % 2), [(T["FP%d" % (r % 2)][:, f0:f0 + 32, q:q + 2], T.FT[p, c0:c0 + 128], T.IDB[p, p])
+                                                 for q in range(0, 16, 2)])
+
         lc = late_constants_v() if t == 0 else []
-        fills = {2: [lambda: V("AUX", "DV0", "ts", T.DV[:, 0:16], T.AUX[:, 0:16], 2.0 ** -16, None, AO.mult)],
-                 3: [lambda: V(suk, both("C", 1), "tc", T.CB[:, 0:16], st[:, 272:288])],
-                 4: [lambda: V(suk, both("H", 0), "tc", T.H5[:, 0:16], st[:, 288:304])],
-                 5: lc[0:1], 6: lc[1:3], 7: lc[3:5]}
+        fills = {5: lc[0:1], 6: lc[1:3], 7: lc[3:4]}
 
-        last = {"M": least, "H": row, "I": place, "J": places, "F": chosen, "K": kept, "T": turn, "A": turned}
+        last = {"M": least, "H": row, "B": court, "L": courts, "J": places, "F": chosen,
+                "D0": lambda X, s: spread(X, 0), "D1": lambda X, s: spread(X, 1), "P0": lambda X, s: route(X, 0), "P1": lambda X, s: route(X, 1)}
+        facts = {"K": kept, "T": turn, "C": turned}
 
         def call(name, n):
             X, s, j = n % 2, n // 2 + 1, int(name[1:] or 0)
-            s0, s1 = SHARE.get(n, SHARE[None])
             if name == "E":
                 entries(X, s)
             elif name in last:
                 if n >= 2:
                     last[name](X, s - 1)
-                    for f in fills[n] if name == "M" else []:
+                    for f in fills.get(n, []) if name == "M" else []:
                         f()
-            elif name == "S":
-                rules("S", n, s0, s1)
-            elif name[0] == "G":
-                rules("V", n, CUTS[j], min(s0, CUTS[j + 1]))
-                rules("V", n, max(s1, CUTS[j]), CUTS[j + 1])
-            elif name[0] in "LP":
-                {"L": less, "P": plus}[name[0]](n, j)
+            elif name in facts:
+                facts[name](X, s - 1)
+            elif name[0] in "GS":
+                rules("V" if name == "G" else "S", n, *shares(n)[name])
+            elif name[0] == "R":
+                repeat(X, j)
+            elif name == "Y":
+                payloads(n)
+            elif name[0] == "N":
+                smaller(n, j)
             else:
-                {"Z": size, "U": sums}[name[0]](X, j)
-        for _, name, n in sorted((at(name, n), name, n) for n in range(8) for name in PHASE):
-            call(name, n)
+                sums(n, name)
+        todo = sorted((at(name, n), name, n) for n in range(8) for name in PHASE)
+
+        def until(place):
+            while todo and todo[0][0] < place:
+                call(*todo.pop(0)[1:])
 
         def miss(i):
             s, j = HITS[i]
@@ -392,9 +418,10 @@ def rank_program(g, core, T, topo):
                              float(ODD[i + 1] - EVEN[i + 1]), float(EVEN[i + 1]), AO.mult, AO.add)
 
         def slot(i):
-            c, k, b = slice(256 * i, 256 * i + 256), str(i), "DB%d DC%d" % (i, i)
-            vl, vk = (T.LE[:, 80:96], "LE") if i == 0 else (T.LV[:, 16 * i - 16:16 * i], "LV")
-            cl, ck = (T.LE[:, 16:32], "LE PFT") if i == 0 else (T.LC[:, 16 * i:16 * i + 16], both("LC", i + 1))
+            c, k, j = slice(256 * i, 256 * i + 256), str(i), (0, 0, 1)[i]
+            b = BANKS[j]
+            vl, vk = (T.LE[:, 80:96], "LE") if i == 0 else (T.LL[:, 2, 16 * i + 16:16 * i + 32], both("LF", i + 1))
+            cl, ck = (T.LE[:, 16:32], "LE PFT") if i == 0 else (T.LL[:, 0, 16 * i:16 * i + 16], both("LC", i + 1))
             out = {"OM" + k: (lambda: V("OHW " + vk, "OM" + k, "tc", T.OM[:, c], T.OHW[:, 0:16].indirect(vl))) if "OM" + k in ON_V else
                              (lambda: S("OHW " + vk, "OM" + k, T.OM[:, c], T.OHW[:, 0:16].indirect(vl), AF.Copy)),
                    "OL" + k: lambda: S("%s %s" % (ck, PFA), "OL" + k, T.OL[:, c], T.PF[:, 0:4864 if i == 0 else 4096].indirect(cl), AF.Copy)}
@@ -402,9 +429,9 @@ def rank_program(g, core, T, topo):
                 out["OC0"] = lambda: S("OM0 ONE", b, bank(0, 256), T.OM[:, c], AF.Identity, scale=-1.0, bias=T.ONE[:, 0:1])
                 out["NP0"] = lambda: V("OL0 " + b, "NP0", "tt", T.NP[:, c], T.OL[:, c], bank(0, 256), AO.mult)
             else:
-                out["OC" + k] = lambda: mms("IDF NB OL%s OM%s" % (k, k), b, [(bank(i, 256), T.NB[:], T.OM[:, c], True, False),
-                                                                             (bank(i, 256), T.IDF[:], T.OL[:, c], False, True)])
-                out["NP" + k] = lambda: S(b, "NP" + k, T.NP[:, c], bank(i, 256), AF.Relu)
+                out["OC" + k] = lambda: mms("IDF NB OL%s OM%s" % (k, k), b, [(bank(j, 256), T.NB[:], T.OM[:, c], True, False),
+                                                                             (bank(j, 256), T.IDF[:], T.OL[:, c], False, True)])
+                out["NP" + k] = lambda: S(b, "NP" + k, T.NP[:, c], bank(j, 256), AF.Relu)
             return out
 
         def decider(h):
@@ -412,19 +439,23 @@ def rank_program(g, core, T, topo):
 
             def new(i):
                 d = slice(256 * i + 128 * h, 256 * i + 128 * h + 128)
-                return lambda: V("KEY%da KEY%db OM%d" % (h, h, i), "BB%d%d" % (i, h), "tt", T.BB[:, d], T["KEY%d" % h][:, 0:128], T.OM[:, d], AO.mult)
+                return lambda: V("KEY%d OM%d" % (h, i), "BB%d%d" % (i, h), "tt", T.BB[:, d], T["KEY%d" % h][:, 0:128], T.OM[:, d], AO.mult)
             out = {"BB%d%d" % (i, h): new(i) for i in range(3)}
             out.update({"OHD%d" % h: lambda: V("OHW LE", "OHD%d" % h, "tc", T.OHD[:, c], T.OHW[:, 0:16].indirect(T.LE[:, 64 + 8 * h:72 + 8 * h])),
                         "SEL%d" % h: lambda: V("OHD%d LE %s" % (h, PFA), "SEL%d" % h, "tt", T.SEL[:, c],
                                                T.PF[:, 0:4096].indirect(T.LE[:, 8 * h:8 * h + 8]), T.OHD[:, c], AO.mult),
-                        "DEC%d" % h: lambda: mms("BO SEL%d" % h, "KEY%da KEY%db" % (h, h), [(T["KEY%d" % h][:, 0:128], T.BO[:], T.SEL[:, c], True, True)])})
+                        "DEC%d" % h: lambda: mms("BO SEL%d" % h, "KEY%d" % h, [(T["KEY%d" % h][:, 0:128], T.BO[:], T.SEL[:, c], True, True)])})
             return out
 
         def finish(name, X):
             return lambda: last[name](X, 4)
 
+        def last_row(X):
+            return lambda: V("DB2", "H%d4" % X, "tc", T.H5[:, 64 + 8 * X:72 + 8 * X], T.DB2[:, 8:16])
+
         def hand_on():
-            S("LO " + " ".join(both("FH", s) for s in range(1, 5)), fok, fo[:], T.FH[:, 0:1024].indirect(T.LO[:]), AF.Abs)
+            S("LO FHT " + " ".join("FH%d%da" % (X, s) for X in range(2) for s in range(1, 5)), fok, fo[:],
+              T.FH[:, 0:2560].indirect(T.LO[:]), AF.Abs)
             if t < 2:
                 send((rank + 1) % nrank, fo[:], T["FIN%d" % (t + 1)][:], "aF%d" % (t + 1), fok)
             else:
@@ -432,26 +463,28 @@ def rank_program(g, core, T, topo):
 
         def closed():
             if t == 0:
-                V("DB3 DC3", "ZA", "tc", T.ZA[:, 0:1], bank(3, 1))
+                V("DB1", "ZA", "tc", T.ZA[:, 0:1], bank(1, 1))
             else:
-                V("DB3 DC3 ZA", "ZA", "tt", T.ZA[:, 0:1], bank(3, 1), T.ZA[:, 0:1], AO.add)
-        H13, CA = [" ".join(both(k, s) for s in ss) for k, ss in (("H", (1, 2, 3)), ("C", (1, 2, 3, 4)))]
+                V("DB1 ZA", "ZA", "tt", T.ZA[:, 0:1], bank(1, 1), T.ZA[:, 0:1], AO.add)
+        H13, CA = [" ".join(both(k, s) for s in ss) for k, ss in (("H", (1, 2, 3)), ("LC", (1, 2, 3, 4)))]
         H4 = both("H", 4)
         end = {
-            "DV": lambda: V(" ".join(both("SC", s) for s in (1, 2, 3)), "DV1", "ts", T.DV[:, 16:64], T.SC[:, 16:816:17], 16, None, AO.arith_shift_right),
-            "AS": lambda: V("DV0 DV1", "AS", "tt", T.AS[:], T.DV[:, 0:48], T.DV[:, 16:64], AO.add),
+            "HA": lambda: V(" ".join(both("LF", s) for s in (1, 2, 3)), H13, "tc", T.H5[:, 16:64], T.LL[:, 2, 16:64]),
+            "SUM": lambda: mms("WB " + " ".join("FH%d%da" % (X, s) for X in range(2) for s in range(4)), "DB0",
+                               [(T.DB0[:, 0:64], T.WB[:, 15 - b:143 - b], T.FH[:, 2 * b:2048:32], b == 0, b == 15) for b in range(16)]),
+            "DV": lambda: V("DB0", "DV", "tc", T.DV[:], T.DB0[:, 0:64]),
+            "AS": lambda: V("DV", "AS", "tt", T.AS[:], T.DV[:, 0:48], T.DV[:, 16:64], AO.add),
             "AZ": lambda: V("AS ZA", "AZ", "ts", T.AZ[:], T.AS[:], T.ZA[:, 0:1] if t else 0.0, None, AO.add),
             "OD": lambda: V("AZ", "OD", "ts", T.OD[:], T.AZ[:], 1, None, AO.bitwise_and),
-            "C16": lambda: V(CA, "C16", "ts", T.C16[:], T.CB[:], 16.0, None, AO.mult),
+            "C16": lambda: V(CA, "C16", "ts", T.C16[:], T.LL[:, 0, 0:64], 16.0, None, AO.mult),
             "C16T": lambda: V("C16 TR", "C16T", "tt", T.C16T[:], T.C16[:], T.TR[:], AO.subtract),
-            "LV": lambda: V(both("H", 2) + " " + both("H", 3), "LV", "tc", T.LV[:], T.H5[:, 32:64]),
             "PPa": lambda: V("C16 " + H13, "PPa", "tt", T.PP[:, 0:48], T.H5[:, 16:64], T.C16[:, 0:48], AO.add),
             "PTa": lambda: V("C16T " + H13, "PTa", "tt", T.PT[:, 0:48], T.H5[:, 16:64], T.C16T[:, 0:48], AO.add),
             "PPb": lambda: V("C16 " + H4, "PPb", "tt", T.PP[:, 48:64], T.H5[:, 64:80], T.C16[:, 48:64], AO.add),
             "PTb": lambda: V("C16T " + H4, "PTb", "tt", T.PT[:, 48:64], T.H5[:, 64:80], T.C16T[:, 48:64], AO.add),
             "CO": lambda: V("NE %s %s" % (" ".join("NE%d" % i for i in range(10)), CDA), "CO", "scan", T.CO[:], T.NE[:], T.CD[:], 0.0, AO.mult, AO.max),
             "CW": lambda: V("CO LW POW", "CW", "tt", T.CW[:], T.CO[:, 0:176].indirect(T.LW[:]), T.POW[:], AO.mult),
-            "FI": lambda: V("CO", "FI", "ts", T.FI[:], T.CO[:, 10::11], 8, 1023, AO.arith_shift_right, AO.bitwise_and),
+            "FI": lambda: V("CO", "FI", "ts", T.FI[:], T.CO[:, 10::11], 7, 7 << 9, AO.arith_shift_right, AO.bitwise_and),
             "FJ": lambda: V("FI XQ", "FJ", "tt", T.FJ[:], T.FI[:], T.XQ[:], AO.add),
             "LO": lambda: V("FJ", "LO", "tc", T.LO[:], T.FJ[:]),
             "FO": hand_on,
@@ -474,25 +507,28 @@ def rank_program(g, core, T, topo):
             end.update(slot(i))
         for X in range(2):
             end.update(decider(X))
-            end.update({name + str(X): finish(name, X) for name in "MHIJF"})
+            end.update({name + str(X): finish(name, X) for name in ("M", "H", "D1", "P1", "J", "F")})
+            end["HR%d" % X] = last_row(X)
         if t < 2:
             end.update({"ZR": lambda: V("DC", "ZR", "red", T.ZR[:, 0:1], T.DC[:], AxisListType.X, AO.add),
-                        "ZP": lambda: mms("ONE ZR", "DB3 DC3", [(bank(3, 1), T.ONE[:], T.ZR[:, 0:1], True, True)]),
-                        "ZA": closed, "LC": lambda: first_courts(t + 1)})
+                        "ZP": lambda: mms("ONE ZR", "DB1", [(bank(1, 1), T.ONE[:], T.ZR[:, 0:1], True, True)]),
+                        "ZA": closed})
+            end.update(first(t + 1))
         for name in END:
-            if name in end:
+            if name[0] == "@":
+                until(float(name[1:]))
+            elif name in end:
                 end[name]()
-        if t < 2:
-            first_facts(T["FIN%d" % (t + 1)], "FIN%d" % (t + 1))
     c0, q = 0, 0
     for pieces in OUT:
         d0, keys = c0, ""
         for n in pieces:
+            b = BANKS[q % 4]
             if q == 0:
-                V(PFA, "DB0", "ts", bank(0, n), T.PF[:, 2048:2048 + n], 4096.0, None, AO.mult)
+                V(PFA, b, "ts", bank(0, n), T.PF[:, 2048:2048 + n], 4096.0, None, AO.mult)
             else:
-                S(PFA, "DB%d" % (q % 4), bank(q % 4, n), T.PF[:, 2048 + c0:2048 + c0 + n], AF.Copy, scale=4096.0)
-            V("DB%d %s" % (q % 4, PFA), "YO%d" % q, "tt", T.YO[:, c0:c0 + n], bank(q % 4, n), T.PF[:, c0:c0 + n], AO.add)
+                S(PFA, b, bank(q % 4, n), T.PF[:, 2048 + c0:2048 + c0 + n], AF.Copy, scale=4096.0)
+            V("%s %s" % (b, PFA), "YO%d" % q, "tt", T.YO[:, c0:c0 + n], bank(q % 4, n), T.PF[:, c0:c0 + n], AO.add)
             c0, q, keys = c0 + n, q + 1, keys + " YO%d" % q
         dma("Y", keys, "yp%d" % q, T.yp[:, d0:c0], T.YO[:, d0:c0])
     for sem in SEMAPHORES:

@@ -3,23 +3,20 @@ import comms_topo
 
 AO = AluOpType
 AF = ActivationFunctionType
-SHARE = {None: (32, 80, 96), 0: (32, 32, 96)}
-PHASE = {"M": -1.15, "H": -1.12, "B": -1.036, "D1": -1.021, "P1": -0.961, "D0": -0.928, "J": -0.853, "P0": -0.789, "L": -0.641, "F": -0.638,
-         "E": -0.596, "K": -0.522, "S1": -0.491, "T": -0.398, "G": -0.285, "C": -0.28, "R1": -0.195, "S0": -0.063, "S2": -0.052, "R0": -0.014,
-         "Y": 0.045, "N1": 0.104, "N0": 0.194, "R3": 0.387, "R2": 0.413, "N3": 0.484, "U": 0.501, "N2": 0.507, "W": 0.799}
-OTHER = {("E", 0): -2.104, ("K", 0): -1.786, ("T", 0): -1.0, ("C", 0): -0.861, ("G", 0): -0.596, ("R1", 0): -0.456, ("N0", 0): 0.012,
-         ("R2", 0): 0.378, ("N3", 0): 0.527, ("U", 0): 0.586, ("W", 0): 0.624, ("K", 1): -1.214, ("T", 1): -0.664, ("C", 1): -0.467,
-         ("R0", 1): -0.033, ("P0", 6): -0.869, ("R1", 6): -0.197, ("N3", 6): 0.677, ("J", 7): -0.784, ("T", 7): -0.287, ("C", 7): -0.215,
-         ("R1", 7): -0.189, ("N1", 7): 0.18, ("N3", 7): 0.564, ("N2", 7): 0.576}
-START = ("L8 IDF IL SRB LR JQ XQ MK SRG WF XM AI KB MS JM TW0 HP0 IDB TW1 OHW KA GU TW2 TW3 SH SL PH3 K0 CB HP1 LW HP2 PH2 HP3 PL0 LC GW "
-         "PL1 HS PH1 WB PH0 PL3 PL2").split()
-END = ("@6.395 C16 @6.446 HA @6.593 SUM N4 @6.750 DV @6.874 AS @6.942 N5 C16T @7.112 M0 N8 H0 @7.291 N9 @7.400 PTa @7.457 D10 P10 "
-       "@7.687 HR0 K0 N6 AZ @9 J0 OL1 OD Y2 Y5 N7 PPa M1 Y7 OM2 H1 D11 Y4 CB P11 F0 OL2 Y1 HR1 J1 Y0 N2 N0 N1 N3 PPb CO F1 CW FI PTb CH DC "
-       "PC PD YY FJ OC2 D1 OM1 VVb OC1 NP1 VVa LO VUb VUa LE OHD0 OHD1 FO SEL0 OM0 SEL1 OL0 LC ZR DEC0 OC0 DEC1 BB00 NP2 BB10 ZP BB01 BB11 "
-       "BB20 NP0 BB21 ZA PUT HS").split()
-ON_V = ("PH3", "C")
+SHARE = {None: (64, 104), 0: (32, 72), 1: (64, 112), 7: (64, 96)}
+PHASE = {"M": -1.34, "B": -1.317, "H": -1.255, "D0": -1.174, "P0": -1.134, "D1": -1.054, "P1": -0.965, "J": -0.942, "L": -0.881, "F": -0.751,
+         "K": -0.722, "E": -0.7, "Y": -0.661, "T": -0.572, "S0": -0.509, "G": -0.482, "C": -0.44, "S1": -0.251, "R0": -0.232, "N0": 0.047,
+         "R1": 0.116, "U": 0.143, "N1": 0.407, "W": 0.536}
+OTHER = {("E", 0): -2.051, ("K", 0): -1.997, ("T", 0): -1.499, ("C", 0): -1.133, ("R1", 0): -0.601, ("S0", 0): -0.096, ("N0", 0): 0.456,
+         ("K", 1): -2.552, ("T", 1): -0.969, ("N0", 1): -0.006, ("W", 6): 0.71, ("T", 7): -0.304, ("C", 7): -0.246, ("N1", 7): 0.16}
+START = ("IDB L8 AI IDF LR WF JQ MK GW SRB XQ KB NI SH TW0 WB SRG MS TW1 JM HP0 KA PH0 PL0 PH1 HP1 TW2 TW3 SL XR PH3 K0 HP2 XM HP3 PL2 HS CB "
+         "PL1 LC PL3 GU HB PH2").split()
+END = ("@6.373 SUM @6.907 HA M0 OM2 H0 CF D10 @7.081 DV @7.348 NP2 P10 AS CT OM1 J0 @9 OD M1 OM40 OF H1 F0 Y2 DF Y1 D11 Q0 P11 Y7 NP1 NE0 OM3 "
+       "NP40 J1 Y5 Y4 Q1 NP3 Y0 NE1 CO ONE OM41 FL2 FL0 FL1 LS NP41 LQ CW SEL0 CH SEL1 F1 PC DEC0 YY VV FO DEC1 OM0 BB2 BB1 BB0 LE NP0 ZR ZP "
+       "PUT ZA").split()
 LOADS = ((0, 1), (1, 2), (2, 3), (3, 4))
 OUT = ((384,), (512,), (512,), (384,), (256,))
+TABLE = {2: 0, 3: 1, 1: 2, 4: 3}
 HITS = [(s, j) for s in (4, 3, 2, 1) for j in range(s)]
 
 F32, BF, I32, U16 = "float32", "bfloat16", "int32", "uint16"
@@ -32,23 +29,20 @@ def _s(name, cols, dtype, where="sbuf"):
 
 for _n, _c, _d in [
         ("R", 4096, BF), ("PF", 4864, F32), ("PK", 2048, I32), ("TW", 2048, F32), ("YO", 2048, F32),
-        ("JI", 256, I32), ("JQ", 256, F32), ("SRI", 256, I32), ("SRB", 256, BF),
-        ("MS", 256, F32), ("JM", 256, F32), ("K0", 16, I32), ("CB", 16, I32),
+        ("JI", 256, I32), ("JQ", 256, F32), ("SRI", 256, I32), ("SRB", 256, BF), ("JM", 256, F32), ("K0", 16, I32), ("CB", 32, I32),
         ("FX0", 256, BF), ("FIN1", 256, BF), ("FIN2", 256, BF), ("FO0", 256, BF), ("FO1", 256, BF), ("FO2", 256, BF),
-        ("ST0", 544, BF), ("ST1", 544, BF), ("ST2", 544, BF),
+        ("ST0", 528, BF), ("ST1", 528, BF), ("ST2", 528, BF), ("LL0", [3, 80], U16), ("LL1", [3, 80], U16), ("LL2", [3, 80], U16),
         ("RG", 8192, BF), ("A", 4096, BF), ("FH", 2560, BF), ("FT", 512, BF), ("FD", 256, BF),
-        ("NU", 256, U16), ("SC", 256, I32), ("HC", 32, I32), ("KC", 256, F32), ("KH", 256, BF), ("LL", [3, 80], U16), ("H5", 80, I32),
-        ("DV", 64, F32), ("AS", 48, F32), ("AZ", 48, I32), ("OD", 48, I32), ("C16", 64, F32), ("C16T", 64, F32),
-        ("NE", 176, F32), ("CD", 176, F32), ("CO", 176, I32), ("CW", 64, I32), ("FJ", 16, F32),
-        ("CH", 64, I32), ("DC", 64, I32), ("PP", 64, F32), ("PT", 64, F32), ("PC", 64, F32), ("PD", 64, F32), ("D1", 32, F32),
-        ("YY", 48, F32), ("VV", 64, I32), ("VU", 96, I32), ("LE", 96, U16), ("FI", 16, I32), ("LO", 16, U16),
-        ("OHD", 256, F32), ("SEL", 256, F32), ("OL", 768, F32), ("OM", 768, BF), ("NP", 768, F32), ("BB", 768, F32),
-        ("ZR", 1, F32), ("ZA", 1, F32),
+        ("NU", 256, U16), ("SC", 256, I32), ("HC", 32, I32), ("KC", 256, F32), ("KH", 256, BF), ("H5", 48, BF),
+        ("DV", 48, F32), ("AS", 48, I32), ("OD", 48, I32), ("OF", 48, F32), ("CC", 64, F32), ("CT", 64, F32),
+        ("NE", 176, F32), ("CD", 176, F32), ("CO", 176, I32), ("CW", 80, I32), ("CH", 80, I32), ("FL", 48, I32), ("LS", 48, F32), ("LQ", 48, U16),
+        ("PC", 64, F32), ("YY", 48, F32), ("VV", 48, F32), ("LE", 48, U16),
+        ("SEL", 256, F32), ("OM", 1280, BF), ("NP", 1280, F32), ("BB", 768, F32), ("ZR", 1, F32), ("ZA", 1, F32),
         ("IM", 160, F32), ("IG", 128, F32), ("IB", 128, F32), ("IPI", 2, I32), ("IQI", 4, I32), ("CF", 8, F32), ("RS", 128, F32),
-        ("IDB", 128, BF), ("IDF", 128, F32), ("NB", 128, BF), ("WB", 144, BF), ("WF", 144, F32), ("BO", 128, F32), ("ONE", 128, F32),
+        ("IDB", 128, BF), ("IDF", 128, F32), ("NI", 128, BF), ("WB", 144, BF), ("WF", 144, F32), ("BO", 128, F32), ("ONE", 128, F32), ("ONB", 256, BF),
         ("GU", 8, BF), ("GW", 8, BF), ("AI", 8, BF), ("MK", 128, F32), ("XM", 128, BF), ("LR", 8, U16),
-        ("L8", 128, BF), ("MG", 8, F32), ("OHW", 24, F32), ("IA", 16, F32), ("XQ", 16, F32), ("BI", 2, F32),
-        ("POW", 64, F32), ("IL", 4, F32), ("LW", 4, U16), ("TRI", 64, F32), ("TR", 64, F32)]:
+        ("L8", 128, BF), ("MG", 8, F32), ("OHW", 24, F32), ("IA", 32, F32), ("XQ", 48, F32), ("BI", 2, F32), ("YB", 11, F32),
+        ("POW", 80, F32), ("IL", 6, F32), ("LW", 6, U16), ("TRI", 64, F32), ("TR", 64, F32)]:
     _s(_n, _c, _d)
 for _n in ["DB0", "DB1", "DB2", "KEY0", "KEY1"]:
     _s(_n, 512, F32, "psum")
@@ -56,7 +50,7 @@ _s("FTP", 1024, BF, "psum")
 for _n in ["FP0", "FP1"]:
     _s(_n, [64, 16], BF, "psum")
 
-SEMAPHORES = ["sv", "ss", "sp", "sg", "aS1", "aS2", "aF1", "aF2", "ls"] + ["d%d" % i for i in range(16)]
+SEMAPHORES = ["sv", "ss", "sp", "sg", "aS1", "aS2", "aF1", "aF2", "aL1", "aL2", "ls"] + ["d%d" % i for i in range(16)]
 
 
 def at(name, n):
@@ -64,15 +58,16 @@ def at(name, n):
 
 
 def shares(n):
-    c0, c1, c2 = SHARE.get(n, SHARE[None])
-    return {"S0": (0, c0), "S1": (c0, c1), "G": (c1, c2), "S2": (c2, 128)}
+    c0, c1 = SHARE.get(n, SHARE[None])
+    return {"S0": (0, c0), "S1": (c0, c1), "G": (c1, 128)}
 
 
 def codes(odd):
-    out = [(4 << 16) + (11 << 20)]
+    out = [(3 << 13) + (11 << 17)]
     for i, (s, j) in enumerate(HITS):
         d = s if odd else j + 1
-        out.append(sum(8 >> (u - 1) for u in range(j + 1, s + 1) if u != d) + (128 >> (d - 1)) + (s << 16) + ((10 - i) << 20))
+        ch = sum(8 >> (u - 1) for u in range(j + 1, s + 1) if u != d)
+        out.append(ch + 16 + (TABLE[d] << 8) + (TABLE[4 if ch & 1 else 1] << 10) + (s - 1 << 13) + ((10 - i) << 17))
     return out
 
 
@@ -84,10 +79,6 @@ def rank_program(g, core, T, topo):
     ENG = {"V": (g.vector, "sv"), "S": (g.scalar, "ss"), "P": (g.tensor, "sp"), "G": (g, "sg"), "Y": (g.sync, None)}
     cnt = {s: 0 for s in SEMAPHORES}
     waited, Wr, Rd, ndma = {}, {}, {}, [0]
-    BANKS = ("DB0", "DB1", "DB2", "KEY1", "KEY0")
-
-    def bank(j, n=512):
-        return T[BANKS[j]][:, 0:n]
 
     def need(e, sem, val):
         if waited.get((e, sem), 0) < val:
@@ -176,8 +167,8 @@ def rank_program(g, core, T, topo):
     run("G", "", "IPI", "iota", T.IPI[:], [[0, 2]], 0, 1)
     iota("IM", T.IM[:], [[1, 160]], 0)
     iota("IG", T.IG[:], [[1, 8], [0, 16]], 0)
-    iota("IA", T.IA[:], [[32, 16]], 0)
     iota("IB", T.IB[:], [[0, 8], [1, 16]], 0)
+    iota("IA", T.IA[:], [[0, 2], [16, 16]], 0)
     iota("RS", T.RS[:], [[0, 128]], 1 - 2 ** 24)
     iota("RS", T.RS[:, 0::16], [[0, 8]], 2 ** 24 - 1)
     CUT, BIG = 4096.0 * 2047 + 2047.5, 1.5 * 2.0 ** 35
@@ -185,13 +176,12 @@ def rank_program(g, core, T, topo):
     V("", "BI1", "memset", T.BI[:, 1:2], 4096.0 * 2047 - BIG)
     V("IPI", "IQ0", "ts", T.IQI[:, 0:2], T.IPI[:], 15, None, AO.bitwise_and)
     V("IPI", "IQ1", "ts", T.IQI[:, 2:4], T.IPI[:], 4, None, AO.arith_shift_right)
-    V("IQ0", "CF5", "ts", T.CF[:, 5:6], T.IQI[:, 0:1], 4096.0, None, AO.mult)
+    V("IQ0", "CF4", "ts", T.CF[:, 4:5], T.IQI[:, 0:1], 4096.0, None, AO.mult)
     V("IPI", "CF0", "tc", T.CF[:, 0:1], T.IPI[:, 0:1])
     V("IQ0 IQ1", "CF1", "tc", T.CF[:, 1:3], T.IQI[:, 0:4:2])
-    V("IQ0", "CF3", "ts", T.CF[:, 3:4], T.IQI[:, 0:1], 2.0, None, AO.mult)
-    V("IQ1", "CF4", "ts", T.CF[:, 4:5], T.IQI[:, 2:3], 16.0, 15.0, AO.mult, AO.add)
-    V("IPI", "CF6", "ts", T.CF[:, 6:7], T.IPI[:, 0:1], 16.0, None, AO.mult)
-    p_c, q_c, g_c, r_c, e_c, k_c, x_c = [T.CF[:, i:i + 1] for i in range(7)]
+    V("IQ1", "CF3", "ts", T.CF[:, 3:4], T.IQI[:, 2:3], 16.0, 15.0, AO.mult, AO.add)
+    V("IPI", "CF5", "ts", T.CF[:, 5:6], T.IPI[:, 0:1], 16.0, None, AO.mult)
+    p_c, q_c, g_c, e_c, k_c, x_c = [T.CF[:, i:i + 1] for i in range(6)]
     V("IM CF1", "MG", "ts", T.MG[:], T.IM[:, 0:8], g_c, None, AO.is_equal)
 
     EVEN, ODD = codes(0), codes(1)
@@ -202,116 +192,118 @@ def rank_program(g, core, T, topo):
         iota("TRIa", T.TRI[:, 0:48], [[16, 48]], 4096)
         iota("TRIb", T.TRI[:, 48:64], [[16, 16]], 4096)
         iota("ONE", T.ONE[:], [[0, 128]], 1)
-        iota("NE", T.NE[:, 0::11], [[0, 16]], 0)
-        for u in range(4):
-            iota("POW", T.POW[:, 16 * u:16 * u + 16], [[0, 16]], 2 ** u)
+        iota("ONB", T.ONB[:], [[0, 256]], 1)
+        for u, m in enumerate((2, 4, 8, 16, 1)):
+            iota("POW", T.POW[:, 16 * u:16 * u + 16], [[0, 16]], m)
         for i in range(11):
             if EVEN[i] == ODD[i]:
                 iota("CD%d" % i, T.CD[:, i::11], [[0, 16]], EVEN[i])
+            else:
+                iota("YB", T.YB[:, i:i + 1], [[0, 1]], EVEN[i])
 
     def late_constants_v():
-        return [lambda: V("TRIa TRIb CF1", "TR", "ts", T.TR[:], T.TRI[:], q_c, 16.0, AO.add, AO.mult),
+        return [lambda: V("IM CF1", "OHW", "ts", T.OHW[:], T.IM[:, 0:24], q_c, 4096.0, AO.is_equal, AO.mult),
+                lambda: V("IM CF1", "IL", "ts", T.IL[:], T.IM[:, 0:6], 0.0, q_c, AO.mult, AO.add),
+                lambda: V("IL", "LW", "ts", T.LW[:], T.IL[:], 11.0, 10.0, AO.mult, AO.add),
+                lambda: V("TRIa TRIb CF1", "TR", "ts", T.TR[:], T.TRI[:], q_c, None, AO.add),
                 lambda: V("TR", "YY", "tc", T.YY[:], T.TR[:, 0:48]),
-                lambda: V("IDB", "NB", "ts", T.NB[:], T.IDB[:], -4096.0, None, AO.mult),
-                lambda: V("IG CF1", "BO", "ts", T.BO[:], T.IG[:], g_c, None, AO.is_equal)]
+                lambda: V("IG CF1", "BO", "ts", T.BO[:], T.IG[:], g_c, -2.0 ** -12, AO.is_equal, AO.mult)]
     CDA = " ".join("CD%d" % i for i in range(11))
     PFA = " ".join("PFH%d PFL%d" % (q, q) for q in range(4))
 
     def both(k, s):
         return "%s0%d %s1%d" % (k, s, k, s)
 
-    def first(t):
-        st = T["ST%d" % t]
-        return {"K0": lambda: V("SH%d SL%d" % (t, t), "K0", "tt", T.K0[:], st[:, 256:272], st[:, 528:544], AO.add),
-                "CB": lambda: V("K0", "CB", "ts", T.CB[:], T.K0[:], 4095, None, AO.bitwise_and),
-                "LC": lambda: V("CB", both("LC", 1), "tc", T.LL[:, 0, 0:16], T.CB[:]),
-                "HS": lambda: V("K0", both("H", 0), "ts", T.H5[:, 0:16], T.K0[:], 12, None, AO.arith_shift_right)}
-
     def unpack(q):
-        c, h, k, j = slice(512 * q, 512 * q + 512), slice(2048 + 512 * q, 2560 + 512 * q), str(q), (q + 3) % 5
+        c, h, k, b = slice(512 * q, 512 * q + 512), slice(2048 + 512 * q, 2560 + 512 * q), str(q), ("KEY1", "KEY0", "DB0", "DB2")[q]
         return {"TW" + k: lambda: V("PK" + k, "TW" + k, "ts", T.TW[:, c], T.PK[:, c], CUT, BIG, AO.subtract, AO.add),
-                "HP" + k: lambda: S("TW%s BI1" % k, BANKS[j], bank(j), T.TW[:, c], AF.Identity, bias=T.BI[:, 1:2]),
+                "HP" + k: lambda: S("TW%s BI1" % k, b, T[b][:], T.TW[:, c], AF.Identity, bias=T.BI[:, 1:2]),
                 "PH" + k: (lambda: V("TW" + k, "PFH" + k, "ts", T.PF[:, h], T.TW[:, c], 2.0 ** -12, 2047 - BIG / 4096, AO.mult, AO.add))
-                if "PH" + k in ON_V else
+                if q == 3 else
                 (lambda: S("TW%s BI0" % k, "PFH" + k, T.PF[:, h], T.TW[:, c], AF.Identity, scale=2.0 ** -12, bias=T.BI[:, 0:1])),
-                "PL" + k: lambda: V("PK%s %s" % (k, BANKS[j]), "PFL" + k, "tt", T.PF[:, c], T.PK[:, c], bank(j), AO.subtract)}
+                "PL" + k: lambda: V("PK%s %s" % (k, b), "PFL" + k, "tt", T.PF[:, c], T.PK[:, c], T[b][:], AO.subtract)}
 
     start = {
-        "WF": lambda: V("IM CF4", "WF", "ts", T.WF[:, 0:143], T.IM[:, 0:143], e_c, None, AO.is_equal),
-        "OHW": lambda: V("IM CF1", "OHW", "ts", T.OHW[:], T.IM[:, 0:24], q_c, None, AO.is_equal),
+        "WF": lambda: V("IM CF3", "WF", "ts", T.WF[:, 0:143], T.IM[:, 0:143], e_c, None, AO.is_equal),
         "L8": lambda: V("IG CF0", "L8", "ts", T.L8[0:8, :], T.IG[0:8, :], T.CF[0:8, 0:1], None, AO.is_equal),
         "WB": lambda: S("WF", "WB", T.WB[:, 0:143], T.WF[:, 0:143], AF.Copy),
         "GU": lambda: S("MG", "GU", T.GU[:], T.MG[:], AF.Copy, scale=65536.0),
         "GW": lambda: S("MG", "GW", T.GW[:], T.MG[:], AF.Copy, scale=-131072.0),
         "AI": lambda: S("MG", "AI", T.AI[:], T.MG[:], AF.Copy),
         "IDF": lambda: V("IM CF0", "IDF", "ts", T.IDF[:], T.IM[:, 0:128], p_c, None, AO.is_equal),
+        "IDB": lambda: V("IM CF0", "IDB", "ts", T.IDB[:], T.IM[:, 0:128], p_c, None, AO.is_equal),
+        "NI": lambda: S("IDB", "NI", T.NI[:], T.IDB[:], AF.Copy, scale=-1.0),
         "LR": lambda: V("IM", "LR", "tc", T.LR[:], T.IM[:, 0:8]),
         "MK": lambda: V("IB CF1", "MK", "ts", T.MK[:], T.IB[:], q_c, None, AO.is_equal),
-        "XM": lambda: S("MK CF6", "XM", T.XM[:], T.MK[:], AF.Identity, scale=x_c),
-        "IDB": lambda: V("IM CF0", "IDB", "ts", T.IDB[:], T.IM[:, 0:128], p_c, None, AO.is_equal),
-        "XQ": lambda: S("IA CF3", "XQ", T.XQ[:], T.IA[:], AF.Identity, bias=r_c),
-        "IL": lambda: V("IM CF1", "IL", "ts", T.IL[:], T.IM[:, 0:4], 0.0, q_c, AO.mult, AO.add),
-        "LW": lambda: V("IL", "LW", "ts", T.LW[:], T.IL[:], 11.0, 10.0, AO.mult, AO.add),
-        "JQ": lambda: V("JI CF5", "JQ", "ts", T.JQ[:], T.JI[:], k_c, None, AO.add),
+        "XM": lambda: S("MK CF5", "XM", T.XM[:], T.MK[:], AF.Identity, scale=x_c),
+        "XQ": lambda: S("IA CF1", "XQ", T.XQ[:, 0:32], T.IA[:], AF.Identity, bias=q_c),
+        "XR": lambda: S("XQ", "XR", T.XQ[:, 32:48], T.XQ[:, 0:16], AF.Copy, scale=2.0),
+        "JQ": lambda: V("JI CF4", "JQ", "ts", T.JQ[:], T.JI[:], k_c, None, AO.add),
         "SRB": lambda: V("SRI", "SRB", "tc", T.SRB[0:8, :], T.SRI[0:8, :]),
         "SRG": lambda: mms("L8 SRB", "DB1", [(T.DB1[:, 0:256], T.L8[0:8, :], T.SRB[0:8, :], True, True)]),
-        "MS": lambda: V("DB1 CF1", "MS", "ts", T.MS[:], T.DB1[:, 0:256], q_c, None, AO.is_equal),
-        "JM": lambda: V("MS JQ", "JM", "tt", T.JM[:], T.MS[:], T.JQ[:], AO.mult),
-        "KA": lambda: mms("WF JM", "DB2",
-                          [(T.DB2[:, 256:272], T.WF[:, 15 - b:143 - b], T.JM[:, b::16], b == 0, b == 15) for b in range(16)]),
+        "MS": lambda: V("DB1 CF1", "DB0", "ts", T.DB0[:, 0:256], T.DB1[:, 0:256], q_c, None, AO.is_equal),
+        "JM": lambda: V("DB0 JQ", "JM", "tt", T.JM[:], T.DB0[:, 0:256], T.JQ[:], AO.mult),
+        "KA": lambda: mms("WF JM", "DB1",
+                          [(T.DB1[:, 0:16], T.WF[:, 15 - b:143 - b], T.JM[:, b::16], b == 0, b == 15) for b in range(16)]),
+        "K0": lambda: V("DB1", "K0", "tc", T.K0[:], T.DB1[:, 0:16]),
+        "CB": lambda: V("K0", "CB", "ts", T.CB[:, 0:16], T.K0[:], 4095, None, AO.bitwise_and),
+        "LC": lambda: V("CB", "LS0", "tc", T.LL0[:, 0, 0:16], T.CB[:, 0:16]),
+        "HS": lambda: V("K0", "HS", "ts", T.CB[:, 16:32], T.K0[:], 12, None, AO.arith_shift_right),
+        "HB": lambda: V("HS", "SR0", "tc", T.ST0[:, 512:528], T.CB[:, 16:32]),
         "KB": lambda: mms("JQ IDF", "DB2", [(T.DB2[:, 128 * X:128 * X + 128], T.JQ[:, 128 * X:128 * X + 128], T.IDF[:], True, True) for X in range(2)]),
-        "SH": lambda: S("DB2", "SH0", T.ST0[:, 0:272], T.DB2[:, 0:272], AF.Copy),
-        "SL": lambda: V("DB2 SH0", "SL0", "tt", T.ST0[:, 272:544], T.DB2[:, 0:272], T.ST0[:, 0:272], AO.subtract)}
-    start.update(first(0))
+        "SH": lambda: S("DB2", "SH0", T.ST0[:, 0:256], T.DB2[:, 0:256], AF.Copy),
+        "SL": lambda: V("DB2 SH0", "SL0", "tt", T.ST0[:, 256:512], T.DB2[:, 0:256], T.ST0[:, 0:256], AO.subtract)}
     for q in range(4):
         start.update(unpack(q))
     for name in START:
         start[name]()
-    send((rank + 1) % nrank, T.ST0[:], T.ST1[:], "aS1", "SH0 SL0")
-    send((rank + 2) % nrank, T.ST0[:], T.ST2[:], "aS2", "SH0 SL0")
+    for t in (1, 2):
+        send((rank + t) % nrank, T.ST0[:], T["ST%d" % t][:], "aS%d" % t, "SH0 SL0 SR0 R")
+        send((rank + t) % nrank, T.LL0[:, 0, 0:16], T["LL%d" % t][:, 0, 0:16], "aL%d" % t, "LS0")
     late_constants()
     for t in (1, 2):
-        Wr["SH%d" % t], Wr["SL%d" % t], Wr["FIN%d" % t] = {"aS%d" % t: narr}, {"aS%d" % t: narr}, {"aF%d" % t: narr}
+        for key, sem in (("SH", "aS"), ("SL", "aS"), ("SR", "aS"), ("FIN", "aF"), ("LS", "aL")):
+            Wr["%s%d" % (key, t)] = {"%s%d" % (sem, t): narr}
 
     for t in range(3):
         st, stk = T["ST%d" % t], "SH%d SL%d" % (t, t)
         fin, fk = (T.FX0, "FX0") if t == 0 else (T["FIN%d" % t], "FIN%d" % t)
-        fo, fok = T["FO%d" % t], "FO%d" % t
+        fo, fok, ll = T["FO%d" % t], "FO%d" % t, T["LL%d" % t]
+
+        def lc(X, s):
+            return "LC%d%d" % (X, s) if s > 1 else "LS%d" % t
 
         def entries(X, s):
             l0 = 16 * s - 16 + 8 * X
-            V("%s LC%d%d" % (PFA, X, s), "NU%d" % X, "tc", T.NU[:, 128 * X:128 * X + 128], T.PF[:, 0:4096].indirect(T.LL[:, 0, l0:l0 + 8]))
+            V("%s %s" % (PFA, lc(X, s)), "NU%d" % X, "tc", T.NU[:, 128 * X:128 * X + 128], T.PF[:, 0:4096].indirect(ll[:, 0, l0:l0 + 8]))
 
-        def got(w, rows):
-            return " ".join("RG%d%d%s" % (w, r, e) for r in rows for e in "VS")
+        def got(w, halves):
+            return " ".join("RG%d%d%s" % (w, h, e) for h in halves for e in ("G", "S0", "S1"))
 
-        def rules(e, n, x0, x1):
-            if x0 >= x1:
-                return
+        def rules(name, n):
+            x0, x1 = shares(n)[name]
             X, w = n % 2, n % 4
-            wr = " ".join("RG%d%d%s" % (w, r, e) for r in range(x0 // 32, (x1 + 31) // 32))
+            wr = " ".join("RG%d%d%s" % (w, h, name) for h in range(x0 // 64, (x1 + 63) // 64))
             out, src = T.RG[:, 2048 * w + 16 * x0:2048 * w + 16 * x1], T.R[:, 0:4096].indirect(T.NU[:, 128 * X + x0:128 * X + x1])
-            if e == "V":
+            if name == "G":
                 V("R NU%d" % X, wr, "tc", out, src)
             else:
                 S("R NU%d" % X, wr, out, src, AF.Copy)
 
-        def smaller(n, r):
-            X, w, f0 = n % 2, n % 4, 32 * (r // 2)
-            a0, r0 = 2048 * X + 512 * r, 2048 * w + 512 * r
-            V("FP%d %s" % (r % 2, got(w, [r])), "A%d%d" % (X, r), "tt", T.A[:, a0:a0 + 512], T.RG[:, r0:r0 + 512],
-              T["FP%d" % (r % 2)][:, f0:f0 + 32, :], AO.min)
+        def smaller(n, h):
+            X, w = n % 2, n % 4
+            a0, r0 = 2048 * X + 1024 * h, 2048 * w + 1024 * h
+            V("FP%d %s" % (h, got(w, [h])), "A%d%d" % (X, h), "tt", T.A[:, a0:a0 + 1024], T.RG[:, r0:r0 + 1024], T["FP%d" % h][:, :, :], AO.min)
 
         def payloads(n):
             X = n % 2
             k = T["KEY%d" % X][:, 0:128]
             mms("IDB " + stk, "KEY%d" % X, [(k, T.IDB[:], st[:, 128 * X:128 * X + 128], True, False),
-                                            (k, T.IDB[:], st[:, 272 + 128 * X:400 + 128 * X], False, False)])
+                                            (k, T.IDB[:], st[:, 256 + 128 * X:384 + 128 * X], False, False)])
 
         def sums(n, of):
             X, w = n % 2, n % 4
-            rd, src, c0, m = (("GU " + got(w, range(4)), T.RG, 2048 * w, T.GU) if of == "U" else
-                              ("GW " + " ".join("A%d%d" % (X, r) for r in range(4)), T.A, 2048 * X, T.GW))
+            rd, src, c0, m = ("GU " + got(w, (0, 1)), T.RG, 2048 * w, T.GU) if of == "U" else ("GW A%d0 A%d1" % (X, X), T.A, 2048 * X, T.GW)
             mms(rd, "KEY%d" % X, [(T["KEY%d" % X][:, k:128:16], src[:, c0 + k:c0 + 2048:16], m[:], False, of == "W" and k == 15) for k in range(16)])
 
         def least(X, s):
@@ -339,17 +331,17 @@ def rank_program(g, core, T, topo):
 
         def courts(X, s):
             a0 = 16 * s + 8 * X
-            V("DB1", "LC%d%d" % (X, s + 1), "tc", T.LL[:, 0, a0:a0 + 8], T.DB1[:, 0:8])
+            V("DB1", lc(X, s + 1), "tc", ll[:, 0, a0:a0 + 8], T.DB1[:, 0:8])
 
         def places(X, s):
             a0 = 16 * s + 8 * X
-            V("DB2", "LF%d%d" % (X, s), "tc", T.LL[:, 1:3, a0:a0 + 8], T.DB2[:, 0:16])
+            V("DB2", "LF%d%d" % (X, s), "tc", ll[:, 1:3, a0:a0 + 8], T.DB2[:, 0:16])
 
         def chosen(X, s):
             f0, w, a0 = 512 * s + 256 * X, (2 * s - 2 + X) % 4, 16 * s + 8 * X
             out, key = (T.FD[:, 128 * X:128 * X + 128], "FD%d" % X) if s < 4 else (T.FH[:, f0:f0 + 256:2], "FH%d4a" % X)
-            V("LF%d%d FH%d%da %s" % (X, s, X, s - 1, got(w, range(4))), key, "tt", out,
-              T.RG[:, 2048 * w:2048 * w + 2048].indirect(T.LL[:, 1, a0:a0 + 8]), T.FH[:, f0 - 512:f0 - 256:2], AO.subtract)
+            V("LF%d%d FH%d%da %s" % (X, s, X, s - 1, got(w, (0, 1))), key, "tt", out,
+              T.RG[:, 2048 * w:2048 * w + 2048].indirect(ll[:, 1, a0:a0 + 8]), T.FH[:, f0 - 512:f0 - 256:2], AO.subtract)
 
         def kept(X, s):
             f0 = 512 * s + 256 * X
@@ -363,18 +355,13 @@ def rank_program(g, core, T, topo):
                   [(T.FTP[:, 128 * h:128 * h + 128], T.FH[:, f0 + 128 * h:f0 + 128 * h + 128], T.IDB[:]) for h in range(2)])
 
         def turned(X, s):
-            if "C" in ON_V:
-                V("FTP", "FT%d" % X, "tc", T.FT[:, 256 * X:256 * X + 256], T.FTP[:, 0:256])
-            else:
-                S("FTP", "FT%d" % X, T.FT[:, 256 * X:256 * X + 256], T.FTP[:, 0:256], AF.Copy)
+            V("FTP", "FT%d" % X, "tc", T.FT[:, 256 * X:256 * X + 256], T.FTP[:, 0:256])
 
-        def repeat(X, r):
-            p, f0, c0 = slice(64 * (r % 2), 64 * (r % 2) + 64), 32 * (r // 2), 256 * X + 128 * (r // 2)
-            turns("FT%d" % X, "FP%d" % (r % 2), [(T["FP%d" % (r % 2)][:, f0:f0 + 32, q:q + 2], T.FT[p, c0:c0 + 128], T.IDB[p, p])
-                                                 for q in range(0, 16, 2)])
+        def repeat(X, h):
+            turns("FT%d" % X, "FP%d" % h, [(T["FP%d" % h][:, :, q:q + 2], T.FT[:, 256 * X + 128 * h:256 * X + 128 * h + 128], T.IDB[:])
+                                           for q in range(0, 16, 2)])
 
-        lc = late_constants_v() if t == 0 else []
-        fills = {5: lc[0:1], 6: lc[1:3], 7: lc[3:4]}
+        lv = late_constants_v() if t == 0 else []
 
         last = {"M": least, "H": row, "B": court, "L": courts, "J": places, "F": chosen,
                 "D0": lambda X, s: spread(X, 0), "D1": lambda X, s: spread(X, 1), "P0": lambda X, s: route(X, 0), "P1": lambda X, s: route(X, 1)}
@@ -387,12 +374,12 @@ def rank_program(g, core, T, topo):
             elif name in last:
                 if n >= 2:
                     last[name](X, s - 1)
-                    for f in fills.get(n, []) if name == "M" else []:
-                        f()
+                    if name == "M" and lv:
+                        lv.pop(0)()
             elif name in facts:
                 facts[name](X, s - 1)
             elif name[0] in "GS":
-                rules("V" if name == "G" else "S", n, *shares(n)[name])
+                rules(name, n)
             elif name[0] == "R":
                 repeat(X, j)
             elif name == "Y":
@@ -407,55 +394,51 @@ def rank_program(g, core, T, topo):
             while todo and todo[0][0] < place:
                 call(*todo.pop(0)[1:])
 
-        def miss(i):
-            s, j = HITS[i]
-            return lambda: V("NE %s %s" % (both("H", s), both("H", j)), "NE%d" % i, "tt", T.NE[:, i + 1::11],
-                             T.H5[:, 16 * j:16 * j + 16], T.H5[:, 16 * s:16 * s + 16], AO.not_equal)
+        def rows(s, x0, n):
+            return st[:, 512 + x0:512 + x0 + n] if s == 0 else T.H5[:, 16 * s - 16 + x0:16 * s - 16 + x0 + n]
+
+        def apart():
+            mms("IDB NI HA SR%d" % t, "DB0", [(T.DB0[:, i:176:11], m, rows(u, 0, 16), k == 0, k == 1)
+                                              for i, (s, j) in enumerate([(0, 0)] + HITS) if s < 4
+                                              for k, (m, u) in enumerate(((T.IDB[:], s), (T.NI[:], j)))])
+
+        def apart4(X):
+            return lambda: mms("AI NI HA SR%d KH%d" % (t, X), "DB0",
+                               [(T.DB0[:, 88 * X + j + 1:88 * X + 88:11], m, r, k == 0, k == 1) for j in range(4)
+                                for k, (m, r) in enumerate(((T.KH[:, 128 * X:128 * X + 128], T.AI[:]), (T.NI[:], rows(j, 8 * X, 8))))])
+
+        def miss(X):
+            return lambda: S("DB0", "NE%d" % X, T.NE[:, 88 * X:88 * X + 88], T.DB0[:, 88 * X:88 * X + 88], AF.Abs, scale=2.0 ** 22)
 
         def meaning(i):
             j = HITS[i][1]
-            return lambda: V("OD", "CD%d" % (i + 1), "ts", T.CD[:, i + 1::11], T.OD[:, 16 * j:16 * j + 16],
-                             float(ODD[i + 1] - EVEN[i + 1]), float(EVEN[i + 1]), AO.mult, AO.add)
+            return lambda: S("OF YB", "CD%d" % (i + 1), T.CD[:, i + 1::11], T.OF[:, 16 * j:16 * j + 16], AF.Identity,
+                             scale=float(ODD[i + 1] - EVEN[i + 1]), bias=T.YB[:, i + 1:i + 2])
 
-        def slot(i):
-            c, k, j = slice(256 * i, 256 * i + 256), str(i), (0, 0, 1)[i]
-            b = BANKS[j]
-            vl, vk = (T.LE[:, 80:96], "LE") if i == 0 else (T.LL[:, 2, 16 * i + 16:16 * i + 32], both("LF", i + 1))
-            cl, ck = (T.LE[:, 16:32], "LE PFT") if i == 0 else (T.LL[:, 0, 16 * i:16 * i + 16], both("LC", i + 1))
-            out = {"OM" + k: (lambda: V("OHW " + vk, "OM" + k, "tc", T.OM[:, c], T.OHW[:, 0:16].indirect(vl))) if "OM" + k in ON_V else
-                             (lambda: S("OHW " + vk, "OM" + k, T.OM[:, c], T.OHW[:, 0:16].indirect(vl), AF.Copy)),
-                   "OL" + k: lambda: S("%s %s" % (ck, PFA), "OL" + k, T.OL[:, c], T.PF[:, 0:4864 if i == 0 else 4096].indirect(cl), AF.Copy)}
-            if i == 0:
-                out["OC0"] = lambda: S("OM0 ONE", b, bank(0, 256), T.OM[:, c], AF.Identity, scale=-1.0, bias=T.ONE[:, 0:1])
-                out["NP0"] = lambda: V("OL0 " + b, "NP0", "tt", T.NP[:, c], T.OL[:, c], bank(0, 256), AO.mult)
-            else:
-                out["OC" + k] = lambda: mms("IDF NB OL%s OM%s" % (k, k), b, [(bank(j, 256), T.NB[:], T.OM[:, c], True, False),
-                                                                             (bank(j, 256), T.IDF[:], T.OL[:, c], False, True)])
-                out["NP" + k] = lambda: S(b, "NP" + k, T.NP[:, c], bank(j, 256), AF.Relu)
-            return out
+        def column(u, k, x0, n):
+            c0, l0 = 256 * TABLE[u] + 256 + x0, 16 * u + x0 // 16
+            c = slice(c0, c0 + n)
+            return {"OM" + k: lambda: S("OHW " + (both("LF", u) if u < 4 else "LF%s4" % k[1]), "OM" + k, T.OM[:, c],
+                                        T.OHW[:, 0:16].indirect(ll[:, 2, l0:l0 + n // 16]), AF.Copy),
+                    "NP" + k: lambda: V("OM%s %s %s %s" % (k, lc(0, u), lc(1, u), PFA), "NP" + k, "tt", T.NP[:, c],
+                                        T.PF[:, 0:4096].indirect(ll[:, 0, l0 - 16:l0 - 16 + n // 16]), T.OM[:, c], AO.subtract)}
 
         def decider(h):
             c = slice(128 * h, 128 * h + 128)
+            return {"SEL%d" % h: lambda: S("LQ " + NPA, "SEL%d" % h, T.SEL[:, c], T.NP[:, 256:1280].indirect(T.LQ[:, 8 * h:8 * h + 8]),
+                                           AF.Relu, scale=-1.0),
+                    "DEC%d" % h: lambda: mms("BO SEL%d" % h, "KEY1", [(T.KEY1[:, c], T.BO[:], T.SEL[:, c], False, h == 1)])}
 
-            def new(i):
-                d = slice(256 * i + 128 * h, 256 * i + 128 * h + 128)
-                return lambda: V("KEY%d OM%d" % (h, i), "BB%d%d" % (i, h), "tt", T.BB[:, d], T["KEY%d" % h][:, 0:128], T.OM[:, d], AO.mult)
-            out = {"BB%d%d" % (i, h): new(i) for i in range(3)}
-            out.update({"OHD%d" % h: lambda: V("OHW LE", "OHD%d" % h, "tc", T.OHD[:, c], T.OHW[:, 0:16].indirect(T.LE[:, 64 + 8 * h:72 + 8 * h])),
-                        "SEL%d" % h: lambda: V("OHD%d LE %s" % (h, PFA), "SEL%d" % h, "tt", T.SEL[:, c],
-                                               T.PF[:, 0:4096].indirect(T.LE[:, 8 * h:8 * h + 8]), T.OHD[:, c], AO.mult),
-                        "DEC%d" % h: lambda: mms("BO SEL%d" % h, "KEY%d" % h, [(T["KEY%d" % h][:, 0:128], T.BO[:], T.SEL[:, c], True, True)])})
-            return out
+        def new(i):
+            d = slice(256 * i, 256 * i + 256)
+            return lambda: V("KEY1 OM%d" % (i and i + 1), "BB%d" % i, "tt", T.BB[:, d], T.KEY1[:, 0:256], T.OM[:, d], AO.mult)
 
         def finish(name, X):
             return lambda: last[name](X, 4)
 
-        def last_row(X):
-            return lambda: V("DB2", "H%d4" % X, "tc", T.H5[:, 64 + 8 * X:72 + 8 * X], T.DB2[:, 8:16])
-
         def hand_on():
-            S("LO FHT " + " ".join("FH%d%da" % (X, s) for X in range(2) for s in range(1, 5)), fok, fo[:],
-              T.FH[:, 0:2560].indirect(T.LO[:]), AF.Abs)
+            S("LQ FHT " + " ".join("FH%d%d%s" % (X, s, c) for X in range(2) for s in range(1, 5) for c in "ab"), fok, fo[:],
+              T.FH[:, 512:2560].indirect(T.LQ[:, 32:48]), AF.Abs)
             if t < 2:
                 send((rank + 1) % nrank, fo[:], T["FIN%d" % (t + 1)][:], "aF%d" % (t + 1), fok)
             else:
@@ -463,57 +446,55 @@ def rank_program(g, core, T, topo):
 
         def closed():
             if t == 0:
-                V("DB1", "ZA", "tc", T.ZA[:, 0:1], bank(1, 1))
+                V("DB1", "ZA", "tc", T.ZA[:, 0:1], T.DB1[:, 0:1])
             else:
-                V("DB1 ZA", "ZA", "tt", T.ZA[:, 0:1], bank(1, 1), T.ZA[:, 0:1], AO.add)
-        H13, CA = [" ".join(both(k, s) for s in ss) for k, ss in (("H", (1, 2, 3)), ("LC", (1, 2, 3, 4)))]
-        H4 = both("H", 4)
+                V("DB1 ZA", "ZA", "tt", T.ZA[:, 0:1], T.DB1[:, 0:1], T.ZA[:, 0:1], AO.add)
+        OMA, NPA = "OM1 OM2 OM3 OM40 OM41", "NP1 NP2 NP3 NP40 NP41"
         end = {
-            "HA": lambda: V(" ".join(both("LF", s) for s in (1, 2, 3)), H13, "tc", T.H5[:, 16:64], T.LL[:, 2, 16:64]),
+            "HA": lambda: V(" ".join(both("LF", s) for s in (1, 2, 3)), "HA", "tc", T.H5[:], ll[:, 2, 16:64]),
             "SUM": lambda: mms("WB " + " ".join("FH%d%da" % (X, s) for X in range(2) for s in range(4)), "DB0",
                                [(T.DB0[:, 0:64], T.WB[:, 15 - b:143 - b], T.FH[:, 2 * b:2048:32], b == 0, b == 15) for b in range(16)]),
-            "DV": lambda: V("DB0", "DV", "tc", T.DV[:], T.DB0[:, 0:64]),
-            "AS": lambda: V("DV", "AS", "tt", T.AS[:], T.DV[:, 0:48], T.DV[:, 16:64], AO.add),
-            "AZ": lambda: V("AS ZA", "AZ", "ts", T.AZ[:], T.AS[:], T.ZA[:, 0:1] if t else 0.0, None, AO.add),
-            "OD": lambda: V("AZ", "OD", "ts", T.OD[:], T.AZ[:], 1, None, AO.bitwise_and),
-            "C16": lambda: V(CA, "C16", "ts", T.C16[:], T.LL[:, 0, 0:64], 16.0, None, AO.mult),
-            "C16T": lambda: V("C16 TR", "C16T", "tt", T.C16T[:], T.C16[:], T.TR[:], AO.subtract),
-            "PPa": lambda: V("C16 " + H13, "PPa", "tt", T.PP[:, 0:48], T.H5[:, 16:64], T.C16[:, 0:48], AO.add),
-            "PTa": lambda: V("C16T " + H13, "PTa", "tt", T.PT[:, 0:48], T.H5[:, 16:64], T.C16T[:, 0:48], AO.add),
-            "PPb": lambda: V("C16 " + H4, "PPb", "tt", T.PP[:, 48:64], T.H5[:, 64:80], T.C16[:, 48:64], AO.add),
-            "PTb": lambda: V("C16T " + H4, "PTb", "tt", T.PT[:, 48:64], T.H5[:, 64:80], T.C16T[:, 48:64], AO.add),
-            "CO": lambda: V("NE %s %s" % (" ".join("NE%d" % i for i in range(10)), CDA), "CO", "scan", T.CO[:], T.NE[:], T.CD[:], 0.0, AO.mult, AO.max),
-            "CW": lambda: V("CO LW POW", "CW", "tt", T.CW[:], T.CO[:, 0:176].indirect(T.LW[:]), T.POW[:], AO.mult),
-            "FI": lambda: V("CO", "FI", "ts", T.FI[:], T.CO[:, 10::11], 7, 7 << 9, AO.arith_shift_right, AO.bitwise_and),
-            "FJ": lambda: V("FI XQ", "FJ", "tt", T.FJ[:], T.FI[:], T.XQ[:], AO.add),
-            "LO": lambda: V("FJ", "LO", "tc", T.LO[:], T.FJ[:]),
+            "DV": (lambda: S("DB0 ZA", "DV", T.DV[:], T.DB0[:, 0:48], AF.Identity, bias=T.ZA[:, 0:1])) if t else
+                  (lambda: S("DB0", "DV", T.DV[:], T.DB0[:, 0:48], AF.Copy)),
+            "AS": lambda: V("DV DB0", "AS", "tt", T.AS[:], T.DV[:], T.DB0[:, 16:64], AO.add),
+            "OD": lambda: V("AS", "OD", "ts", T.OD[:], T.AS[:], 1, None, AO.bitwise_and),
+            "OF": lambda: V("OD", "OF", "tc", T.OF[:], T.OD[:]),
+            "DF": apart,
+            "CF": lambda: V(" ".join(lc(X, s) for X in range(2) for s in range(1, 5)), "CC", "tc", T.CC[:], ll[:, 0, 0:64]),
+            "CT": lambda: V("CC TR", "CT", "tt", T.CT[:], T.CC[:], T.TR[:], AO.subtract),
+            "CO": lambda: V("NE0 NE1 " + CDA, "CO", "scan", T.CO[:], T.NE[:], T.CD[:], 0.0, AO.min, AO.max),
+            "FL0": lambda: V("CO", "FL0", "ts", T.FL[:, 0:16], T.CO[:, 10::11], 3 << 8, None, AO.bitwise_and),
+            "FL1": lambda: V("CO", "FL1", "ts", T.FL[:, 16:32], T.CO[:, 10::11], 2, 3 << 8, AO.arith_shift_right, AO.bitwise_and),
+            "FL2": lambda: V("CO", "FL2", "ts", T.FL[:, 32:48], T.CO[:, 10::11], 4, 3 << 9, AO.arith_shift_right, AO.bitwise_and),
+            "LS": lambda: V("FL0 FL1 FL2 XQ XR", "LS", "tt", T.LS[:], T.FL[:], T.XQ[:], AO.add),
+            "LQ": lambda: V("LS", "LQ", "tc", T.LQ[:], T.LS[:]),
+            "OM0": lambda: S("LQ " + OMA, "OM0", T.OM[:, 0:256], T.OM[:, 256:1280].indirect(T.LQ[:, 16:32]), AF.Copy),
+            "NP0": lambda: S("LQ " + NPA, "NP0", T.NP[:, 0:256], T.NP[:, 256:1280].indirect(T.LQ[:, 16:32]), AF.Copy),
             "FO": hand_on,
-            "DC": lambda: V("CW", "DC", "ts", T.DC[:], T.CW[:], 7, 1, AO.arith_shift_right, AO.bitwise_and),
-            "CH": lambda: V("CW", "CH", "ts", T.CH[:], T.CW[:], 3, 1, AO.arith_shift_right, AO.bitwise_and),
-            "PD": lambda: V("DC PPa PPb", "PD", "tt", T.PD[:], T.DC[:], T.PP[:], AO.mult),
-            "PC": lambda: V("CH PTa PTb", "PC", "tt", T.PC[:], T.CH[:], T.PT[:], AO.mult),
-            "D1": lambda: V("PD", "D1", "tt", T.D1[:], T.PD[:, 0:32], T.PD[:, 32:64], AO.add),
+            "ONE": lambda: mms("IDB ONB", "KEY1", [(T.KEY1[:, 0:256], T.IDB[:], T.ONB[:], True, False)]),
+            "CW": lambda: V("CO LW POW", "CW", "tt", T.CW[:], T.CO[:, 0:176].indirect(T.LW[:, 0:5]), T.POW[:], AO.mult),
+            "CH": lambda: V("CW", "CH", "ts", T.CH[:], T.CW[:], 4, 1, AO.arith_shift_right, AO.bitwise_and),
+            "PC": lambda: V("CH CT", "PC", "tt", T.PC[:], T.CH[:, 0:64], T.CT[:], AO.mult),
             "YY": lambda: V("PC TR YY", "YY", "tt", T.YY[:, 0:16], T.PC[:, 48:64], T.TR[:, 0:16], AO.add),
-            "VVa": lambda: V("D1", "VVa", "tt", T.VV[:, 0:16], T.D1[:, 0:16], T.D1[:, 16:32], AO.add),
-            "VVb": lambda: V("PC YY", "VVb", "tt", T.VV[:, 16:64], T.PC[:, 0:48], T.YY[:], AO.add),
-            "VUa": lambda: V("VVa VVb", "VUa", "ts", T.VU[:, 0:64], T.VV[:], 4, None, AO.arith_shift_right),
-            "VUb": lambda: V("VVa VVb", "VUb", "ts", T.VU[:, 64:96], T.VV[:, 0:32], 15, None, AO.bitwise_and),
-            "LE": lambda: V("VUa VUb", "LE", "tc", T.LE[:], T.VU[:]),
-            "PUT": lambda: V("NP0 NP1 NP2 BB00 BB01 BB10 BB11 BB20 BB21 LE", "PFT " + PFA, "tt",
-                             T.PF[:, 0:4864].indirect(T.LE[:, 16:64]), T.NP[:], T.BB[:], AO.add)}
+            "VV": lambda: V("PC YY", "VV", "tt", T.VV[:], T.PC[:, 0:48], T.YY[:], AO.add),
+            "LE": lambda: V("VV", "LE", "tc", T.LE[:], T.VV[:]),
+            "PUT": lambda: V("NP0 NP2 NP3 BB0 BB1 BB2 LE", "PFT " + PFA, "tt", T.PF[:, 0:4864].indirect(T.LE[:]), T.NP[:, 0:768], T.BB[:], AO.max)}
         for i in range(10):
-            end.update({"N%d" % i: miss(i), "Y%d" % i: meaning(i)})
-        for i in range(3):
-            end.update(slot(i))
+            end["Y%d" % i] = meaning(i)
+        for u in (1, 2, 3):
+            end.update(column(u, str(u), 0, 256))
+            end["BB%d" % (u - 1)] = new(u - 1)
         for X in range(2):
             end.update(decider(X))
             end.update({name + str(X): finish(name, X) for name in ("M", "H", "D1", "P1", "J", "F")})
-            end["HR%d" % X] = last_row(X)
+            end.update(column(4, "4%d" % X, 128 * X, 128))
+            end.update({"Q%d" % X: apart4(X), "NE%d" % X: miss(X)})
         if t < 2:
-            end.update({"ZR": lambda: V("DC", "ZR", "red", T.ZR[:, 0:1], T.DC[:], AxisListType.X, AO.add),
-                        "ZP": lambda: mms("ONE ZR", "DB1", [(bank(1, 1), T.ONE[:], T.ZR[:, 0:1], True, True)]),
+            end.update({"ZR": lambda: V("CH", "ZR", "red", T.ZR[:, 0:1], T.CH[:, 64:80], AxisListType.X, AO.add),
+                        "ZP": lambda: mms("ONE ZR", "DB1", [(T.DB1[:, 0:1], T.ONE[:], T.ZR[:, 0:1], True, True)]),
                         "ZA": closed})
-            end.update(first(t + 1))
+        if t == 2:
+            end["ZA"] = end.pop("FO")
         for name in END:
             if name[0] == "@":
                 until(float(name[1:]))
@@ -523,17 +504,17 @@ def rank_program(g, core, T, topo):
     for pieces in OUT:
         d0, keys = c0, ""
         for n in pieces:
-            b = BANKS[q % 4]
+            b = ("DB0", "DB1", "DB2", "KEY1")[q % 4]
             if q == 0:
-                V(PFA, b, "ts", bank(0, n), T.PF[:, 2048:2048 + n], 4096.0, None, AO.mult)
+                V(PFA, b, "ts", T[b][:, 0:n], T.PF[:, 2048:2048 + n], 4096.0, None, AO.mult)
             else:
-                S(PFA, b, bank(q % 4, n), T.PF[:, 2048 + c0:2048 + c0 + n], AF.Copy, scale=4096.0)
-            V("%s %s" % (b, PFA), "YO%d" % q, "tt", T.YO[:, c0:c0 + n], bank(q % 4, n), T.PF[:, c0:c0 + n], AO.add)
+                S(PFA, b, T[b][:, 0:n], T.PF[:, 2048 + c0:2048 + c0 + n], AF.Copy, scale=4096.0)
+            V("%s %s" % (b, PFA), "YO%d" % q, "tt", T.YO[:, c0:c0 + n], T[b][:, 0:n], T.PF[:, c0:c0 + n], AO.add)
             c0, q, keys = c0 + n, q + 1, keys + " YO%d" % q
         dma("Y", keys, "yp%d" % q, T.yp[:, d0:c0], T.YO[:, d0:c0])
     for sem in SEMAPHORES:
         if cnt[sem] and sem != "ls":
             need("G", sem, cnt[sem])
     need("G", "ls", cnt["ls"])
-    for sem in ("aS1", "aS2", "aF1", "aF2"):
+    for sem in ("aS1", "aS2", "aF1", "aF2", "aL1", "aL2"):
         need("G", sem, narr)

from concourse.mybir import dt, AluOpType, AxisListType, ActivationFunctionType
import comms_topo

AO = AluOpType
AF = ActivationFunctionType
SHARE = {None: (64, 104), 0: (32, 72), 1: (64, 112), 7: (64, 96)}
PHASE = {"M": -1.34, "B": -1.317, "H": -1.255, "D0": -1.174, "P0": -1.134, "D1": -1.054, "P1": -0.965, "J": -0.942, "L": -0.881, "F": -0.751,
         "K": -0.722, "E": -0.7, "Y": -0.661, "T": -0.572, "S0": -0.509, "G": -0.482, "C": -0.44, "S1": -0.251, "R0": -0.232, "N0": 0.047,
         "R1": 0.116, "U": 0.143, "N1": 0.407, "W": 0.536}
OTHER = {("E", 0): -2.051, ("K", 0): -1.997, ("T", 0): -1.499, ("C", 0): -1.133, ("R1", 0): -0.601, ("S0", 0): -0.096, ("N0", 0): 0.456,
         ("K", 1): -2.552, ("T", 1): -0.969, ("N0", 1): -0.006, ("W", 6): 0.71, ("T", 7): -0.304, ("C", 7): -0.246, ("N1", 7): 0.16}
START = ("IDB L8 AI IDF LR WF JQ MK GW SRB XQ KB NI SH TW0 WB SRG MS TW1 JM HP0 KA PH0 PL0 PH1 HP1 TW2 TW3 SL XR PH3 K0 HP2 XM HP3 PL2 HS CB "
         "PL1 LC PL3 GU HB PH2").split()
END = ("@6.373 SUM @6.907 HA M0 OM2 H0 CF D10 @7.081 DV @7.348 NP2 P10 AS CT OM1 J0 @9 OD M1 OM40 OF H1 F0 Y2 DF Y1 D11 Q0 P11 Y7 NP1 NE0 OM3 "
       "NP40 J1 Y5 Y4 Q1 NP3 Y0 NE1 CO ONE OM41 FL2 FL0 FL1 LS NP41 LQ CW SEL0 CH SEL1 F1 PC DEC0 YY VV FO DEC1 OM0 BB2 BB1 BB0 LE NP0 ZR ZP "
       "PUT ZA").split()
LOADS = ((0, 1), (1, 2), (2, 3), (3, 4))
OUT = ((384,), (512,), (512,), (384,), (256,))
TABLE = {2: 0, 3: 1, 1: 2, 4: 3}
HITS = [(s, j) for s in (4, 3, 2, 1) for j in range(s)]

F32, BF, I32, U16 = "float32", "bfloat16", "int32", "uint16"
SCRATCH = {}


def _s(name, cols, dtype, where="sbuf"):
    SCRATCH[name] = (where, [128] + (cols if isinstance(cols, list) else [cols]), dtype)


for _n, _c, _d in [
        ("R", 4096, BF), ("PF", 4864, F32), ("PK", 2048, I32), ("TW", 2048, F32), ("YO", 2048, F32),
        ("JI", 256, I32), ("JQ", 256, F32), ("SRI", 256, I32), ("SRB", 256, BF), ("JM", 256, F32), ("K0", 16, I32), ("CB", 32, I32),
        ("FX0", 256, BF), ("FIN1", 256, BF), ("FIN2", 256, BF), ("FO0", 256, BF), ("FO1", 256, BF), ("FO2", 256, BF),
        ("ST0", 528, BF), ("ST1", 528, BF), ("ST2", 528, BF), ("LL0", [3, 80], U16), ("LL1", [3, 80], U16), ("LL2", [3, 80], U16),
        ("RG", 8192, BF), ("A", 4096, BF), ("FH", 2560, BF), ("FT", 512, BF), ("FD", 256, BF),
        ("NU", 256, U16), ("SC", 256, I32), ("HC", 32, I32), ("KC", 256, F32), ("KH", 256, BF), ("H5", 48, BF),
        ("DV", 48, F32), ("AS", 48, I32), ("OD", 48, I32), ("OF", 48, F32), ("CC", 64, F32), ("CT", 64, F32),
        ("NE", 176, F32), ("CD", 176, F32), ("CO", 176, I32), ("CW", 80, I32), ("CH", 80, I32), ("FL", 48, I32), ("LS", 48, F32), ("LQ", 48, U16),
        ("PC", 64, F32), ("YY", 48, F32), ("VV", 48, F32), ("LE", 48, U16),
        ("SEL", 256, F32), ("OM", 1280, BF), ("NP", 1280, F32), ("BB", 768, F32), ("ZR", 1, F32), ("ZA", 1, F32),
        ("IM", 160, F32), ("IG", 128, F32), ("IB", 128, F32), ("IPI", 2, I32), ("IQI", 4, I32), ("CF", 8, F32), ("RS", 128, F32),
        ("IDB", 128, BF), ("IDF", 128, F32), ("NI", 128, BF), ("WB", 144, BF), ("WF", 144, F32), ("BO", 128, F32), ("ONE", 128, F32), ("ONB", 256, BF),
        ("GU", 8, BF), ("GW", 8, BF), ("AI", 8, BF), ("MK", 128, F32), ("XM", 128, BF), ("LR", 8, U16),
        ("L8", 128, BF), ("MG", 8, F32), ("OHW", 24, F32), ("IA", 32, F32), ("XQ", 48, F32), ("BI", 2, F32), ("YB", 11, F32),
        ("POW", 80, F32), ("IL", 6, F32), ("LW", 6, U16), ("TRI", 64, F32), ("TR", 64, F32)]:
    _s(_n, _c, _d)
for _n in ["DB0", "DB1", "DB2", "KEY0", "KEY1"]:
    _s(_n, 512, F32, "psum")
_s("FTP", 1024, BF, "psum")
for _n in ["FP0", "FP1"]:
    _s(_n, [64, 16], BF, "psum")

SEMAPHORES = ["sv", "ss", "sp", "sg", "aS1", "aS2", "aF1", "aF2", "aL1", "aL2", "ls"] + ["d%d" % i for i in range(16)]


def at(name, n):
    return n + OTHER.get((name, n), PHASE[name])


def shares(n):
    c0, c1 = SHARE.get(n, SHARE[None])
    return {"S0": (0, c0), "S1": (c0, c1), "G": (c1, 128)}


def codes(odd):
    out = [(3 << 13) + (11 << 17)]
    for i, (s, j) in enumerate(HITS):
        d = s if odd else j + 1
        ch = sum(8 >> (u - 1) for u in range(j + 1, s + 1) if u != d)
        out.append(ch + 16 + (TABLE[d] << 8) + (TABLE[4 if ch & 1 else 1] << 10) + (s - 1 << 13) + ((10 - i) << 17))
    return out


def rank_program(g, core, T, topo):
    rank = T.rank_of(core)
    if rank is None:
        return
    nrank = len(T.cores)
    ENG = {"V": (g.vector, "sv"), "S": (g.scalar, "ss"), "P": (g.tensor, "sp"), "G": (g, "sg"), "Y": (g.sync, None)}
    cnt = {s: 0 for s in SEMAPHORES}
    waited, Wr, Rd, ndma = {}, {}, {}, [0]

    def need(e, sem, val):
        if waited.get((e, sem), 0) < val:
            ENG[e][0].wait_ge(T.sem[sem], val)
            waited[(e, sem)] = val

    def sync(e, reads, writes):
        todo = {}
        for k in reads:
            for s, v in Wr.get(k, {}).items():
                todo[s] = max(todo.get(s, 0), v)
        for k in writes:
            for s, v in Wr.get(k, {}).items():
                todo[s] = max(todo.get(s, 0), v)
            for s, v in Rd.get(k, {}).items():
                todo[s] = max(todo.get(s, 0), v)
        if e == "P":
            todo.pop("sp", None)
        for s, v in todo.items():
            need(e, s, v)

    def note(sem, val, reads, writes):
        for k in reads:
            Rd.setdefault(k, {})[sem] = val
        for k in writes:
            Wr.setdefault(k, {})[sem] = val

    def run(e, reads, writes, name, *a, **kw):
        reads, writes = reads.split(), writes.split()
        sync(e, reads, writes)
        q, sem = ENG[e]
        ins = {"tc": lambda: q.tensor_copy(*a, **kw), "tt": lambda: q.tensor_tensor(*a, **kw), "ts": lambda: q.tensor_scalar(*a, **kw),
               "scan": lambda: q.tensor_tensor_scan(*a, **kw), "memset": lambda: q.memset(*a, **kw), "red": lambda: q.tensor_reduce(*a, **kw),
               "act": lambda: q.activation(*a, **kw), "mm": lambda: q.matmul(*a, **kw), "iota": lambda: q.iota(*a, **kw),
               "tr": lambda: q.transpose(*a, **kw)}[name]()
        cnt[sem] += 1
        ins.then_inc(T.sem[sem], 1)
        note(sem, cnt[sem], reads, writes)

    def V(reads, writes, name, *a, **kw):
        run("V", reads, writes, name, *a, **kw)

    def S(reads, writes, out, in_, func, **kw):
        run("S", reads, writes, "act", out, in_, func, **kw)

    def mms(reads, writes, calls):
        sync("P", reads.split(), writes.split())
        for c in calls[:-1]:
            g.tensor.matmul(*c)
        run("P", reads, writes, "mm", *calls[-1])

    def turns(reads, writes, calls):
        sync("P", reads.split() + ["IDB"], writes.split())
        for c in calls[:-1]:
            g.tensor.transpose(*c)
        run("P", reads + " IDB", writes, "tr", *calls[-1])

    def dma(e, reads, writes, out, in_):
        reads, writes = reads.split(), writes.split()
        sync(e, reads, writes)
        sem = "d%d" % ndma[0]
        ndma[0] += 1
        ENG[e][0].dma_start(out, in_).then_inc(T.sem[sem], 16)
        cnt[sem] = 16
        note(sem, 16, reads, writes)

    def send(dst_rank, src, dst, arr, key):
        d = T.cores[dst_rank]
        rid, pid, _ = topo.addr(d)
        sync("G", key.split(), [])
        g.remote_dma(out_ap=dst, in_ap=src, remote_sem=T.sem[arr], local_sem=T.sem["ls"], pid=pid, routing_id=rid,
                     dma_engine_mask=topo.mask(core, d))
        cnt["ls"] += len(topo.engines(core, d))

    narr = len(topo.engines(core, T.cores[(rank + 1) % nrank]))

    dma("Y", "", "JI", T.JI[:], T.jc[:])
    dma("S", "", "SRI", T.SRI[0:8, :], T.sr[:])
    for q0, q1 in LOADS:
        dma("Y", "", " ".join("PK%d" % q for q in range(q0, q1)), T.PK[:, 512 * q0:512 * q1], T.pk[:, 512 * q0:512 * q1])
    dma("Y", "", "FX0", T.FX0[:], T.fx[:])
    dma("Y", "", "R", T.R[:], T.rt[:])

    def iota(key, out, pat, base, cm=0):
        run("G", "", key, "iota", out, pat, base, cm, allow_small_or_imprecise_dtypes=True)
    run("G", "", "IPI", "iota", T.IPI[:], [[0, 2]], 0, 1)
    iota("IM", T.IM[:], [[1, 160]], 0)
    iota("IG", T.IG[:], [[1, 8], [0, 16]], 0)
    iota("IB", T.IB[:], [[0, 8], [1, 16]], 0)
    iota("IA", T.IA[:], [[0, 2], [16, 16]], 0)
    iota("RS", T.RS[:], [[0, 128]], 1 - 2 ** 24)
    iota("RS", T.RS[:, 0::16], [[0, 8]], 2 ** 24 - 1)
    CUT, BIG = 4096.0 * 2047 + 2047.5, 1.5 * 2.0 ** 35
    V("", "BI0", "memset", T.BI[:, 0:1], 2047 - BIG / 4096)
    V("", "BI1", "memset", T.BI[:, 1:2], 4096.0 * 2047 - BIG)
    V("IPI", "IQ0", "ts", T.IQI[:, 0:2], T.IPI[:], 15, None, AO.bitwise_and)
    V("IPI", "IQ1", "ts", T.IQI[:, 2:4], T.IPI[:], 4, None, AO.arith_shift_right)
    V("IQ0", "CF4", "ts", T.CF[:, 4:5], T.IQI[:, 0:1], 4096.0, None, AO.mult)
    V("IPI", "CF0", "tc", T.CF[:, 0:1], T.IPI[:, 0:1])
    V("IQ0 IQ1", "CF1", "tc", T.CF[:, 1:3], T.IQI[:, 0:4:2])
    V("IQ1", "CF3", "ts", T.CF[:, 3:4], T.IQI[:, 2:3], 16.0, 15.0, AO.mult, AO.add)
    V("IPI", "CF5", "ts", T.CF[:, 5:6], T.IPI[:, 0:1], 16.0, None, AO.mult)
    p_c, q_c, g_c, e_c, k_c, x_c = [T.CF[:, i:i + 1] for i in range(6)]
    V("IM CF1", "MG", "ts", T.MG[:], T.IM[:, 0:8], g_c, None, AO.is_equal)

    EVEN, ODD = codes(0), codes(1)

    def late_constants():
        iota("PFT", T.PF[:, 4096:4864], [[0, 768]], 0)
        iota("FHT", T.FH[:, 2049:2560:2], [[0, 256]], 0)
        iota("TRIa", T.TRI[:, 0:48], [[16, 48]], 4096)
        iota("TRIb", T.TRI[:, 48:64], [[16, 16]], 4096)
        iota("ONE", T.ONE[:], [[0, 128]], 1)
        iota("ONB", T.ONB[:], [[0, 256]], 1)
        for u, m in enumerate((2, 4, 8, 16, 1)):
            iota("POW", T.POW[:, 16 * u:16 * u + 16], [[0, 16]], m)
        for i in range(11):
            if EVEN[i] == ODD[i]:
                iota("CD%d" % i, T.CD[:, i::11], [[0, 16]], EVEN[i])
            else:
                iota("YB", T.YB[:, i:i + 1], [[0, 1]], EVEN[i])

    def late_constants_v():
        return [lambda: V("IM CF1", "OHW", "ts", T.OHW[:], T.IM[:, 0:24], q_c, 4096.0, AO.is_equal, AO.mult),
                lambda: V("IM CF1", "IL", "ts", T.IL[:], T.IM[:, 0:6], 0.0, q_c, AO.mult, AO.add),
                lambda: V("IL", "LW", "ts", T.LW[:], T.IL[:], 11.0, 10.0, AO.mult, AO.add),
                lambda: V("TRIa TRIb CF1", "TR", "ts", T.TR[:], T.TRI[:], q_c, None, AO.add),
                lambda: V("TR", "YY", "tc", T.YY[:], T.TR[:, 0:48]),
                lambda: V("IG CF1", "BO", "ts", T.BO[:], T.IG[:], g_c, -2.0 ** -12, AO.is_equal, AO.mult)]
    CDA = " ".join("CD%d" % i for i in range(11))
    PFA = " ".join("PFH%d PFL%d" % (q, q) for q in range(4))

    def both(k, s):
        return "%s0%d %s1%d" % (k, s, k, s)

    def unpack(q):
        c, h, k, b = slice(512 * q, 512 * q + 512), slice(2048 + 512 * q, 2560 + 512 * q), str(q), ("KEY1", "KEY0", "DB0", "DB2")[q]
        return {"TW" + k: lambda: V("PK" + k, "TW" + k, "ts", T.TW[:, c], T.PK[:, c], CUT, BIG, AO.subtract, AO.add),
                "HP" + k: lambda: S("TW%s BI1" % k, b, T[b][:], T.TW[:, c], AF.Identity, bias=T.BI[:, 1:2]),
                "PH" + k: (lambda: V("TW" + k, "PFH" + k, "ts", T.PF[:, h], T.TW[:, c], 2.0 ** -12, 2047 - BIG / 4096, AO.mult, AO.add))
                if q == 3 else
                (lambda: S("TW%s BI0" % k, "PFH" + k, T.PF[:, h], T.TW[:, c], AF.Identity, scale=2.0 ** -12, bias=T.BI[:, 0:1])),
                "PL" + k: lambda: V("PK%s %s" % (k, b), "PFL" + k, "tt", T.PF[:, c], T.PK[:, c], T[b][:], AO.subtract)}

    start = {
        "WF": lambda: V("IM CF3", "WF", "ts", T.WF[:, 0:143], T.IM[:, 0:143], e_c, None, AO.is_equal),
        "L8": lambda: V("IG CF0", "L8", "ts", T.L8[0:8, :], T.IG[0:8, :], T.CF[0:8, 0:1], None, AO.is_equal),
        "WB": lambda: S("WF", "WB", T.WB[:, 0:143], T.WF[:, 0:143], AF.Copy),
        "GU": lambda: S("MG", "GU", T.GU[:], T.MG[:], AF.Copy, scale=65536.0),
        "GW": lambda: S("MG", "GW", T.GW[:], T.MG[:], AF.Copy, scale=-131072.0),
        "AI": lambda: S("MG", "AI", T.AI[:], T.MG[:], AF.Copy),
        "IDF": lambda: V("IM CF0", "IDF", "ts", T.IDF[:], T.IM[:, 0:128], p_c, None, AO.is_equal),
        "IDB": lambda: V("IM CF0", "IDB", "ts", T.IDB[:], T.IM[:, 0:128], p_c, None, AO.is_equal),
        "NI": lambda: S("IDB", "NI", T.NI[:], T.IDB[:], AF.Copy, scale=-1.0),
        "LR": lambda: V("IM", "LR", "tc", T.LR[:], T.IM[:, 0:8]),
        "MK": lambda: V("IB CF1", "MK", "ts", T.MK[:], T.IB[:], q_c, None, AO.is_equal),
        "XM": lambda: S("MK CF5", "XM", T.XM[:], T.MK[:], AF.Identity, scale=x_c),
        "XQ": lambda: S("IA CF1", "XQ", T.XQ[:, 0:32], T.IA[:], AF.Identity, bias=q_c),
        "XR": lambda: S("XQ", "XR", T.XQ[:, 32:48], T.XQ[:, 0:16], AF.Copy, scale=2.0),
        "JQ": lambda: V("JI CF4", "JQ", "ts", T.JQ[:], T.JI[:], k_c, None, AO.add),
        "SRB": lambda: V("SRI", "SRB", "tc", T.SRB[0:8, :], T.SRI[0:8, :]),
        "SRG": lambda: mms("L8 SRB", "DB1", [(T.DB1[:, 0:256], T.L8[0:8, :], T.SRB[0:8, :], True, True)]),
        "MS": lambda: V("DB1 CF1", "DB0", "ts", T.DB0[:, 0:256], T.DB1[:, 0:256], q_c, None, AO.is_equal),
        "JM": lambda: V("DB0 JQ", "JM", "tt", T.JM[:], T.DB0[:, 0:256], T.JQ[:], AO.mult),
        "KA": lambda: mms("WF JM", "DB1",
                          [(T.DB1[:, 0:16], T.WF[:, 15 - b:143 - b], T.JM[:, b::16], b == 0, b == 15) for b in range(16)]),
        "K0": lambda: V("DB1", "K0", "tc", T.K0[:], T.DB1[:, 0:16]),
        "CB": lambda: V("K0", "CB", "ts", T.CB[:, 0:16], T.K0[:], 4095, None, AO.bitwise_and),
        "LC": lambda: V("CB", "LS0", "tc", T.LL0[:, 0, 0:16], T.CB[:, 0:16]),
        "HS": lambda: V("K0", "HS", "ts", T.CB[:, 16:32], T.K0[:], 12, None, AO.arith_shift_right),
        "HB": lambda: V("HS", "SR0", "tc", T.ST0[:, 512:528], T.CB[:, 16:32]),
        "KB": lambda: mms("JQ IDF", "DB2", [(T.DB2[:, 128 * X:128 * X + 128], T.JQ[:, 128 * X:128 * X + 128], T.IDF[:], True, True) for X in range(2)]),
        "SH": lambda: S("DB2", "SH0", T.ST0[:, 0:256], T.DB2[:, 0:256], AF.Copy),
        "SL": lambda: V("DB2 SH0", "SL0", "tt", T.ST0[:, 256:512], T.DB2[:, 0:256], T.ST0[:, 0:256], AO.subtract)}
    for q in range(4):
        start.update(unpack(q))
    for name in START:
        start[name]()
    for t in (1, 2):
        send((rank + t) % nrank, T.ST0[:], T["ST%d" % t][:], "aS%d" % t, "SH0 SL0 SR0 R")
        send((rank + t) % nrank, T.LL0[:, 0, 0:16], T["LL%d" % t][:, 0, 0:16], "aL%d" % t, "LS0")
    late_constants()
    for t in (1, 2):
        for key, sem in (("SH", "aS"), ("SL", "aS"), ("SR", "aS"), ("FIN", "aF"), ("LS", "aL")):
            Wr["%s%d" % (key, t)] = {"%s%d" % (sem, t): narr}

    for t in range(3):
        st, stk = T["ST%d" % t], "SH%d SL%d" % (t, t)
        fin, fk = (T.FX0, "FX0") if t == 0 else (T["FIN%d" % t], "FIN%d" % t)
        fo, fok, ll = T["FO%d" % t], "FO%d" % t, T["LL%d" % t]

        def lc(X, s):
            return "LC%d%d" % (X, s) if s > 1 else "LS%d" % t

        def entries(X, s):
            l0 = 16 * s - 16 + 8 * X
            V("%s %s" % (PFA, lc(X, s)), "NU%d" % X, "tc", T.NU[:, 128 * X:128 * X + 128], T.PF[:, 0:4096].indirect(ll[:, 0, l0:l0 + 8]))

        def got(w, halves):
            return " ".join("RG%d%d%s" % (w, h, e) for h in halves for e in ("G", "S0", "S1"))

        def rules(name, n):
            x0, x1 = shares(n)[name]
            X, w = n % 2, n % 4
            wr = " ".join("RG%d%d%s" % (w, h, name) for h in range(x0 // 64, (x1 + 63) // 64))
            out, src = T.RG[:, 2048 * w + 16 * x0:2048 * w + 16 * x1], T.R[:, 0:4096].indirect(T.NU[:, 128 * X + x0:128 * X + x1])
            if name == "G":
                V("R NU%d" % X, wr, "tc", out, src)
            else:
                S("R NU%d" % X, wr, out, src, AF.Copy)

        def smaller(n, h):
            X, w = n % 2, n % 4
            a0, r0 = 2048 * X + 1024 * h, 2048 * w + 1024 * h
            V("FP%d %s" % (h, got(w, [h])), "A%d%d" % (X, h), "tt", T.A[:, a0:a0 + 1024], T.RG[:, r0:r0 + 1024], T["FP%d" % h][:, :, :], AO.min)

        def payloads(n):
            X = n % 2
            k = T["KEY%d" % X][:, 0:128]
            mms("IDB " + stk, "KEY%d" % X, [(k, T.IDB[:], st[:, 128 * X:128 * X + 128], True, False),
                                            (k, T.IDB[:], st[:, 256 + 128 * X:384 + 128 * X], False, False)])

        def sums(n, of):
            X, w = n % 2, n % 4
            rd, src, c0, m = ("GU " + got(w, (0, 1)), T.RG, 2048 * w, T.GU) if of == "U" else ("GW A%d0 A%d1" % (X, X), T.A, 2048 * X, T.GW)
            mms(rd, "KEY%d" % X, [(T["KEY%d" % X][:, k:128:16], src[:, c0 + k:c0 + 2048:16], m[:], False, of == "W" and k == 15) for k in range(16)])

        def least(X, s):
            V("RS KEY%d" % X, "SC%d" % X, "scan", T.SC[:, 128 * X:128 * X + 128], T.RS[:], T["KEY%d" % X][:, 0:128], 0.0, AO.max, AO.min)

        def row(X, s):
            V("SC%d" % X, "HX%d" % X, "ts", T.HC[:, 16 * X + 8:16 * X + 16], T.SC[:, 128 * X + 15:128 * X + 128:16], 12, 15,
              AO.arith_shift_right, AO.bitwise_and)

        def court(X, s):
            V("SC%d" % X, "CX%d" % X, "ts", T.HC[:, 16 * X:16 * X + 8], T.SC[:, 128 * X + 15:128 * X + 128:16], 4095, None, AO.bitwise_and)

        def spread(X, j):
            c0 = 16 * X + 8 * j
            V("LR MK %sX%d" % ("CH"[j], X), "K%s%d" % ("CH"[j], X), "tt", (T.KC, T.KH)[j][:, 128 * X:128 * X + 128],
              T.HC[:, c0:c0 + 8].indirect(T.LR[:]), T.MK[:], AO.mult)

        def route(X, j):
            c = slice(128 * X, 128 * X + 128)
            if j == 0:
                mms("MG KC%d" % X, "DB1", [(T.DB1[:, 0:8], T.KC[:, c], T.MG[:], True, True)])
            else:
                mms("AI XM KH%d" % X, "DB2", [(T.DB2[:, 0:8], T.XM[:], T.AI[:], True, False), (T.DB2[:, 0:8], T.KH[:, c], T.AI[:], False, True),
                                              (T.DB2[:, 8:16], T.KH[:, c], T.AI[:], True, True)])

        def courts(X, s):
            a0 = 16 * s + 8 * X
            V("DB1", lc(X, s + 1), "tc", ll[:, 0, a0:a0 + 8], T.DB1[:, 0:8])

        def places(X, s):
            a0 = 16 * s + 8 * X
            V("DB2", "LF%d%d" % (X, s), "tc", ll[:, 1:3, a0:a0 + 8], T.DB2[:, 0:16])

        def chosen(X, s):
            f0, w, a0 = 512 * s + 256 * X, (2 * s - 2 + X) % 4, 16 * s + 8 * X
            out, key = (T.FD[:, 128 * X:128 * X + 128], "FD%d" % X) if s < 4 else (T.FH[:, f0:f0 + 256:2], "FH%d4a" % X)
            V("LF%d%d FH%d%da %s" % (X, s, X, s - 1, got(w, (0, 1))), key, "tt", out,
              T.RG[:, 2048 * w:2048 * w + 2048].indirect(ll[:, 1, a0:a0 + 8]), T.FH[:, f0 - 512:f0 - 256:2], AO.subtract)

        def kept(X, s):
            f0 = 512 * s + 256 * X
            src, key = (T.FD, "FD%d" % X) if s else (fin, fk)
            for c in range(2):
                S(key, "FH%d%d%s" % (X, s, "ab"[c]), T.FH[:, f0 + c:f0 + 256:2], src[:, 128 * X:128 * X + 128], AF.Abs)

        def turn(X, s):
            f0 = 512 * s + 256 * X
            turns("FH%d%da FH%d%db" % (X, s, X, s), "FTP",
                  [(T.FTP[:, 128 * h:128 * h + 128], T.FH[:, f0 + 128 * h:f0 + 128 * h + 128], T.IDB[:]) for h in range(2)])

        def turned(X, s):
            V("FTP", "FT%d" % X, "tc", T.FT[:, 256 * X:256 * X + 256], T.FTP[:, 0:256])

        def repeat(X, h):
            turns("FT%d" % X, "FP%d" % h, [(T["FP%d" % h][:, :, q:q + 2], T.FT[:, 256 * X + 128 * h:256 * X + 128 * h + 128], T.IDB[:])
                                           for q in range(0, 16, 2)])

        lv = late_constants_v() if t == 0 else []

        last = {"M": least, "H": row, "B": court, "L": courts, "J": places, "F": chosen,
                "D0": lambda X, s: spread(X, 0), "D1": lambda X, s: spread(X, 1), "P0": lambda X, s: route(X, 0), "P1": lambda X, s: route(X, 1)}
        facts = {"K": kept, "T": turn, "C": turned}

        def call(name, n):
            X, s, j = n % 2, n // 2 + 1, int(name[1:] or 0)
            if name == "E":
                entries(X, s)
            elif name in last:
                if n >= 2:
                    last[name](X, s - 1)
                    if name == "M" and lv:
                        lv.pop(0)()
            elif name in facts:
                facts[name](X, s - 1)
            elif name[0] in "GS":
                rules(name, n)
            elif name[0] == "R":
                repeat(X, j)
            elif name == "Y":
                payloads(n)
            elif name[0] == "N":
                smaller(n, j)
            else:
                sums(n, name)
        todo = sorted((at(name, n), name, n) for n in range(8) for name in PHASE)

        def until(place):
            while todo and todo[0][0] < place:
                call(*todo.pop(0)[1:])

        def rows(s, x0, n):
            return st[:, 512 + x0:512 + x0 + n] if s == 0 else T.H5[:, 16 * s - 16 + x0:16 * s - 16 + x0 + n]

        def apart():
            mms("IDB NI HA SR%d" % t, "DB0", [(T.DB0[:, i:176:11], m, rows(u, 0, 16), k == 0, k == 1)
                                              for i, (s, j) in enumerate([(0, 0)] + HITS) if s < 4
                                              for k, (m, u) in enumerate(((T.IDB[:], s), (T.NI[:], j)))])

        def apart4(X):
            return lambda: mms("AI NI HA SR%d KH%d" % (t, X), "DB0",
                               [(T.DB0[:, 88 * X + j + 1:88 * X + 88:11], m, r, k == 0, k == 1) for j in range(4)
                                for k, (m, r) in enumerate(((T.KH[:, 128 * X:128 * X + 128], T.AI[:]), (T.NI[:], rows(j, 8 * X, 8))))])

        def miss(X):
            return lambda: S("DB0", "NE%d" % X, T.NE[:, 88 * X:88 * X + 88], T.DB0[:, 88 * X:88 * X + 88], AF.Abs, scale=2.0 ** 22)

        def meaning(i):
            j = HITS[i][1]
            return lambda: S("OF YB", "CD%d" % (i + 1), T.CD[:, i + 1::11], T.OF[:, 16 * j:16 * j + 16], AF.Identity,
                             scale=float(ODD[i + 1] - EVEN[i + 1]), bias=T.YB[:, i + 1:i + 2])

        def column(u, k, x0, n):
            c0, l0 = 256 * TABLE[u] + 256 + x0, 16 * u + x0 // 16
            c = slice(c0, c0 + n)
            return {"OM" + k: lambda: S("OHW " + (both("LF", u) if u < 4 else "LF%s4" % k[1]), "OM" + k, T.OM[:, c],
                                        T.OHW[:, 0:16].indirect(ll[:, 2, l0:l0 + n // 16]), AF.Copy),
                    "NP" + k: lambda: V("OM%s %s %s %s" % (k, lc(0, u), lc(1, u), PFA), "NP" + k, "tt", T.NP[:, c],
                                        T.PF[:, 0:4096].indirect(ll[:, 0, l0 - 16:l0 - 16 + n // 16]), T.OM[:, c], AO.subtract)}

        def decider(h):
            c = slice(128 * h, 128 * h + 128)
            return {"SEL%d" % h: lambda: S("LQ " + NPA, "SEL%d" % h, T.SEL[:, c], T.NP[:, 256:1280].indirect(T.LQ[:, 8 * h:8 * h + 8]),
                                           AF.Relu, scale=-1.0),
                    "DEC%d" % h: lambda: mms("BO SEL%d" % h, "KEY1", [(T.KEY1[:, c], T.BO[:], T.SEL[:, c], False, h == 1)])}

        def new(i):
            d = slice(256 * i, 256 * i + 256)
            return lambda: V("KEY1 OM%d" % (i and i + 1), "BB%d" % i, "tt", T.BB[:, d], T.KEY1[:, 0:256], T.OM[:, d], AO.mult)

        def finish(name, X):
            return lambda: last[name](X, 4)

        def hand_on():
            S("LQ FHT " + " ".join("FH%d%d%s" % (X, s, c) for X in range(2) for s in range(1, 5) for c in "ab"), fok, fo[:],
              T.FH[:, 512:2560].indirect(T.LQ[:, 32:48]), AF.Abs)
            if t < 2:
                send((rank + 1) % nrank, fo[:], T["FIN%d" % (t + 1)][:], "aF%d" % (t + 1), fok)
            else:
                dma("Y", fok, "yf", T.yf[:], fo[:])

        def closed():
            if t == 0:
                V("DB1", "ZA", "tc", T.ZA[:, 0:1], T.DB1[:, 0:1])
            else:
                V("DB1 ZA", "ZA", "tt", T.ZA[:, 0:1], T.DB1[:, 0:1], T.ZA[:, 0:1], AO.add)
        OMA, NPA = "OM1 OM2 OM3 OM40 OM41", "NP1 NP2 NP3 NP40 NP41"
        end = {
            "HA": lambda: V(" ".join(both("LF", s) for s in (1, 2, 3)), "HA", "tc", T.H5[:], ll[:, 2, 16:64]),
            "SUM": lambda: mms("WB " + " ".join("FH%d%da" % (X, s) for X in range(2) for s in range(4)), "DB0",
                               [(T.DB0[:, 0:64], T.WB[:, 15 - b:143 - b], T.FH[:, 2 * b:2048:32], b == 0, b == 15) for b in range(16)]),
            "DV": (lambda: S("DB0 ZA", "DV", T.DV[:], T.DB0[:, 0:48], AF.Identity, bias=T.ZA[:, 0:1])) if t else
                  (lambda: S("DB0", "DV", T.DV[:], T.DB0[:, 0:48], AF.Copy)),
            "AS": lambda: V("DV DB0", "AS", "tt", T.AS[:], T.DV[:], T.DB0[:, 16:64], AO.add),
            "OD": lambda: V("AS", "OD", "ts", T.OD[:], T.AS[:], 1, None, AO.bitwise_and),
            "OF": lambda: V("OD", "OF", "tc", T.OF[:], T.OD[:]),
            "DF": apart,
            "CF": lambda: V(" ".join(lc(X, s) for X in range(2) for s in range(1, 5)), "CC", "tc", T.CC[:], ll[:, 0, 0:64]),
            "CT": lambda: V("CC TR", "CT", "tt", T.CT[:], T.CC[:], T.TR[:], AO.subtract),
            "CO": lambda: V("NE0 NE1 " + CDA, "CO", "scan", T.CO[:], T.NE[:], T.CD[:], 0.0, AO.min, AO.max),
            "FL0": lambda: V("CO", "FL0", "ts", T.FL[:, 0:16], T.CO[:, 10::11], 3 << 8, None, AO.bitwise_and),
            "FL1": lambda: V("CO", "FL1", "ts", T.FL[:, 16:32], T.CO[:, 10::11], 2, 3 << 8, AO.arith_shift_right, AO.bitwise_and),
            "FL2": lambda: V("CO", "FL2", "ts", T.FL[:, 32:48], T.CO[:, 10::11], 4, 3 << 9, AO.arith_shift_right, AO.bitwise_and),
            "LS": lambda: V("FL0 FL1 FL2 XQ XR", "LS", "tt", T.LS[:], T.FL[:], T.XQ[:], AO.add),
            "LQ": lambda: V("LS", "LQ", "tc", T.LQ[:], T.LS[:]),
            "OM0": lambda: S("LQ " + OMA, "OM0", T.OM[:, 0:256], T.OM[:, 256:1280].indirect(T.LQ[:, 16:32]), AF.Copy),
            "NP0": lambda: S("LQ " + NPA, "NP0", T.NP[:, 0:256], T.NP[:, 256:1280].indirect(T.LQ[:, 16:32]), AF.Copy),
            "FO": hand_on,
            "ONE": lambda: mms("IDB ONB", "KEY1", [(T.KEY1[:, 0:256], T.IDB[:], T.ONB[:], True, False)]),
            "CW": lambda: V("CO LW POW", "CW", "tt", T.CW[:], T.CO[:, 0:176].indirect(T.LW[:, 0:5]), T.POW[:], AO.mult),
            "CH": lambda: V("CW", "CH", "ts", T.CH[:], T.CW[:], 4, 1, AO.arith_shift_right, AO.bitwise_and),
            "PC": lambda: V("CH CT", "PC", "tt", T.PC[:], T.CH[:, 0:64], T.CT[:], AO.mult),
            "YY": lambda: V("PC TR YY", "YY", "tt", T.YY[:, 0:16], T.PC[:, 48:64], T.TR[:, 0:16], AO.add),
            "VV": lambda: V("PC YY", "VV", "tt", T.VV[:], T.PC[:, 0:48], T.YY[:], AO.add),
            "LE": lambda: V("VV", "LE", "tc", T.LE[:], T.VV[:]),
            "PUT": lambda: V("NP0 NP2 NP3 BB0 BB1 BB2 LE", "PFT " + PFA, "tt", T.PF[:, 0:4864].indirect(T.LE[:]), T.NP[:, 0:768], T.BB[:], AO.max)}
        for i in range(10):
            end["Y%d" % i] = meaning(i)
        for u in (1, 2, 3):
            end.update(column(u, str(u), 0, 256))
            end["BB%d" % (u - 1)] = new(u - 1)
        for X in range(2):
            end.update(decider(X))
            end.update({name + str(X): finish(name, X) for name in ("M", "H", "D1", "P1", "J", "F")})
            end.update(column(4, "4%d" % X, 128 * X, 128))
            end.update({"Q%d" % X: apart4(X), "NE%d" % X: miss(X)})
        if t < 2:
            end.update({"ZR": lambda: V("CH", "ZR", "red", T.ZR[:, 0:1], T.CH[:, 64:80], AxisListType.X, AO.add),
                        "ZP": lambda: mms("ONE ZR", "DB1", [(T.DB1[:, 0:1], T.ONE[:], T.ZR[:, 0:1], True, True)]),
                        "ZA": closed})
        if t == 2:
            end["ZA"] = end.pop("FO")
        for name in END:
            if name[0] == "@":
                until(float(name[1:]))
            elif name in end:
                end[name]()
    c0, q = 0, 0
    for pieces in OUT:
        d0, keys = c0, ""
        for n in pieces:
            b = ("DB0", "DB1", "DB2", "KEY1")[q % 4]
            if q == 0:
                V(PFA, b, "ts", T[b][:, 0:n], T.PF[:, 2048:2048 + n], 4096.0, None, AO.mult)
            else:
                S(PFA, b, T[b][:, 0:n], T.PF[:, 2048 + c0:2048 + c0 + n], AF.Copy, scale=4096.0)
            V("%s %s" % (b, PFA), "YO%d" % q, "tt", T.YO[:, c0:c0 + n], T[b][:, 0:n], T.PF[:, c0:c0 + n], AO.add)
            c0, q, keys = c0 + n, q + 1, keys + " YO%d" % q
        dma("Y", keys, "yp%d" % q, T.yp[:, d0:c0], T.YO[:, d0:c0])
    for sem in SEMAPHORES:
        if cnt[sem] and sem != "ls":
            need("G", sem, cnt[sem])
    need("G", "ls", cnt["ls"])
    for sem in ("aS1", "aS2", "aF1", "aF2", "aL1", "aL2"):
        need("G", sem, narr)
